import numpy as np
import ml_dtypes


def mxq(x, axis, fmt="e4m3"):
    dtype, down = {"e4m3": (ml_dtypes.float8_e4m3fn, 7), "e5m2": (ml_dtypes.float8_e5m2, 14)}[fmt]
    v = np.moveaxis(np.asarray(x, np.float32).astype(ml_dtypes.bfloat16).astype(np.float64), axis, -1)
    blocks = v.reshape(v.shape[:-1] + (-1, 32))
    amax = np.abs(blocks).max(-1, keepdims=True)
    byte = np.maximum(np.where(amax > 0, np.frexp(amax)[1] - 1 + 127, 0) - down, 1)
    scale = np.exp2(byte - 127.0)
    codes = (blocks / scale).astype(np.float32).astype(dtype).astype(np.float64)
    return np.moveaxis((codes * scale).reshape(v.shape), -1, axis)


WIDE = False


def mx_kscale(k):
    if not WIDE:
        return np.ones(k)
    levels = np.array([10, -10, 5, -5, 0])
    if k % 512:
        return np.exp2(np.random.permutation(np.resize(levels, k // 32))).repeat(32)
    a = np.empty((k // 512, 16))
    for p in range(k // 512):
        a[p, :8] = np.random.permutation(np.resize(levels, 8))
        for g in range(8):
            far = levels[np.abs(levels - a[p, g]) >= 10]
            a[p, g + 8] = far[np.random.randint(len(far))]
    return np.exp2(a.ravel()).repeat(32)


BF16 = ml_dtypes.bfloat16


def bf(x):
    return np.asarray(x, np.float32).astype(BF16)


def f64(x):
    return np.asarray(x).astype(np.float64)


E2M1 = np.array([0.0, 0.5, 1.0, 1.5, 2.0, 3.0, 4.0, 6.0, -0.0, -0.5, -1.0, -1.5, -2.0, -3.0, -4.0, -6.0])


def pack_weight(w, fmt):
    k, n = w.shape
    w = f64(bf(w)).reshape(k // 32, 32, n)
    amax = np.abs(w).max(1)
    if fmt == "e4m3":
        byte = np.frexp(amax)[1] - 1 + 127 - 7
    else:
        mant, ex = np.frexp(amax / 6.0)
        byte = np.where(mant > 0.5, ex, ex - 1) + 127
    byte = np.clip(np.where(amax > 0, byte, 1), 1, 254)
    scaled = (w * np.exp2(127.0 - byte)[:, None, :]).reshape(k, n).astype(np.float32)
    by_word = np.ascontiguousarray(scaled.reshape(k // 512, 128, 4, n).transpose(0, 1, 3, 2))
    if fmt == "e4m3":
        words = by_word.astype(ml_dtypes.float8_e4m3fn).view(np.uint8)
    else:
        c = by_word.astype(ml_dtypes.float4_e2m1fn).view(np.uint8) & 0xF
        words = c[..., 0::2] | (c[..., 1::2] << 4)
    return np.ascontiguousarray(words), np.ascontiguousarray(byte.astype(np.uint8).reshape(k // 512, 16, n))


def unpack_weight(words, scales, fmt):
    g, p, n, _ = words.shape
    if fmt == "e4m3":
        vals = np.ascontiguousarray(words).view(ml_dtypes.float8_e4m3fn).astype(np.float64)
    else:
        nib = np.empty((g, p, n, 4), np.uint8)
        nib[..., 0::2] = words & 0xF
        nib[..., 1::2] = words >> 4
        vals = E2M1[nib]
    vals = vals * np.repeat(np.exp2(scales.astype(np.float64) - 127.0), 8, axis=1)[..., None]
    return vals.transpose(0, 1, 3, 2).reshape(g * 512, n)
def pack4(w):
    words, scales = pack_weight(w, "e2m1")
    return words.reshape(words.shape[0], 128, -1), scales


def unpack4(words, scales):
    return unpack_weight(words.reshape(words.shape[0], 128, -1, 2), scales, "e2m1")


M, D, H = 1024, 2048, 512


def setup_inputs():
    s, u, t = mx_kscale(H), mx_kscale(M), mx_kscale(D)
    w = np.random.standard_normal((D, H)) / (3.0 * np.sqrt(H))
    wd_words, wd_scales = pack4(w.T / s[:, None] * t)
    wb_words, wb_scales = pack4(w / t[:, None])
    pt = np.random.standard_normal((M, M)) / (3.0 * np.sqrt(M))
    pt_words, pt_scales = pack4(pt / u[:, None])
    return {"x": bf(np.random.standard_normal((M, D)) * u[:, None] * t),
            "c": bf(np.random.standard_normal((M, H)) * u[:, None] * s),
            "wd_words": wd_words, "wd_scales": wd_scales,
            "pt_words": pt_words, "pt_scales": pt_scales,
            "wb_words": wb_words, "wb_scales": wb_scales,
            "a": bf((1 + 0.1 * np.random.standard_normal(M)) / u),
            "rate": bf(1 + 0.1 * np.random.standard_normal(H))}


def reference(x, c, wd_words, wd_scales, pt_words, pt_scales, wb_words, wb_scales, a, rate):
    wd = unpack4(wd_words, wd_scales)
    pt = unpack4(pt_words, pt_scales)
    wb = unpack4(wb_words, wb_scales)
    e = f64(x) - (mxq(f64(c), 1, "e4m3") @ wd)
    f = f64(a)[:, None] * e + (pt.T @ mxq(e, 0, "e4m3"))
    return f64(rate) * (mxq(f, 1, "e4m3") @ wb)

@@ -1,0 +1,338 @@
+from contextlib import ExitStack
+
+import concourse.mybir as mybir
+from concourse.masks import make_identity
+
+M, D, H = 1024, 2048, 512
+FLOPS = 2 * (M * H * D + M * M * D + M * D * H)
+
+F32 = mybir.dt.float32
+BF16 = mybir.dt.bfloat16
+I32 = mybir.dt.int32
+U32 = mybir.dt.uint32
+U8 = mybir.dt.uint8
+E4M3X4 = mybir.dt.float8_e4m3fn_x4
+E2M1X4 = mybir.dt.float4_e2m1fn_x4
+ALU = mybir.AluOpType
+
+P = 128
+N = 512
+CHUNKS = D // N
+HALVES = 2 * CHUNKS
+SLOTS = 4
+
+
+def tile_tied_autoencoder_code_step_t2_kernel(
+    tc, x, c, wd_words, wd_scales, pt_words, pt_scales, wb_words, wb_scales, a, rate, out
+):
+    nc = tc.nc
+    with ExitStack() as ctx:
+        keep = ctx.enter_context(tc.tile_pool(name="keep", bufs=1))
+        work = ctx.enter_context(tc.tile_pool(name="work", bufs=2))
+        psum = ctx.enter_context(tc.psum_pool(name="psum", bufs=1))
+        ctx.enter_context(tc.manual_schedule())
+
+        ident = keep.tile([P, P], F32, name="ident")
+        warm = keep.tile([P, 2], F32, name="warm")
+        c_raw = [keep.tile([P, 2, H], BF16, name="c_raw%d" % k) for k in range(4)]
+        c_codes = keep.tile([P, M], U32, name="c_codes", align_bytes=64)
+        c_planes = keep.tile([P, M], U8, name="c_planes", align_bytes=64)
+        x_sb = [keep.tile([P, SLOTS, N], BF16, name="x_sb%d" % s) for s in range(HALVES)]
+        wd_sb = keep.tile([P, 2 * D], U8, name="wd_sb", align_bytes=64)
+        wd_pl = keep.tile([P, D], U8, name="wd_pl", align_bytes=64)
+        pt_raw = keep.tile([P, 2, 2 * M], U8, name="pt_raw", align_bytes=64)
+        pt_sb = keep.tile([P, 2, 2 * M], U8, name="pt_sb", align_bytes=64)
+        pt_plraw = keep.tile([P, 2, M], U8, name="pt_plraw", align_bytes=64)
+        pt_pl = keep.tile([P, 2, M], U8, name="pt_pl", align_bytes=64)
+        wb_sb = keep.tile([P, CHUNKS, 2 * H], U8, name="wb_sb", align_bytes=64)
+        wb_pl = keep.tile([P, CHUNKS, H], U8, name="wb_pl", align_bytes=64)
+        a_sb = keep.tile([P, 2, SLOTS], BF16, name="a_sb")
+        rate_sb = keep.tile([P, H], BF16, name="rate_sb")
+        f_codes = [keep.tile([P, N], U32, name="f_codes%d" % h, align_bytes=64) for h in range(HALVES)]
+        f_planes = [keep.tile([P, N], U8, name="f_planes%d" % h, align_bytes=64) for h in range(HALVES)]
+
+        c_view = c.rearrange("(g p t) k -> g p t k", p=P, t=SLOTS)
+        x_view = x.rearrange("(g p t) d -> g p t d", p=P, t=SLOTS)
+        out_view = out.rearrange("(g p t) h -> g p t h", p=P, t=SLOTS)
+
+        def load_c(k):
+            nc.sync.dma_start(out=c_raw[k][:], in_=c_view[k // 2][:, 2 * (k % 2) : 2 * (k % 2) + 2, :])
+
+        def load_x(s):
+            nc.sync.dma_start(out=x_sb[s][:], in_=x_view[s % 2][:, :, N * (s // 2) : N * (s // 2 + 1)])
+
+        def load_wd(lo, hi):
+            nc.sync.dma_start(
+                out=wd_sb[:, 2 * lo : 2 * hi].bitcast(I32), in_=wd_words[0][:, 2 * lo : 2 * hi].bitcast(I32)
+            )
+
+        nc.gpsimd.memset(warm[:], 0.0)
+        make_identity(nc, ident[:])
+        nc.scalar.copy(out=warm[:, 1:2], in_=warm[:, 0:1])
+
+        nc.vector.memset(wd_pl[:].bitcast(I32), 0)
+        nc.vector.memset(pt_plraw[:].rearrange("p g n -> p (g n)").bitcast(I32), 0)
+        nc.vector.memset(wb_pl[:].rearrange("p g n -> p (g n)").bitcast(I32), 0)
+
+        load_c(0)
+        load_c(1)
+        for r in range(4):
+            queue = nc.scalar if r < 2 else nc.gpsimd
+            queue.dma_start(out=wd_pl[r:P:32, :].bitcast(I32), in_=wd_scales[0][r:16:4, :].bitcast(I32))
+        load_wd(0, N)
+        load_x(0)
+        for g in range(2):
+            nc.sync.dma_start(out=pt_raw[:, g, :].bitcast(I32), in_=pt_words[g].bitcast(I32))
+        load_c(2)
+        load_c(3)
+        load_x(1)
+        for r in range(4):
+            nc.sync.dma_start(
+                out=pt_plraw[r:P:32, :, :].bitcast(I32),
+                in_=pt_scales[:, r:16:4, :].rearrange("g q n -> q g n").bitcast(I32),
+            )
+        for r in range(4):
+            nc.sync.dma_start(
+                out=wb_pl[r:P:32, :, :].bitcast(I32),
+                in_=wb_scales[:, r:16:4, :].rearrange("g q n -> q g n").bitcast(I32),
+            )
+        load_wd(N, D)
+        nc.sync.dma_start(out=a_sb[:], in_=a.rearrange("(g p t) -> p g t", p=P, t=SLOTS))
+        for s in range(2, HALVES):
+            load_x(s)
+            if s == 3:
+                nc.sync.dma_start(
+                    out=wb_sb[:].bitcast(I32), in_=wb_words.rearrange("g p w -> p g w").bitcast(I32)
+                )
+        nc.sync.dma_start(out=rate_sb[:], in_=rate.partition_broadcast(P))
+
+        counts = {"m": 0, "t": 0}
+        depth = {"m": 3, "t": 2}
+
+        def bank(kind):
+            k = counts[kind] % depth[kind]
+            counts[kind] += 1
+            b = psum.tile([P, N], F32, name="%s%d" % (kind, k), tag="%s%d" % (kind, k))
+            return b
+
+        def turn_c(k):
+            turned = bank("t")
+            for i in range(2):
+                words = c_raw[k][:, i, :].bitcast(F32)
+                for u in range(2):
+                    lo = P * (2 * i + u)
+                    nc.tensor.transpose(turned[:, lo : lo + P], words[:, u : 2 * P : 2], ident[:])
+            c_grp = work.tile([P, 4 * 2 * P], BF16, name="c_grp", align_bytes=64)
+            nc.scalar.copy(
+                out=c_grp[:].bitcast(F32).rearrange("p (i r u) -> p i r u", i=2, u=2),
+                in_=turned[:].rearrange("p (i u r) -> p i r u", i=2, u=2),
+            )
+            return c_grp
+
+        def quantize_c(k, c_grp):
+            cols = slice(2 * P * k, 2 * P * (k + 1))
+            nc.vector.quantize_mx(out=c_codes[:, cols].bitcast(E4M3X4), scales=c_planes[:, cols], in_=c_grp[:])
+
+        def permute_pt(g, j):
+            nc.vector.tensor_copy(
+                out=pt_sb[:, g, 1024 * j : 1024 * (j + 1)].rearrange("p (t m b) -> p t m b", t=4, b=2),
+                in_=pt_raw[:, g, 1024 * j : 1024 * (j + 1)].rearrange("p (m t b) -> p t m b", t=4, b=2),
+            )
+
+        def permute_pt_scales(g):
+            nc.vector.tensor_copy(
+                out=pt_pl[:, g, :].rearrange("p (j t m) -> p j t m", j=2, t=4),
+                in_=pt_plraw[:, g, :].rearrange("p (j m t) -> p j t m", j=2, t=4),
+            )
+
+        e32 = {}
+        e_codes = {}
+        e_planes = {}
+        e_grp = {}
+        f_sb = {}
+        f_grp = {}
+        e_bank = {}
+
+        def e_matmul(s, t):
+            ch, g = divmod(s, 2)
+            b = bank("m")
+            e_bank[(s, t)] = b
+            rows = slice(P * (4 * g + t), P * (4 * g + t + 1))
+            nc.tensor.matmul_mx(
+                out=b[:],
+                lhsT=c_codes[:, rows].bitcast(E4M3X4),
+                lhsT_scale=c_planes[:, rows],
+                rhs=wd_sb[:, 2 * N * ch : 2 * N * (ch + 1)].bitcast(E2M1X4),
+                rhs_scale=wd_pl[:, N * ch : N * (ch + 1)],
+                start=True,
+                stop=True,
+            )
+
+        def e_subtract(s, t):
+            if t == 0:
+                e32[s] = work.tile([P, SLOTS, N], F32, name="e32", bufs=4)
+            b = e_bank.pop((s, t))
+            nc.vector.tensor_tensor(
+                out=e32[s][:, t, :].rearrange("p (u m e) -> p u m e", u=2, e=2),
+                in0=x_sb[s][:, t, :].rearrange("p (m u e) -> p u m e", u=2, e=2),
+                in1=b[:].rearrange("p (m u e) -> p u m e", u=2, e=2),
+                op=ALU.subtract,
+            )
+
+        def e_group(s):
+            e_grp[s] = work.tile([P, N, SLOTS], BF16, name="e_grp", bufs=2, align_bytes=64)
+            for k in range(2):
+                cols = slice(N // 2 * k, N // 2 * (k + 1))
+                nc.scalar.copy(
+                    out=e_grp[s][:, cols, :].rearrange("p (n i) t -> p n t i", i=4),
+                    in_=e32[s][:, :, cols].rearrange("p t (n i) -> p n t i", i=4),
+                )
+
+        def e_quantize(s):
+            e_codes[s] = work.tile([P, N], U32, name="e_codes", bufs=4, align_bytes=64)
+            e_planes[s] = work.tile([P, N], U8, name="e_planes", bufs=4, align_bytes=64)
+            nc.vector.quantize_mx(
+                out=e_codes[s][:].bitcast(E4M3X4),
+                scales=e_planes[s][:],
+                in_=e_grp[s][:].rearrange("p n t -> p (n t)"),
+            )
+
+        def f_tile(h, t):
+            ch, g = divmod(h, 2)
+            if t == 0:
+                f_sb[h] = work.tile([P, SLOTS, N], BF16, name="f_sb", bufs=2)
+            b = bank("m")
+            tile_no = 4 * g + t
+            for k in range(2):
+                nc.tensor.matmul_mx(
+                    out=b[:],
+                    lhsT=pt_sb[:, k, 2 * P * tile_no : 2 * P * (tile_no + 1)].bitcast(E2M1X4),
+                    lhsT_scale=pt_pl[:, k, P * tile_no : P * (tile_no + 1)],
+                    rhs=e_codes[2 * ch + k][:].bitcast(E4M3X4),
+                    rhs_scale=e_planes[2 * ch + k][:],
+                    start=(k == 0),
+                    stop=(k == 1),
+                )
+            nc.vector.scalar_tensor_tensor(
+                out=f_sb[h][:, t, :],
+                in0=e32[h][:, t, :],
+                scalar=a_sb[:, g, t : t + 1],
+                in1=b[:],
+                op0=ALU.mult,
+                op1=ALU.add,
+            )
+
+        def f_turn(h, pair):
+            if pair == 0:
+                f_grp[h] = work.tile([P, SLOTS * P * 4], BF16, name="f_grp", bufs=2, align_bytes=64)
+            turned = bank("t")
+            for i in range(2):
+                words = f_sb[h][:, 2 * pair + i, :].bitcast(F32)
+                for u in range(2):
+                    lo = P * (2 * i + u)
+                    nc.tensor.transpose(turned[:, lo : lo + P], words[:, P * u : P * (u + 1)], ident[:])
+            half = slice(1024 * pair, 1024 * (pair + 1))
+            nc.scalar.copy(
+                out=f_grp[h][:, half].bitcast(F32).rearrange("p (i r u) -> p i r u", i=2, u=2),
+                in_=turned[:].rearrange("p (i u r) -> p i r u", i=2, u=2),
+            )
+
+        def f_quantize(h, lo, hi):
+            nc.vector.quantize_mx(
+                out=f_codes[h][:, P * lo : P * hi].bitcast(E4M3X4),
+                scales=f_planes[h][:, P * lo : P * hi],
+                in_=f_grp[h][:, 4 * P * lo : 4 * P * hi],
+            )
+
+        o_bank = {}
+
+        def o_pass(n, ch, tag):
+            if ch == 0:
+                o_new = psum.tile([P, N], F32, name="o", tag=tag)
+                o_bank[n] = o_new
+            g, t = divmod(n, 4)
+            h = 2 * ch + g
+            nc.tensor.matmul_mx(
+                out=o_bank[n][:],
+                lhsT=f_codes[h][:, P * t : P * (t + 1)].bitcast(E4M3X4),
+                lhsT_scale=f_planes[h][:, P * t : P * (t + 1)],
+                rhs=wb_sb[:, ch, :].bitcast(E2M1X4),
+                rhs_scale=wb_pl[:, ch, :],
+                start=(ch == 0),
+                stop=(ch == CHUNKS - 1),
+            )
+
+        def o_store(n):
+            g, t = divmod(n, 4)
+            o_sb = work.tile([P, H], F32, name="o_sb", bufs=4)
+            nc.vector.tensor_tensor(out=o_sb[:], in0=o_bank[n][:], in1=rate_sb[:], op=ALU.mult)
+            nc.sync.dma_start(out=out_view[g][:, t, :], in_=o_sb[:])
+
+        grp = turn_c(0)
+        quantize_c(0, grp)
+        grp = turn_c(1)
+        quantize_c(1, grp)
+
+        tags = ["o0", "o1", "o2", "m2"]
+        for s in range(HALVES + 2):
+            h = s - 2
+            if s < HALVES:
+                e_matmul(s, 0)
+                e_matmul(s, 1)
+                e_subtract(s, 0)
+                e_subtract(s, 1)
+            if h >= 1:
+                f_turn(h - 1, 0)
+                f_turn(h - 1, 1)
+            if 1 <= s <= HALVES:
+                e_quantize(s - 1)
+            if s < HALVES:
+                for t in (2, 3):
+                    e_matmul(s, t)
+                    e_subtract(s, t)
+            if s == 0:
+                permute_pt(0, 0)
+                permute_pt(0, 1)
+                for k in (2, 3):
+                    grp = turn_c(k)
+                    quantize_c(k, grp)
+                permute_pt(1, 0)
+            if s == 1:
+                permute_pt(1, 1)
+                permute_pt_scales(0)
+                permute_pt_scales(1)
+            if s < HALVES:
+                e_group(s)
+            if h >= 1:
+                f_quantize(h - 1, 0, 4)
+            if s == HALVES:
+                depth["m"] = 2
+                counts["m"] = 0
+            if h >= 0:
+                for t in range(4):
+                    f_tile(h, t)
+            if h >= 1 and (h - 1) % 2 == 0:
+                ch = (h - 1) // 2
+                for n in range(3):
+                    o_pass(n, ch, tags[n])
+            if s == HALVES:
+                for ch in range(3):
+                    o_pass(3, ch, tags[3])
+            if s == HALVES + 1:
+                o_pass(3, 3, tags[3])
+                for n in range(4):
+                    o_store(n)
+        last = HALVES - 1
+        f_turn(last, 0)
+        for n in (4, 5):
+            for ch in range(3):
+                o_pass(n, ch, tags[n - 4])
+        f_turn(last, 1)
+        f_quantize(last, 0, 2)
+        for n in (6, 7):
+            for ch in range(3):
+                o_pass(n, ch, tags[n - 4])
+        f_quantize(last, 2, 4)
+        for n in range(4, 8):
+            o_pass(n, 3, tags[n - 4])
+            o_store(n)

@@ -10,6 +10,7 @@ F32 = mybir.dt.float32
 BF16 = mybir.dt.bfloat16
 I32 = mybir.dt.int32
 U32 = mybir.dt.uint32
+U16 = mybir.dt.uint16
 U8 = mybir.dt.uint8
 E4M3X4 = mybir.dt.float8_e4m3fn_x4
 E2M1X4 = mybir.dt.float4_e2m1fn_x4
@@ -33,8 +34,8 @@ def tile_tied_autoencoder_code_step_t2_kernel(
         ctx.enter_context(tc.manual_schedule())
 
         ident = keep.tile([P, P], F32, name="ident")
-        warm = keep.tile([P, 2], F32, name="warm")
         c_raw = [keep.tile([P, 2, H], BF16, name="c_raw%d" % k) for k in range(4)]
+        c_grp = keep.tile([P, 4 * M], BF16, name="c_grp", align_bytes=64)
         c_codes = keep.tile([P, M], U32, name="c_codes", align_bytes=64)
         c_planes = keep.tile([P, M], U8, name="c_planes", align_bytes=64)
         x_sb = [keep.tile([P, SLOTS, N], BF16, name="x_sb%d" % s) for s in range(HALVES)]
@@ -66,44 +67,38 @@ def tile_tied_autoencoder_code_step_t2_kernel(
                 out=wd_sb[:, 2 * lo : 2 * hi].bitcast(I32), in_=wd_words[0][:, 2 * lo : 2 * hi].bitcast(I32)
             )
 
-        nc.gpsimd.memset(warm[:], 0.0)
         make_identity(nc, ident[:])
-        nc.scalar.copy(out=warm[:, 1:2], in_=warm[:, 0:1])
-
         nc.vector.memset(wd_pl[:].bitcast(I32), 0)
         nc.vector.memset(pt_plraw[:].rearrange("p g n -> p (g n)").bitcast(I32), 0)
         nc.vector.memset(wb_pl[:].rearrange("p g n -> p (g n)").bitcast(I32), 0)
 
         load_c(0)
+        load_wd(0, N)
         load_c(1)
         for r in range(4):
-            queue = nc.scalar if r < 2 else nc.gpsimd
-            queue.dma_start(out=wd_pl[r:P:32, :].bitcast(I32), in_=wd_scales[0][r:16:4, :].bitcast(I32))
-        load_wd(0, N)
+            nc.scalar.dma_start(out=wd_pl[r:P:32, :].bitcast(I32), in_=wd_scales[0][r:16:4, :].bitcast(I32))
         load_x(0)
-        for g in range(2):
-            nc.sync.dma_start(out=pt_raw[:, g, :].bitcast(I32), in_=pt_words[g].bitcast(I32))
         load_c(2)
         load_c(3)
+        nc.sync.dma_start(out=pt_raw[:].bitcast(I32), in_=pt_words.rearrange("g p w -> p g w").bitcast(I32))
         load_x(1)
+        load_wd(N, D)
         for r in range(4):
             nc.sync.dma_start(
                 out=pt_plraw[r:P:32, :, :].bitcast(I32),
                 in_=pt_scales[:, r:16:4, :].rearrange("g q n -> q g n").bitcast(I32),
             )
+        load_x(2)
+        nc.sync.dma_start(out=a_sb[:], in_=a.rearrange("(g p t) -> p g t", p=P, t=SLOTS))
+        load_x(3)
         for r in range(4):
             nc.sync.dma_start(
                 out=wb_pl[r:P:32, :, :].bitcast(I32),
                 in_=wb_scales[:, r:16:4, :].rearrange("g q n -> q g n").bitcast(I32),
             )
-        load_wd(N, D)
-        nc.sync.dma_start(out=a_sb[:], in_=a.rearrange("(g p t) -> p g t", p=P, t=SLOTS))
-        for s in range(2, HALVES):
+        nc.sync.dma_start(out=wb_sb[:].bitcast(I32), in_=wb_words.rearrange("g p w -> p g w").bitcast(I32))
+        for s in range(4, HALVES):
             load_x(s)
-            if s == 3:
-                nc.sync.dma_start(
-                    out=wb_sb[:].bitcast(I32), in_=wb_words.rearrange("g p w -> p g w").bitcast(I32)
-                )
         nc.sync.dma_start(out=rate_sb[:], in_=rate.partition_broadcast(P))
 
         counts = {"m": 0, "t": 0}
@@ -115,28 +110,31 @@ def tile_tied_autoencoder_code_step_t2_kernel(
             b = psum.tile([P, N], F32, name="%s%d" % (kind, k), tag="%s%d" % (kind, k))
             return b
 
-        def turn_c(k):
-            turned = bank("t")
-            for i in range(2):
-                words = c_raw[k][:, i, :].bitcast(F32)
+        def turn_c(first, count, tag):
+            turned = psum.tile([P, N], F32, name="turned_c", tag=tag)
+            for i in range(count):
+                k, j = divmod(first + i, 2)
+                words = c_raw[k][:, j, :].bitcast(F32)
                 for u in range(2):
                     lo = P * (2 * i + u)
                     nc.tensor.transpose(turned[:, lo : lo + P], words[:, u : 2 * P : 2], ident[:])
-            c_grp = work.tile([P, 4 * 2 * P], BF16, name="c_grp", align_bytes=64)
             nc.scalar.copy(
-                out=c_grp[:].bitcast(F32).rearrange("p (i r u) -> p i r u", i=2, u=2),
-                in_=turned[:].rearrange("p (i u r) -> p i r u", i=2, u=2),
+                out=c_grp[:, N * first : N * (first + count)].bitcast(F32).rearrange("p (i r u) -> p i r u", i=count, u=2),
+                in_=turned[:, : 2 * P * count].rearrange("p (i u r) -> p i r u", i=count, u=2),
             )
-            return c_grp
 
-        def quantize_c(k, c_grp):
-            cols = slice(2 * P * k, 2 * P * (k + 1))
-            nc.vector.quantize_mx(out=c_codes[:, cols].bitcast(E4M3X4), scales=c_planes[:, cols], in_=c_grp[:])
+        def quantize_c(first, count):
+            cols = slice(P * first, P * (first + count))
+            nc.vector.quantize_mx(
+                out=c_codes[:, cols].bitcast(E4M3X4),
+                scales=c_planes[:, cols],
+                in_=c_grp[:, N * first : N * (first + count)],
+            )
 
-        def permute_pt(g, j):
+        def permute_pt(g):
             nc.vector.tensor_copy(
-                out=pt_sb[:, g, 1024 * j : 1024 * (j + 1)].rearrange("p (t m b) -> p t m b", t=4, b=2),
-                in_=pt_raw[:, g, 1024 * j : 1024 * (j + 1)].rearrange("p (m t b) -> p t m b", t=4, b=2),
+                out=pt_sb[:, g, :].bitcast(U16).rearrange("p (j t m) -> p j t m", j=2, t=4),
+                in_=pt_raw[:, g, :].bitcast(U16).rearrange("p (j m t) -> p j t m", j=2, t=4),
             )
 
         def permute_pt_scales(g):
@@ -184,8 +182,8 @@ def tile_tied_autoencoder_code_step_t2_kernel(
             for k in range(2):
                 cols = slice(N // 2 * k, N // 2 * (k + 1))
                 nc.scalar.copy(
-                    out=e_grp[s][:, cols, :].rearrange("p (n i) t -> p n t i", i=4),
-                    in_=e32[s][:, :, cols].rearrange("p t (n i) -> p n t i", i=4),
+                    out=e_grp[s][:, cols, :],
+                    in_=e32[s][:, :, cols].rearrange("p t n -> p n t"),
                 )
 
         def e_quantize(s):
@@ -197,11 +195,10 @@ def tile_tied_autoencoder_code_step_t2_kernel(
                 in_=e_grp[s][:].rearrange("p n t -> p (n t)"),
             )
 
-        def f_tile(h, t):
+        def g_matmul(h, t):
             ch, g = divmod(h, 2)
-            if t == 0:
-                f_sb[h] = work.tile([P, SLOTS, N], BF16, name="f_sb", bufs=2)
             b = bank("m")
+            e_bank[("g", h, t)] = b
             tile_no = 4 * g + t
             for k in range(2):
                 nc.tensor.matmul_mx(
@@ -213,6 +210,12 @@ def tile_tied_autoencoder_code_step_t2_kernel(
                     start=(k == 0),
                     stop=(k == 1),
                 )
+
+        def f_add(h, t):
+            g = h % 2
+            if t == 0:
+                f_sb[h] = work.tile([P, SLOTS, N], BF16, name="f_sb", bufs=2)
+            b = e_bank.pop(("g", h, t))
             nc.vector.scalar_tensor_tensor(
                 out=f_sb[h][:, t, :],
                 in0=e32[h][:, t, :],
@@ -264,75 +267,94 @@ def tile_tied_autoencoder_code_step_t2_kernel(
 
         def o_store(n):
             g, t = divmod(n, 4)
-            o_sb = work.tile([P, H], F32, name="o_sb", bufs=4)
+            o_sb = work.tile([P, H], F32, name="o_sb", bufs=8)
             nc.vector.tensor_tensor(out=o_sb[:], in0=o_bank[n][:], in1=rate_sb[:], op=ALU.mult)
             nc.sync.dma_start(out=out_view[g][:, t, :], in_=o_sb[:])
 
-        grp = turn_c(0)
-        quantize_c(0, grp)
-        grp = turn_c(1)
-        quantize_c(1, grp)
+        def e_tile(s, t):
+            e_matmul(s, t)
+            e_subtract(s, t)
+
+        def f_tile(h, t):
+            g_matmul(h, t)
+            f_add(h, t)
+
+        def o_passes(tiles, chunks):
+            for n in tiles:
+                for ch in chunks:
+                    o_pass(n, ch, tags[n % 4])
 
         tags = ["o0", "o1", "o2", "m2"]
-        for s in range(HALVES + 2):
+        turn_c(0, 1, "o0")
+        turn_c(1, 1, "o1")
+        turn_c(2, 2, "o2")
+        quantize_c(0, 1)
+        quantize_c(1, 1)
+        quantize_c(2, 2)
+        for t in range(4):
+            e_tile(0, t)
+        turn_c(4, 2, "t0")
+        turn_c(6, 2, "t1")
+        permute_pt(0)
+        quantize_c(4, 2)
+        quantize_c(6, 2)
+        e_group(0)
+        permute_pt(1)
+        for t in range(4):
+            e_tile(1, t)
+        e_group(1)
+        permute_pt_scales(0)
+        e_quantize(0)
+        permute_pt_scales(1)
+
+        for s in range(2, HALVES):
             h = s - 2
-            if s < HALVES:
-                e_matmul(s, 0)
-                e_matmul(s, 1)
-                e_subtract(s, 0)
-                e_subtract(s, 1)
+            e_tile(s, 0)
+            e_tile(s, 1)
             if h >= 1:
                 f_turn(h - 1, 0)
                 f_turn(h - 1, 1)
-            if 1 <= s <= HALVES:
-                e_quantize(s - 1)
-            if s < HALVES:
-                for t in (2, 3):
-                    e_matmul(s, t)
-                    e_subtract(s, t)
-            if s == 0:
-                permute_pt(0, 0)
-                permute_pt(0, 1)
-                for k in (2, 3):
-                    grp = turn_c(k)
-                    quantize_c(k, grp)
-                permute_pt(1, 0)
-            if s == 1:
-                permute_pt(1, 1)
-                permute_pt_scales(0)
-                permute_pt_scales(1)
-            if s < HALVES:
-                e_group(s)
+            e_quantize(s - 1)
+            e_tile(s, 2)
+            e_tile(s, 3)
+            if h >= 2 and h % 2 == 0:
+                o_passes(range(3), [h // 2 - 1])
+            e_group(s)
             if h >= 1:
                 f_quantize(h - 1, 0, 4)
-            if s == HALVES:
-                depth["m"] = 2
-                counts["m"] = 0
-            if h >= 0:
-                for t in range(4):
-                    f_tile(h, t)
-            if h >= 1 and (h - 1) % 2 == 0:
-                ch = (h - 1) // 2
-                for n in range(3):
-                    o_pass(n, ch, tags[n])
-            if s == HALVES:
-                for ch in range(3):
-                    o_pass(3, ch, tags[3])
-            if s == HALVES + 1:
-                o_pass(3, 3, tags[3])
-                for n in range(4):
-                    o_store(n)
-        last = HALVES - 1
-        f_turn(last, 0)
-        for n in (4, 5):
-            for ch in range(3):
-                o_pass(n, ch, tags[n - 4])
-        f_turn(last, 1)
-        f_quantize(last, 0, 2)
-        for n in (6, 7):
-            for ch in range(3):
-                o_pass(n, ch, tags[n - 4])
-        f_quantize(last, 2, 4)
+            for t in range(4):
+                f_tile(h, t)
+        depth["m"] = 2
+        counts["m"] = 0
+        o_passes(range(3), [2])
+        f_turn(5, 0)
+        f_turn(5, 1)
+        e_quantize(7)
+        f_tile(6, 0)
+        f_tile(6, 1)
+        f_quantize(5, 0, 4)
+        f_tile(6, 2)
+        f_tile(6, 3)
+        f_turn(6, 0)
+        f_tile(7, 0)
+        f_turn(6, 1)
+        f_tile(7, 1)
+        f_quantize(6, 0, 2)
+        f_tile(7, 2)
+        o_passes([0, 1], [3])
+        f_quantize(6, 2, 4)
+        f_tile(7, 3)
+        f_turn(7, 0)
+        o_passes([2], [3])
+        o_passes([3], range(4))
+        o_store(0)
+        o_store(1)
+        f_turn(7, 1)
+        o_store(2)
+        f_quantize(7, 0, 2)
+        o_passes([4, 5], range(4))
+        o_store(3)
+        f_quantize(7, 2, 4)
+        o_passes([6, 7], range(4))
         for n in range(4, 8):
-            o_pass(n, 3, tags[n - 4])
             o_store(n)

@@ -101,13 +101,12 @@ def tile_tied_autoencoder_code_step_t2_kernel(
             load_x(s)
         nc.sync.dma_start(out=rate_sb[:], in_=rate.partition_broadcast(P))
 
-        counts = {"m": 0, "t": 0}
-        depth = {"m": 3, "t": 2}
+        ring = {"size": 4, "next": 0}
 
-        def bank(kind):
-            k = counts[kind] % depth[kind]
-            counts[kind] += 1
-            b = psum.tile([P, N], F32, name="%s%d" % (kind, k), tag="%s%d" % (kind, k))
+        def bank():
+            k = ring["next"] % ring["size"]
+            ring["next"] = k + 1
+            b = psum.tile([P, N], F32, name="ring%d" % k, tag="bank%d" % k)
             return b
 
         def turn_c(first, count, tag):
@@ -153,7 +152,7 @@ def tile_tied_autoencoder_code_step_t2_kernel(
 
         def e_matmul(s, t):
             ch, g = divmod(s, 2)
-            b = bank("m")
+            b = bank()
             e_bank[(s, t)] = b
             rows = slice(P * (4 * g + t), P * (4 * g + t + 1))
             nc.tensor.matmul_mx(
@@ -177,6 +176,25 @@ def tile_tied_autoencoder_code_step_t2_kernel(
                 op=ALU.subtract,
             )
 
+        def e_subtract_aside(s, t):
+            if t == 0:
+                e32[s] = work.tile([P, SLOTS, N], F32, name="e32", bufs=4)
+            b = e_bank.pop((s, t))
+            dst = e32[s][:, t, :].rearrange("p (u m e) -> p u m e", u=2, e=2)
+            nc.scalar.copy(out=dst, in_=b[:].rearrange("p (m u e) -> p u m e", u=2, e=2))
+            nc.gpsimd.tensor_tensor(
+                out=dst,
+                in0=x_sb[s][:, t, :].rearrange("p (m u e) -> p u m e", u=2, e=2),
+                in1=dst,
+                op=ALU.subtract,
+            )
+
+        def e_group_half(s, k):
+            if k == 0:
+                e_grp[s] = work.tile([P, N, SLOTS], BF16, name="e_grp", bufs=2, align_bytes=64)
+            cols = slice(N // 2 * k, N // 2 * (k + 1))
+            nc.scalar.copy(out=e_grp[s][:, cols, :], in_=e32[s][:, :, cols].rearrange("p t n -> p n t"))
+
         def e_group(s):
             e_grp[s] = work.tile([P, N, SLOTS], BF16, name="e_grp", bufs=2, align_bytes=64)
             for k in range(2):
@@ -195,21 +213,24 @@ def tile_tied_autoencoder_code_step_t2_kernel(
                 in_=e_grp[s][:].rearrange("p n t -> p (n t)"),
             )
 
-        def g_matmul(h, t):
+        def g_pass(h, t, k):
             ch, g = divmod(h, 2)
-            b = bank("m")
-            e_bank[("g", h, t)] = b
+            if k == 0:
+                e_bank[("g", h, t)] = bank()
             tile_no = 4 * g + t
-            for k in range(2):
-                nc.tensor.matmul_mx(
-                    out=b[:],
-                    lhsT=pt_sb[:, k, 2 * P * tile_no : 2 * P * (tile_no + 1)].bitcast(E2M1X4),
-                    lhsT_scale=pt_pl[:, k, P * tile_no : P * (tile_no + 1)],
-                    rhs=e_codes[2 * ch + k][:].bitcast(E4M3X4),
-                    rhs_scale=e_planes[2 * ch + k][:],
-                    start=(k == 0),
-                    stop=(k == 1),
-                )
+            nc.tensor.matmul_mx(
+                out=e_bank[("g", h, t)][:],
+                lhsT=pt_sb[:, k, 2 * P * tile_no : 2 * P * (tile_no + 1)].bitcast(E2M1X4),
+                lhsT_scale=pt_pl[:, k, P * tile_no : P * (tile_no + 1)],
+                rhs=e_codes[2 * ch + k][:].bitcast(E4M3X4),
+                rhs_scale=e_planes[2 * ch + k][:],
+                start=(k == 0),
+                stop=(k == 1),
+            )
+
+        def g_matmul(h, t):
+            g_pass(h, t, 0)
+            g_pass(h, t, 1)
 
         def f_add(h, t):
             g = h % 2
@@ -227,8 +248,8 @@ def tile_tied_autoencoder_code_step_t2_kernel(
 
         def f_turn(h, pair):
             if pair == 0:
-                f_grp[h] = work.tile([P, SLOTS * P * 4], BF16, name="f_grp", bufs=2, align_bytes=64)
-            turned = bank("t")
+                f_grp[h] = work.tile([P, SLOTS * P * 4], BF16, name="f_grp", bufs=3, align_bytes=64)
+            turned = bank()
             for i in range(2):
                 words = f_sb[h][:, 2 * pair + i, :].bitcast(F32)
                 for u in range(2):
@@ -282,19 +303,18 @@ def tile_tied_autoencoder_code_step_t2_kernel(
         def o_passes(tiles, chunks):
             for n in tiles:
                 for ch in chunks:
-                    o_pass(n, ch, tags[n % 4])
+                    o_pass(n, ch, "bank%d" % (4 + n % 4))
 
-        tags = ["o0", "o1", "o2", "m2"]
-        turn_c(0, 1, "o0")
-        turn_c(1, 1, "o1")
-        turn_c(2, 2, "o2")
+        turn_c(0, 1, "bank4")
+        turn_c(1, 1, "bank5")
+        turn_c(2, 2, "bank6")
         quantize_c(0, 1)
         quantize_c(1, 1)
         quantize_c(2, 2)
         for t in range(4):
             e_tile(0, t)
-        turn_c(4, 2, "t0")
-        turn_c(6, 2, "t1")
+        turn_c(4, 2, "bank7")
+        turn_c(6, 2, "bank4")
         permute_pt(0)
         quantize_c(4, 2)
         quantize_c(6, 2)
@@ -306,55 +326,71 @@ def tile_tied_autoencoder_code_step_t2_kernel(
         permute_pt_scales(0)
         e_quantize(0)
         permute_pt_scales(1)
+        e_tile(2, 0)
 
         for s in range(2, HALVES):
             h = s - 2
-            e_tile(s, 0)
             e_tile(s, 1)
+            e_tile(s, 2)
             if h >= 1:
                 f_turn(h - 1, 0)
                 f_turn(h - 1, 1)
             e_quantize(s - 1)
-            e_tile(s, 2)
             e_tile(s, 3)
-            if h >= 2 and h % 2 == 0:
-                o_passes(range(3), [h // 2 - 1])
-            e_group(s)
+            if h >= 2:
+                o_passes(range(2 * (h % 2), 2 * (h % 2) + 2), [h // 2 - 1])
+            e_group_half(s, 0)
             if h >= 1:
                 f_quantize(h - 1, 0, 4)
-            for t in range(4):
+            f_tile(h, 0)
+            if s + 1 < HALVES:
+                e_matmul(s + 1, 0)
+                e_subtract_aside(s + 1, 0)
+            e_group_half(s, 1)
+            for t in range(1, 4):
                 f_tile(h, t)
-        depth["m"] = 2
-        counts["m"] = 0
-        o_passes(range(3), [2])
+        o_passes(range(2), [2])
         f_turn(5, 0)
+        g_pass(6, 0, 0)
+        o_passes(range(2, 4), [2])
+        g_pass(6, 1, 0)
         f_turn(5, 1)
         e_quantize(7)
-        f_tile(6, 0)
-        f_tile(6, 1)
-        f_quantize(5, 0, 4)
+        f_quantize(5, 0, 2)
+        g_pass(6, 0, 1)
+        g_pass(6, 1, 1)
+        f_add(6, 0)
+        f_add(6, 1)
         f_tile(6, 2)
         f_tile(6, 3)
+        g_matmul(7, 0)
         f_turn(6, 0)
-        f_tile(7, 0)
+        f_quantize(5, 2, 4)
+        f_add(7, 0)
+        g_matmul(7, 1)
         f_turn(6, 1)
-        f_tile(7, 1)
         f_quantize(6, 0, 2)
-        f_tile(7, 2)
+        f_add(7, 1)
+        g_matmul(7, 2)
         o_passes([0, 1], [3])
         f_quantize(6, 2, 4)
-        f_tile(7, 3)
-        f_turn(7, 0)
-        o_passes([2], [3])
-        o_passes([3], range(4))
+        f_add(7, 2)
+        g_matmul(7, 3)
+        o_passes([2, 3], [3])
         o_store(0)
+        f_add(7, 3)
+        f_turn(7, 0)
         o_store(1)
+        o_passes([4], range(3))
         f_turn(7, 1)
         o_store(2)
+        o_passes([5], range(3))
         f_quantize(7, 0, 2)
-        o_passes([4, 5], range(4))
         o_store(3)
+        o_passes([6], range(3))
         f_quantize(7, 2, 4)
-        o_passes([6, 7], range(4))
+        o_passes([4, 5], [3])
+        o_passes([7], range(3))
+        o_passes([6, 7], [3])
         for n in range(4, 8):
             o_store(n)

@@ -35,10 +35,12 @@ def tile_tied_autoencoder_code_step_t2_kernel(
 
         ident = keep.tile([P, P], F32, name="ident")
         c_raw = [keep.tile([P, 2, H], BF16, name="c_raw%d" % k) for k in range(4)]
+        c_sorted = [keep.tile([P, 2, H], BF16, name="c_sorted%d" % k) if k > 0 else None for k in range(4)]
         c_grp = keep.tile([P, 4 * M], BF16, name="c_grp", align_bytes=64)
         c_codes = keep.tile([P, M], U32, name="c_codes", align_bytes=64)
         c_planes = keep.tile([P, M], U8, name="c_planes", align_bytes=64)
-        x_sb = [keep.tile([P, SLOTS, N], BF16, name="x_sb%d" % s) for s in range(HALVES)]
+        x_sb = [[keep.tile([P, 2, N], BF16, name="x_sb%d_%d" % (s, j)) for j in range(2)] if s == 0 else None for s in range(HALVES)]
+        x_all = [keep.tile([P, SLOTS, N], BF16, name="x_sb%d" % s) if s > 0 else None for s in range(HALVES)]
         wd_sb = keep.tile([P, 2 * D], U8, name="wd_sb", align_bytes=64)
         wd_pl = keep.tile([P, D], U8, name="wd_pl", align_bytes=64)
         pt_raw = keep.tile([P, 2, 2 * M], U8, name="pt_raw", align_bytes=64)
@@ -60,34 +62,41 @@ def tile_tied_autoencoder_code_step_t2_kernel(
             nc.sync.dma_start(out=c_raw[k][:], in_=c_view[k // 2][:, 2 * (k % 2) : 2 * (k % 2) + 2, :])
 
         def load_x(s):
-            nc.sync.dma_start(out=x_sb[s][:], in_=x_view[s % 2][:, :, N * (s // 2) : N * (s // 2 + 1)])
+            nc.sync.dma_start(out=x_all[s][:], in_=x_view[s % 2][:, :, N * (s // 2) : N * (s // 2 + 1)])
+
+        def load_x_first(j):
+            nc.sync.dma_start(out=x_sb[0][j][:], in_=x_view[0][:, 2 * j : 2 * j + 2, 0:N])
+
+        def x_row(s, t):
+            return x_sb[0][t // 2][:, t % 2, :] if s == 0 else x_all[s][:, t, :]
 
         def load_wd(lo, hi):
             nc.sync.dma_start(
                 out=wd_sb[:, 2 * lo : 2 * hi].bitcast(I32), in_=wd_words[0][:, 2 * lo : 2 * hi].bitcast(I32)
             )
 
-        make_identity(nc, ident[:])
         nc.vector.memset(wd_pl[:].bitcast(I32), 0)
         nc.vector.memset(pt_plraw[:].rearrange("p g n -> p (g n)").bitcast(I32), 0)
         nc.vector.memset(wb_pl[:].rearrange("p g n -> p (g n)").bitcast(I32), 0)
+        make_identity(nc, ident[:])
 
         load_c(0)
         load_wd(0, N)
         load_c(1)
+        load_c(2)
         for r in range(4):
             nc.scalar.dma_start(out=wd_pl[r:P:32, :].bitcast(I32), in_=wd_scales[0][r:16:4, :].bitcast(I32))
-        load_x(0)
-        load_c(2)
-        load_c(3)
-        nc.sync.dma_start(out=pt_raw[:].bitcast(I32), in_=pt_words.rearrange("g p w -> p g w").bitcast(I32))
-        load_x(1)
-        load_wd(N, D)
         for r in range(4):
-            nc.sync.dma_start(
+            nc.gpsimd.dma_start(
                 out=pt_plraw[r:P:32, :, :].bitcast(I32),
                 in_=pt_scales[:, r:16:4, :].rearrange("g q n -> q g n").bitcast(I32),
             )
+        load_c(3)
+        load_x_first(0)
+        nc.sync.dma_start(out=pt_raw[:].bitcast(I32), in_=pt_words.rearrange("g p w -> p g w").bitcast(I32))
+        load_x_first(1)
+        load_x(1)
+        load_wd(N, D)
         load_x(2)
         nc.sync.dma_start(out=a_sb[:], in_=a.rearrange("(g p t) -> p g t", p=P, t=SLOTS))
         load_x(3)
@@ -101,7 +110,7 @@ def tile_tied_autoencoder_code_step_t2_kernel(
             load_x(s)
         nc.sync.dma_start(out=rate_sb[:], in_=rate.partition_broadcast(P))
 
-        ring = {"size": 4, "next": 0}
+        ring = {"size": 5, "next": 0}
 
         def bank():
             k = ring["next"] % ring["size"]
@@ -113,13 +122,22 @@ def tile_tied_autoencoder_code_step_t2_kernel(
             turned = psum.tile([P, N], F32, name="turned_c", tag=tag)
             for i in range(count):
                 k, j = divmod(first + i, 2)
-                words = c_raw[k][:, j, :].bitcast(F32)
                 for u in range(2):
                     lo = P * (2 * i + u)
-                    nc.tensor.transpose(turned[:, lo : lo + P], words[:, u : 2 * P : 2], ident[:])
+                    if k == 0:
+                        words = c_raw[k][:, j, :].bitcast(F32)[:, u : 2 * P : 2]
+                    else:
+                        words = c_sorted[k][:, j, :].bitcast(F32)[:, P * u : P * (u + 1)]
+                    nc.tensor.transpose(turned[:, lo : lo + P], words, ident[:])
             nc.scalar.copy(
                 out=c_grp[:, N * first : N * (first + count)].bitcast(F32).rearrange("p (i r u) -> p i r u", i=count, u=2),
                 in_=turned[:, : 2 * P * count].rearrange("p (i u r) -> p i r u", i=count, u=2),
+            )
+
+        def sort_c(k):
+            nc.vector.tensor_copy(
+                out=c_sorted[k][:].bitcast(F32).rearrange("p j (u m) -> p j u m", u=2),
+                in_=c_raw[k][:].bitcast(F32).rearrange("p j (m u) -> p j u m", u=2),
             )
 
         def quantize_c(first, count):
@@ -171,7 +189,7 @@ def tile_tied_autoencoder_code_step_t2_kernel(
             b = e_bank.pop((s, t))
             nc.vector.tensor_tensor(
                 out=e32[s][:, t, :].rearrange("p (u m e) -> p u m e", u=2, e=2),
-                in0=x_sb[s][:, t, :].rearrange("p (m u e) -> p u m e", u=2, e=2),
+                in0=x_row(s, t).rearrange("p (m u e) -> p u m e", u=2, e=2),
                 in1=b[:].rearrange("p (m u e) -> p u m e", u=2, e=2),
                 op=ALU.subtract,
             )
@@ -184,7 +202,7 @@ def tile_tied_autoencoder_code_step_t2_kernel(
             nc.scalar.copy(out=dst, in_=b[:].rearrange("p (m u e) -> p u m e", u=2, e=2))
             nc.gpsimd.tensor_tensor(
                 out=dst,
-                in0=x_sb[s][:, t, :].rearrange("p (m u e) -> p u m e", u=2, e=2),
+                in0=x_row(s, t).rearrange("p (m u e) -> p u m e", u=2, e=2),
                 in1=dst,
                 op=ALU.subtract,
             )
@@ -216,7 +234,7 @@ def tile_tied_autoencoder_code_step_t2_kernel(
         def g_pass(h, t, k):
             ch, g = divmod(h, 2)
             if k == 0:
-                e_bank[("g", h, t)] = bank()
+                e_bank[("g", h, t)] = bank() if h > 0 or t == 3 else psum.tile([P, N], F32, name="first_g", tag="bank%d" % (5 + t))
             tile_no = 4 * g + t
             nc.tensor.matmul_mx(
                 out=e_bank[("g", h, t)][:],
@@ -303,32 +321,56 @@ def tile_tied_autoencoder_code_step_t2_kernel(
         def o_passes(tiles, chunks):
             for n in tiles:
                 for ch in chunks:
-                    o_pass(n, ch, "bank%d" % (4 + n % 4))
+                    o_pass(n, ch, "bank%d" % (4 + (n + 1) % 4))
 
-        turn_c(0, 1, "bank4")
+        turn_c(0, 1, "bank7")
         turn_c(1, 1, "bank5")
-        turn_c(2, 2, "bank6")
+        sort_c(1)
         quantize_c(0, 1)
+        sort_c(2)
         quantize_c(1, 1)
-        quantize_c(2, 2)
-        for t in range(4):
-            e_tile(0, t)
+        turn_c(2, 2, "bank6")
+        e_matmul(0, 0)
         turn_c(4, 2, "bank7")
-        turn_c(6, 2, "bank4")
-        permute_pt(0)
+        sort_c(3)
+        quantize_c(2, 2)
+        e_matmul(0, 1)
+        e_subtract(0, 0)
+        e_matmul(0, 2)
+        turn_c(6, 2, "bank5")
         quantize_c(4, 2)
-        quantize_c(6, 2)
+        e_subtract(0, 1)
+        e_subtract(0, 2)
+        e_tile(0, 3)
         e_group(0)
-        permute_pt(1)
+        quantize_c(6, 2)
         for t in range(4):
             e_tile(1, t)
         e_group(1)
+        for t in range(4):
+            e_matmul(2, t)
+        e_subtract_aside(2, 0)
+        permute_pt(0)
         permute_pt_scales(0)
         e_quantize(0)
+        for t in range(4):
+            g_pass(0, t, 0)
+        permute_pt(1)
         permute_pt_scales(1)
-        e_tile(2, 0)
+        e_quantize(1)
+        for t in range(4):
+            g_pass(0, t, 1)
+        for t in range(1, 4):
+            e_subtract(2, t)
+        e_group_half(2, 0)
+        f_add(0, 0)
+        e_matmul(3, 0)
+        e_subtract_aside(3, 0)
+        e_group_half(2, 1)
+        for t in range(1, 4):
+            f_add(0, t)
 
-        for s in range(2, HALVES):
+        for s in range(3, HALVES):
             h = s - 2
             e_tile(s, 1)
             e_tile(s, 2)
@@ -338,7 +380,7 @@ def tile_tied_autoencoder_code_step_t2_kernel(
             e_quantize(s - 1)
             e_tile(s, 3)
             if h >= 2:
-                o_passes(range(2 * (h % 2), 2 * (h % 2) + 2), [h // 2 - 1])
+                o_passes(range(2 * (h % 2), 2 + (h % 2)), [h // 2 - 1])
             e_group_half(s, 0)
             if h >= 1:
                 f_quantize(h - 1, 0, 4)
@@ -349,48 +391,48 @@ def tile_tied_autoencoder_code_step_t2_kernel(
             e_group_half(s, 1)
             for t in range(1, 4):
                 f_tile(h, t)
-        o_passes(range(2), [2])
+        o_passes(range(3), [2])
+        ring["size"] = 4
         f_turn(5, 0)
-        g_pass(6, 0, 0)
-        o_passes(range(2, 4), [2])
-        g_pass(6, 1, 0)
         f_turn(5, 1)
+        g_pass(6, 0, 0)
+        g_pass(6, 1, 0)
         e_quantize(7)
-        f_quantize(5, 0, 2)
         g_pass(6, 0, 1)
         g_pass(6, 1, 1)
         f_add(6, 0)
+        g_matmul(6, 2)
         f_add(6, 1)
-        f_tile(6, 2)
-        f_tile(6, 3)
+        g_matmul(6, 3)
+        f_quantize(5, 0, 4)
+        f_add(6, 2)
+        f_add(6, 3)
         g_matmul(7, 0)
-        f_turn(6, 0)
-        f_quantize(5, 2, 4)
-        f_add(7, 0)
         g_matmul(7, 1)
+        o_passes([3], [0, 1])
+        f_turn(6, 0)
         f_turn(6, 1)
-        f_quantize(6, 0, 2)
+        f_add(7, 0)
         f_add(7, 1)
         g_matmul(7, 2)
-        o_passes([0, 1], [3])
-        f_quantize(6, 2, 4)
-        f_add(7, 2)
+        f_quantize(6, 0, 2)
         g_matmul(7, 3)
-        o_passes([2, 3], [3])
-        o_store(0)
+        f_add(7, 2)
+        f_quantize(6, 2, 4)
+        o_passes(range(3), [3])
+        o_passes([3], [2, 3])
         f_add(7, 3)
+        o_store(0)
         f_turn(7, 0)
+        f_turn(7, 1)
         o_store(1)
         o_passes([4], range(3))
-        f_turn(7, 1)
-        o_store(2)
-        o_passes([5], range(3))
         f_quantize(7, 0, 2)
-        o_store(3)
-        o_passes([6], range(3))
+        o_store(2)
+        o_passes([5], range(4))
+        o_passes([4], [3])
         f_quantize(7, 2, 4)
-        o_passes([4, 5], [3])
-        o_passes([7], range(3))
-        o_passes([6, 7], [3])
-        for n in range(4, 8):
+        o_store(3)
+        o_passes([6, 7], range(4))
+        for n in (5, 4, 6, 7):
             o_store(n)

@@ -21,6 +21,7 @@ N = 512
 CHUNKS = D // N
 HALVES = 2 * CHUNKS
 SLOTS = 4
+SPLIT = 384
 
 
 def tile_tied_autoencoder_code_step_t2_kernel(
@@ -185,7 +186,7 @@ def tile_tied_autoencoder_code_step_t2_kernel(
 
         def e_subtract(s, t):
             if t == 0:
-                e32[s] = work.tile([P, SLOTS, N], F32, name="e32", bufs=4)
+                e32[s] = work.tile([P, SLOTS, N], F32, name="e32", bufs=6)
             b = e_bank.pop((s, t))
             nc.vector.tensor_tensor(
                 out=e32[s][:, t, :].rearrange("p (u m e) -> p u m e", u=2, e=2),
@@ -196,10 +197,13 @@ def tile_tied_autoencoder_code_step_t2_kernel(
 
         def e_subtract_aside(s, t):
             if t == 0:
-                e32[s] = work.tile([P, SLOTS, N], F32, name="e32", bufs=4)
+                e32[s] = work.tile([P, SLOTS, N], F32, name="e32", bufs=6)
             b = e_bank.pop((s, t))
             dst = e32[s][:, t, :].rearrange("p (u m e) -> p u m e", u=2, e=2)
             nc.scalar.copy(out=dst, in_=b[:].rearrange("p (m u e) -> p u m e", u=2, e=2))
+
+        def e_subtract_pool(s, t):
+            dst = e32[s][:, t, :].rearrange("p (u m e) -> p u m e", u=2, e=2)
             nc.gpsimd.tensor_tensor(
                 out=dst,
                 in0=x_row(s, t).rearrange("p (m u e) -> p u m e", u=2, e=2),
@@ -212,6 +216,18 @@ def tile_tied_autoencoder_code_step_t2_kernel(
                 e_grp[s] = work.tile([P, N, SLOTS], BF16, name="e_grp", bufs=2, align_bytes=64)
             cols = slice(N // 2 * k, N // 2 * (k + 1))
             nc.scalar.copy(out=e_grp[s][:, cols, :], in_=e32[s][:, :, cols].rearrange("p t n -> p n t"))
+
+        def e_group_shared(s, split):
+            e_grp[s] = work.tile([P, N, SLOTS], BF16, name="e_grp", bufs=2, align_bytes=64)
+            nc.scalar.copy(out=e_grp[s][:, :split, :], in_=e32[s][:, :, :split].rearrange("p t n -> p n t"))
+            nc.gpsimd.tensor_scalar(
+                out=e_grp[s][:, split:, :],
+                in0=e32[s][:, :, split:].rearrange("p t n -> p n t"),
+                scalar1=1.0,
+                scalar2=0.0,
+                op0=ALU.mult,
+                op1=ALU.add,
+            )
 
         def e_group(s):
             e_grp[s] = work.tile([P, N, SLOTS], BF16, name="e_grp", bufs=2, align_bytes=64)
@@ -266,7 +282,7 @@ def tile_tied_autoencoder_code_step_t2_kernel(
 
         def f_turn(h, pair):
             if pair == 0:
-                f_grp[h] = work.tile([P, SLOTS * P * 4], BF16, name="f_grp", bufs=3, align_bytes=64)
+                f_grp[h] = work.tile([P, SLOTS * P * 4], BF16, name="f_grp", bufs=5, align_bytes=64)
             turned = bank()
             for i in range(2):
                 words = f_sb[h][:, 2 * pair + i, :].bitcast(F32)
@@ -342,8 +358,8 @@ def tile_tied_autoencoder_code_step_t2_kernel(
         e_subtract(0, 1)
         e_subtract(0, 2)
         e_tile(0, 3)
-        e_group(0)
         quantize_c(6, 2)
+        e_group_shared(0, 256)
         for t in range(4):
             e_tile(1, t)
         e_group(1)
@@ -358,71 +374,76 @@ def tile_tied_autoencoder_code_step_t2_kernel(
         permute_pt(1)
         permute_pt_scales(1)
         e_quantize(1)
+        e_subtract_pool(2, 0)
+        e_matmul(3, 0)
+        e_subtract_aside(3, 0)
         for t in range(4):
             g_pass(0, t, 1)
         for t in range(1, 4):
             e_subtract(2, t)
-        e_group_half(2, 0)
-        f_add(0, 0)
-        e_matmul(3, 0)
-        e_subtract_aside(3, 0)
-        e_group_half(2, 1)
-        for t in range(1, 4):
+        e_group_shared(2, SPLIT)
+        e_subtract_pool(3, 0)
+        for t in range(4):
             f_add(0, t)
 
         for s in range(3, HALVES):
             h = s - 2
-            e_tile(s, 1)
-            e_tile(s, 2)
-            if h >= 1:
-                f_turn(h - 1, 0)
-                f_turn(h - 1, 1)
-            e_quantize(s - 1)
-            e_tile(s, 3)
-            if h >= 2:
-                o_passes(range(2 * (h % 2), 2 + (h % 2)), [h // 2 - 1])
-            e_group_half(s, 0)
-            if h >= 1:
-                f_quantize(h - 1, 0, 4)
-            f_tile(h, 0)
+            e_matmul(s, 1)
             if s + 1 < HALVES:
                 e_matmul(s + 1, 0)
                 e_subtract_aside(s + 1, 0)
-            e_group_half(s, 1)
-            for t in range(1, 4):
+            e_matmul(s, 2)
+            e_matmul(s, 3)
+            if h >= 3:
+                o_passes(range(2) if h % 2 == 1 else [2], [(h - 1) // 2 - 1])
+            e_subtract(s, 1)
+            f_turn(h - 1, 0)
+            f_turn(h - 1, 1)
+            e_quantize(s - 1)
+            e_subtract(s, 2)
+            e_subtract(s, 3)
+            e_group_shared(s, SPLIT)
+            if h % 2 == 0:
+                f_quantize(h - 2, 0, 4)
+            if s + 1 < HALVES:
+                e_subtract_pool(s + 1, 0)
+            for t in range(4):
                 f_tile(h, t)
-        o_passes(range(3), [2])
         ring["size"] = 4
+        o_passes([2], [1])
+        g_pass(6, 0, 0)
+        o_passes([3], [0, 1])
+        f_quantize(4, 0, 4)
+        e_quantize(7)
+        f_quantize(1, 0, 4)
         f_turn(5, 0)
         f_turn(5, 1)
-        g_pass(6, 0, 0)
-        g_pass(6, 1, 0)
-        e_quantize(7)
+        o_passes(range(2), [2])
         g_pass(6, 0, 1)
-        g_pass(6, 1, 1)
+        g_matmul(6, 1)
+        o_passes(range(2, 4), [2])
         f_add(6, 0)
         g_matmul(6, 2)
         f_add(6, 1)
         g_matmul(6, 3)
-        f_quantize(5, 0, 4)
         f_add(6, 2)
         f_add(6, 3)
         g_matmul(7, 0)
         g_matmul(7, 1)
-        o_passes([3], [0, 1])
         f_turn(6, 0)
         f_turn(6, 1)
         f_add(7, 0)
         f_add(7, 1)
+        f_quantize(3, 0, 4)
         g_matmul(7, 2)
-        f_quantize(6, 0, 2)
         g_matmul(7, 3)
+        f_quantize(6, 0, 2)
         f_add(7, 2)
         f_quantize(6, 2, 4)
-        o_passes(range(3), [3])
-        o_passes([3], [2, 3])
+        o_passes(range(4), [3])
         f_add(7, 3)
         o_store(0)
+        f_quantize(5, 0, 4)
         f_turn(7, 0)
         f_turn(7, 1)
         o_store(1)

@@ -22,6 +22,7 @@ CHUNKS = D // N
 HALVES = 2 * CHUNKS
 SLOTS = 4
 SPLIT = 384
+SPLIT_ODD = 448
 
 
 def tile_tied_autoencoder_code_step_t2_kernel(
@@ -36,7 +37,6 @@ def tile_tied_autoencoder_code_step_t2_kernel(
 
         ident = keep.tile([P, P], F32, name="ident")
         c_raw = [keep.tile([P, 2, H], BF16, name="c_raw%d" % k) for k in range(4)]
-        c_sorted = [keep.tile([P, 2, H], BF16, name="c_sorted%d" % k) if k > 0 else None for k in range(4)]
         c_grp = keep.tile([P, 4 * M], BF16, name="c_grp", align_bytes=64)
         c_codes = keep.tile([P, M], U32, name="c_codes", align_bytes=64)
         c_planes = keep.tile([P, M], U8, name="c_planes", align_bytes=64)
@@ -82,20 +82,20 @@ def tile_tied_autoencoder_code_step_t2_kernel(
         make_identity(nc, ident[:])
 
         load_c(0)
-        load_wd(0, N)
         load_c(1)
+        load_wd(0, N)
+        for r in range(4):
+            nc.sync.dma_start(out=wd_pl[r:P:32, :].bitcast(I32), in_=wd_scales[0][r:16:4, :].bitcast(I32))
+        nc.sync.dma_start(out=pt_raw[:].bitcast(I32), in_=pt_words.rearrange("g p w -> p g w").bitcast(I32))
         load_c(2)
+        load_x_first(0)
+        load_c(3)
+        load_x_first(1)
         for r in range(4):
-            nc.scalar.dma_start(out=wd_pl[r:P:32, :].bitcast(I32), in_=wd_scales[0][r:16:4, :].bitcast(I32))
-        for r in range(4):
-            nc.gpsimd.dma_start(
+            nc.sync.dma_start(
                 out=pt_plraw[r:P:32, :, :].bitcast(I32),
                 in_=pt_scales[:, r:16:4, :].rearrange("g q n -> q g n").bitcast(I32),
             )
-        load_c(3)
-        load_x_first(0)
-        nc.sync.dma_start(out=pt_raw[:].bitcast(I32), in_=pt_words.rearrange("g p w -> p g w").bitcast(I32))
-        load_x_first(1)
         load_x(1)
         load_wd(N, D)
         load_x(2)
@@ -125,20 +125,11 @@ def tile_tied_autoencoder_code_step_t2_kernel(
                 k, j = divmod(first + i, 2)
                 for u in range(2):
                     lo = P * (2 * i + u)
-                    if k == 0:
-                        words = c_raw[k][:, j, :].bitcast(F32)[:, u : 2 * P : 2]
-                    else:
-                        words = c_sorted[k][:, j, :].bitcast(F32)[:, P * u : P * (u + 1)]
+                    words = c_raw[k][:, j, :].bitcast(F32)[:, u : 2 * P : 2]
                     nc.tensor.transpose(turned[:, lo : lo + P], words, ident[:])
             nc.scalar.copy(
                 out=c_grp[:, N * first : N * (first + count)].bitcast(F32).rearrange("p (i r u) -> p i r u", i=count, u=2),
                 in_=turned[:, : 2 * P * count].rearrange("p (i u r) -> p i r u", i=count, u=2),
-            )
-
-        def sort_c(k):
-            nc.vector.tensor_copy(
-                out=c_sorted[k][:].bitcast(F32).rearrange("p j (u m) -> p j u m", u=2),
-                in_=c_raw[k][:].bitcast(F32).rearrange("p j (m u) -> p j u m", u=2),
             )
 
         def quantize_c(first, count):
@@ -185,7 +176,7 @@ def tile_tied_autoencoder_code_step_t2_kernel(
             )
 
         def e_subtract(s, t):
-            if t == 0:
+            if s not in e32:
                 e32[s] = work.tile([P, SLOTS, N], F32, name="e32", bufs=6)
             b = e_bank.pop((s, t))
             nc.vector.tensor_tensor(
@@ -196,7 +187,7 @@ def tile_tied_autoencoder_code_step_t2_kernel(
             )
 
         def e_subtract_aside(s, t):
-            if t == 0:
+            if s not in e32:
                 e32[s] = work.tile([P, SLOTS, N], F32, name="e32", bufs=6)
             b = e_bank.pop((s, t))
             dst = e32[s][:, t, :].rearrange("p (u m e) -> p u m e", u=2, e=2)
@@ -218,8 +209,17 @@ def tile_tied_autoencoder_code_step_t2_kernel(
             nc.scalar.copy(out=e_grp[s][:, cols, :], in_=e32[s][:, :, cols].rearrange("p t n -> p n t"))
 
         def e_group_shared(s, split):
+            e_group_scalar(s, split)
+            e_group_pool(s, split)
+
+        def e_group_scalar(s, split):
             e_grp[s] = work.tile([P, N, SLOTS], BF16, name="e_grp", bufs=2, align_bytes=64)
             nc.scalar.copy(out=e_grp[s][:, :split, :], in_=e32[s][:, :, :split].rearrange("p t n -> p n t"))
+
+        def e_group_vector(s, split):
+            nc.vector.tensor_copy(out=e_grp[s][:, split:, :], in_=e32[s][:, :, split:].rearrange("p t n -> p n t"))
+
+        def e_group_pool(s, split):
             nc.gpsimd.tensor_scalar(
                 out=e_grp[s][:, split:, :],
                 in0=e32[s][:, :, split:].rearrange("p t n -> p n t"),
@@ -320,6 +320,14 @@ def tile_tied_autoencoder_code_step_t2_kernel(
                 stop=(ch == CHUNKS - 1),
             )
 
+        def o_store_last(n):
+            g, t = divmod(n, 4)
+            for k in range(2):
+                cols = slice(H // 2 * k, H // 2 * (k + 1))
+                o_half = work.tile([P, H // 2], F32, name="o_half", bufs=2)
+                nc.vector.tensor_tensor(out=o_half[:], in0=o_bank[n][:, cols], in1=rate_sb[:, cols], op=ALU.mult)
+                nc.sync.dma_start(out=out_view[g][:, t, cols], in_=o_half[:])
+
         def o_store(n):
             g, t = divmod(n, 4)
             o_sb = work.tile([P, H], F32, name="o_sb", bufs=8)
@@ -341,46 +349,45 @@ def tile_tied_autoencoder_code_step_t2_kernel(
 
         turn_c(0, 1, "bank7")
         turn_c(1, 1, "bank5")
-        sort_c(1)
-        quantize_c(0, 1)
-        sort_c(2)
-        quantize_c(1, 1)
         turn_c(2, 2, "bank6")
+        quantize_c(0, 1)
+        quantize_c(1, 1)
+        permute_pt(0)
+        permute_pt(1)
         e_matmul(0, 0)
         turn_c(4, 2, "bank7")
-        sort_c(3)
         quantize_c(2, 2)
         e_matmul(0, 1)
         e_subtract(0, 0)
         e_matmul(0, 2)
         turn_c(6, 2, "bank5")
-        quantize_c(4, 2)
+        permute_pt_scales(0)
         e_subtract(0, 1)
+        quantize_c(4, 2)
         e_subtract(0, 2)
         e_tile(0, 3)
         quantize_c(6, 2)
         e_group_shared(0, 256)
         for t in range(4):
             e_tile(1, t)
-        e_group(1)
+        e_group_scalar(1, 320)
         for t in range(4):
             e_matmul(2, t)
         e_subtract_aside(2, 0)
-        permute_pt(0)
-        permute_pt_scales(0)
         e_quantize(0)
         for t in range(4):
             g_pass(0, t, 0)
-        permute_pt(1)
         permute_pt_scales(1)
+        e_group_vector(1, 320)
+        e_subtract(2, 1)
         e_quantize(1)
         e_subtract_pool(2, 0)
         e_matmul(3, 0)
         e_subtract_aside(3, 0)
         for t in range(4):
             g_pass(0, t, 1)
-        for t in range(1, 4):
-            e_subtract(2, t)
+        e_subtract(2, 2)
+        e_subtract(2, 3)
         e_group_shared(2, SPLIT)
         e_subtract_pool(3, 0)
         for t in range(4):
@@ -399,10 +406,13 @@ def tile_tied_autoencoder_code_step_t2_kernel(
             e_subtract(s, 1)
             f_turn(h - 1, 0)
             f_turn(h - 1, 1)
-            e_quantize(s - 1)
+            if s % 2 == 0:
+                e_quantize(s - 1)
             e_subtract(s, 2)
+            if s % 2 == 1:
+                e_quantize(s - 1)
             e_subtract(s, 3)
-            e_group_shared(s, SPLIT)
+            e_group_shared(s, SPLIT if s % 2 == 0 or s == HALVES - 1 else SPLIT_ODD)
             if h % 2 == 0:
                 f_quantize(h - 2, 0, 4)
             if s + 1 < HALVES:
@@ -455,5 +465,6 @@ def tile_tied_autoencoder_code_step_t2_kernel(
         f_quantize(7, 2, 4)
         o_store(3)
         o_passes([6, 7], range(4))
-        for n in (5, 4, 6, 7):
+        for n in (5, 4, 6):
             o_store(n)
+        o_store_last(7)

@@ -21,6 +21,7 @@ N = 512
 CHUNKS = D // N
 HALVES = 2 * CHUNKS
 SLOTS = 4
+MOVING_CODES, MOVING_SCALES, STILL_CODES, STILL_SCALES = 0, 64, 128, 192
 SPLIT = 384
 SPLIT_ODD = 448
 
@@ -35,25 +36,30 @@ def tile_tied_autoencoder_code_step_t2_kernel(
         psum = ctx.enter_context(tc.psum_pool(name="psum", bufs=1))
         ctx.enter_context(tc.manual_schedule())
 
+        def placed(pool, name, columns, dtype, size, start, bufs=1):
+            lead = start // size
+            whole = pool.tile([P, lead + columns], dtype, name=name, bufs=bufs, align_bytes=256)
+            return whole[:, lead : lead + columns]
+
         ident = keep.tile([P, P], F32, name="ident")
         c_raw = [keep.tile([P, 2, H], BF16, name="c_raw%d" % k) for k in range(4)]
         c_grp = keep.tile([P, 4 * M], BF16, name="c_grp", align_bytes=64)
-        c_codes = keep.tile([P, M], U32, name="c_codes", align_bytes=64)
-        c_planes = keep.tile([P, M], U8, name="c_planes", align_bytes=64)
+        c_codes = placed(keep, "c_codes", M, U32, 4, STILL_CODES)
+        c_planes = placed(keep, "c_planes", M, U8, 1, STILL_SCALES)
         x_sb = [[keep.tile([P, 2, N], BF16, name="x_sb%d_%d" % (s, j)) for j in range(2)] if s == 0 else None for s in range(HALVES)]
         x_all = [keep.tile([P, SLOTS, N], BF16, name="x_sb%d" % s) if s > 0 else None for s in range(HALVES)]
-        wd_sb = keep.tile([P, 2 * D], U8, name="wd_sb", align_bytes=64)
-        wd_pl = keep.tile([P, D], U8, name="wd_pl", align_bytes=64)
+        wd_sb = placed(keep, "wd_sb", 2 * D, U8, 1, MOVING_CODES)
+        wd_pl = placed(keep, "wd_pl", D, U8, 1, MOVING_SCALES)
         pt_raw = keep.tile([P, 2, 2 * M], U8, name="pt_raw", align_bytes=64)
-        pt_sb = keep.tile([P, 2, 2 * M], U8, name="pt_sb", align_bytes=64)
+        pt_sb = placed(keep, "pt_sb", 4 * M, U8, 1, STILL_CODES).rearrange("p (g w) -> p g w", g=2)
         pt_plraw = keep.tile([P, 2, M], U8, name="pt_plraw", align_bytes=64)
-        pt_pl = keep.tile([P, 2, M], U8, name="pt_pl", align_bytes=64)
-        wb_sb = keep.tile([P, CHUNKS, 2 * H], U8, name="wb_sb", align_bytes=64)
-        wb_pl = keep.tile([P, CHUNKS, H], U8, name="wb_pl", align_bytes=64)
+        pt_pl = placed(keep, "pt_pl", 2 * M, U8, 1, STILL_SCALES).rearrange("p (g w) -> p g w", g=2)
+        wb_sb = placed(keep, "wb_sb", CHUNKS * 2 * H, U8, 1, MOVING_CODES).rearrange("p (g w) -> p g w", g=CHUNKS)
+        wb_pl = placed(keep, "wb_pl", CHUNKS * H, U8, 1, MOVING_SCALES).rearrange("p (g w) -> p g w", g=CHUNKS)
         a_sb = keep.tile([P, 2, SLOTS], BF16, name="a_sb")
         rate_sb = keep.tile([P, H], BF16, name="rate_sb")
-        f_codes = [keep.tile([P, N], U32, name="f_codes%d" % h, align_bytes=64) for h in range(HALVES)]
-        f_planes = [keep.tile([P, N], U8, name="f_planes%d" % h, align_bytes=64) for h in range(HALVES)]
+        f_codes = [placed(keep, "f_codes%d" % h, N, U32, 4, STILL_CODES) for h in range(HALVES)]
+        f_planes = [placed(keep, "f_planes%d" % h, N, U8, 1, STILL_SCALES) for h in range(HALVES)]
 
         c_view = c.rearrange("(g p t) k -> g p t k", p=P, t=SLOTS)
         x_view = x.rearrange("(g p t) d -> g p t d", p=P, t=SLOTS)
@@ -239,8 +245,8 @@ def tile_tied_autoencoder_code_step_t2_kernel(
                 )
 
         def e_quantize(s):
-            e_codes[s] = work.tile([P, N], U32, name="e_codes", bufs=4, align_bytes=64)
-            e_planes[s] = work.tile([P, N], U8, name="e_planes", bufs=4, align_bytes=64)
+            e_codes[s] = placed(work, "e_codes", N, U32, 4, MOVING_CODES, bufs=4)
+            e_planes[s] = placed(work, "e_planes", N, U8, 1, MOVING_SCALES, bufs=4)
             nc.vector.quantize_mx(
                 out=e_codes[s][:].bitcast(E4M3X4),
                 scales=e_planes[s][:],

@@ -23,7 +23,6 @@ HALVES = 2 * CHUNKS
 SLOTS = 4
 MOVING_CODES, MOVING_SCALES, STILL_CODES, STILL_SCALES = 0, 64, 128, 192
 SPLIT = 384
-SPLIT_ODD = 448
 
 
 def tile_tied_autoencoder_code_step_t2_kernel(
@@ -49,7 +48,8 @@ def tile_tied_autoencoder_code_step_t2_kernel(
         x_sb = [[keep.tile([P, 2, N], BF16, name="x_sb%d_%d" % (s, j)) for j in range(2)] if s == 0 else None for s in range(HALVES)]
         x_all = [keep.tile([P, SLOTS, N], BF16, name="x_sb%d" % s) if s > 0 else None for s in range(HALVES)]
         wd_sb = placed(keep, "wd_sb", 2 * D, U8, 1, MOVING_CODES)
-        wd_pl = placed(keep, "wd_pl", D, U8, 1, MOVING_SCALES)
+        wd_pl_first = placed(keep, "wd_pl_first", N, U8, 1, MOVING_SCALES)
+        wd_pl_rest = placed(keep, "wd_pl_rest", D - N, U8, 1, MOVING_SCALES)
         pt_raw = keep.tile([P, 2, 2 * M], U8, name="pt_raw", align_bytes=64)
         pt_sb = placed(keep, "pt_sb", 4 * M, U8, 1, STILL_CODES).rearrange("p (g w) -> p g w", g=2)
         pt_plraw = keep.tile([P, 2, M], U8, name="pt_plraw", align_bytes=64)
@@ -82,16 +82,22 @@ def tile_tied_autoencoder_code_step_t2_kernel(
                 out=wd_sb[:, 2 * lo : 2 * hi].bitcast(I32), in_=wd_words[0][:, 2 * lo : 2 * hi].bitcast(I32)
             )
 
-        nc.vector.memset(wd_pl[:].bitcast(I32), 0)
+        def load_wd_scales(plane, lo, hi):
+            for r in range(4):
+                nc.sync.dma_start(
+                    out=plane[r:P:32, :].bitcast(I32), in_=wd_scales[0][r:16:4, lo:hi].bitcast(I32)
+                )
+
+        nc.vector.memset(wd_pl_first[:].bitcast(I32), 0)
         nc.vector.memset(pt_plraw[:].rearrange("p g n -> p (g n)").bitcast(I32), 0)
+        nc.vector.memset(wd_pl_rest[:].bitcast(I32), 0)
         nc.vector.memset(wb_pl[:].rearrange("p g n -> p (g n)").bitcast(I32), 0)
         make_identity(nc, ident[:])
 
         load_c(0)
         load_c(1)
         load_wd(0, N)
-        for r in range(4):
-            nc.sync.dma_start(out=wd_pl[r:P:32, :].bitcast(I32), in_=wd_scales[0][r:16:4, :].bitcast(I32))
+        load_wd_scales(wd_pl_first, 0, N)
         nc.sync.dma_start(out=pt_raw[:].bitcast(I32), in_=pt_words.rearrange("g p w -> p g w").bitcast(I32))
         load_c(2)
         load_x_first(0)
@@ -104,6 +110,7 @@ def tile_tied_autoencoder_code_step_t2_kernel(
             )
         load_x(1)
         load_wd(N, D)
+        load_wd_scales(wd_pl_rest, N, D)
         load_x(2)
         nc.sync.dma_start(out=a_sb[:], in_=a.rearrange("(g p t) -> p g t", p=P, t=SLOTS))
         load_x(3)
@@ -176,7 +183,7 @@ def tile_tied_autoencoder_code_step_t2_kernel(
                 lhsT=c_codes[:, rows].bitcast(E4M3X4),
                 lhsT_scale=c_planes[:, rows],
                 rhs=wd_sb[:, 2 * N * ch : 2 * N * (ch + 1)].bitcast(E2M1X4),
-                rhs_scale=wd_pl[:, N * ch : N * (ch + 1)],
+                rhs_scale=wd_pl_first[:] if ch == 0 else wd_pl_rest[:, N * (ch - 1) : N * ch],
                 start=True,
                 stop=True,
             )
@@ -361,17 +368,18 @@ def tile_tied_autoencoder_code_step_t2_kernel(
         permute_pt(0)
         permute_pt(1)
         e_matmul(0, 0)
+        e_matmul(0, 1)
         turn_c(4, 2, "bank7")
         quantize_c(2, 2)
-        e_matmul(0, 1)
         e_subtract(0, 0)
+        e_subtract(0, 1)
         e_matmul(0, 2)
         turn_c(6, 2, "bank5")
-        permute_pt_scales(0)
-        e_subtract(0, 1)
+        e_matmul(0, 3)
         quantize_c(4, 2)
         e_subtract(0, 2)
-        e_tile(0, 3)
+        permute_pt_scales(0)
+        e_subtract(0, 3)
         quantize_c(6, 2)
         e_group_shared(0, 256)
         for t in range(4):
@@ -418,7 +426,7 @@ def tile_tied_autoencoder_code_step_t2_kernel(
             if s % 2 == 1:
                 e_quantize(s - 1)
             e_subtract(s, 3)
-            e_group_shared(s, SPLIT if s % 2 == 0 or s == HALVES - 1 else SPLIT_ODD)
+            e_group_shared(s, SPLIT)
             if h % 2 == 0:
                 f_quantize(h - 2, 0, 4)
             if s + 1 < HALVES:

@@ -23,6 +23,7 @@ HALVES = 2 * CHUNKS
 SLOTS = 4
 MOVING_CODES, MOVING_SCALES, STILL_CODES, STILL_SCALES = 0, 64, 128, 192
 SPLIT = 384
+EARLY = 1
 
 
 def tile_tied_autoencoder_code_step_t2_kernel(
@@ -263,7 +264,7 @@ def tile_tied_autoencoder_code_step_t2_kernel(
         def g_pass(h, t, k):
             ch, g = divmod(h, 2)
             if k == 0:
-                e_bank[("g", h, t)] = bank() if h > 0 or t == 3 else psum.tile([P, N], F32, name="first_g", tag="bank%d" % (5 + t))
+                e_bank[("g", h, t)] = bank() if h > 1 or t == 3 or (h == 1 and t >= EARLY) else psum.tile([P, N], F32, name="first_g", tag="bank%d" % (5 + t))
             tile_no = 4 * g + t
             nc.tensor.matmul_mx(
                 out=e_bank[("g", h, t)][:],
@@ -414,6 +415,9 @@ def tile_tied_autoencoder_code_step_t2_kernel(
                 e_matmul(s + 1, 0)
                 e_subtract_aside(s + 1, 0)
             e_matmul(s, 2)
+            if h == 1:
+                for t in range(EARLY):
+                    g_matmul(h, t)
             e_matmul(s, 3)
             if h >= 3:
                 o_passes(range(2) if h % 2 == 1 else [2], [(h - 1) // 2 - 1])
@@ -432,7 +436,9 @@ def tile_tied_autoencoder_code_step_t2_kernel(
             if s + 1 < HALVES:
                 e_subtract_pool(s + 1, 0)
             for t in range(4):
-                f_tile(h, t)
+                if h > 1 or t >= EARLY:
+                    g_matmul(h, t)
+                f_add(h, t)
         ring["size"] = 4
         o_passes([2], [1])
         g_pass(6, 0, 0)
@@ -440,6 +446,7 @@ def tile_tied_autoencoder_code_step_t2_kernel(
         f_quantize(4, 0, 4)
         e_quantize(7)
         f_quantize(1, 0, 4)
+        f_quantize(3, 0, 4)
         f_turn(5, 0)
         f_turn(5, 1)
         o_passes(range(2), [2])
@@ -449,6 +456,7 @@ def tile_tied_autoencoder_code_step_t2_kernel(
         f_add(6, 0)
         g_matmul(6, 2)
         f_add(6, 1)
+        f_quantize(5, 0, 4)
         g_matmul(6, 3)
         f_add(6, 2)
         f_add(6, 3)
@@ -458,7 +466,6 @@ def tile_tied_autoencoder_code_step_t2_kernel(
         f_turn(6, 1)
         f_add(7, 0)
         f_add(7, 1)
-        f_quantize(3, 0, 4)
         g_matmul(7, 2)
         g_matmul(7, 3)
         f_quantize(6, 0, 2)
@@ -467,17 +474,16 @@ def tile_tied_autoencoder_code_step_t2_kernel(
         o_passes(range(4), [3])
         f_add(7, 3)
         o_store(0)
-        f_quantize(5, 0, 4)
         f_turn(7, 0)
         f_turn(7, 1)
         o_store(1)
         o_passes([4], range(3))
-        f_quantize(7, 0, 2)
         o_store(2)
+        f_quantize(7, 0, 2)
         o_passes([5], range(4))
         o_passes([4], [3])
-        f_quantize(7, 2, 4)
         o_store(3)
+        f_quantize(7, 2, 4)
         o_passes([6, 7], range(4))
         for n in (5, 4, 6):
             o_store(n)

@@ -18,12 +18,17 @@ ALU = mybir.AluOpType
 
 P = 128
 N = 512
-CHUNKS = D // N
-HALVES = 2 * CHUNKS
 SLOTS = 4
+GROUPS = M // (P * SLOTS)
+CHUNKS = D // N
+PARTS = GROUPS * CHUNKS
+LAG = 2
+
 MOVING_CODES, MOVING_SCALES, STILL_CODES, STILL_SCALES = 0, 64, 128, 192
-SPLIT = 384
-EARLY = 1
+
+SCALAR_SHARE = 384
+SCALAR_SHARE_PART0 = 256
+SCALAR_SHARE_PART1 = 320
 
 
 def tile_tied_autoencoder_code_step_t2_kernel(
@@ -36,8 +41,8 @@ def tile_tied_autoencoder_code_step_t2_kernel(
         psum = ctx.enter_context(tc.psum_pool(name="psum", bufs=1))
         ctx.enter_context(tc.manual_schedule())
 
-        def placed(pool, name, columns, dtype, size, start, bufs=1):
-            lead = start // size
+        def placed(pool, name, columns, dtype, item_bytes, start, bufs=1):
+            lead = start // item_bytes
             whole = pool.tile([P, lead + columns], dtype, name=name, bufs=bufs, align_bytes=256)
             return whole[:, lead : lead + columns]
 
@@ -46,21 +51,21 @@ def tile_tied_autoencoder_code_step_t2_kernel(
         c_grp = keep.tile([P, 4 * M], BF16, name="c_grp", align_bytes=64)
         c_codes = placed(keep, "c_codes", M, U32, 4, STILL_CODES)
         c_planes = placed(keep, "c_planes", M, U8, 1, STILL_SCALES)
-        x_sb = [[keep.tile([P, 2, N], BF16, name="x_sb%d_%d" % (s, j)) for j in range(2)] if s == 0 else None for s in range(HALVES)]
-        x_all = [keep.tile([P, SLOTS, N], BF16, name="x_sb%d" % s) if s > 0 else None for s in range(HALVES)]
+        x_first = [keep.tile([P, 2, N], BF16, name="x_sb0_%d" % j) for j in range(2)]
+        x_rest = {s: keep.tile([P, SLOTS, N], BF16, name="x_sb%d" % s) for s in range(1, PARTS)}
         wd_sb = placed(keep, "wd_sb", 2 * D, U8, 1, MOVING_CODES)
         wd_pl_first = placed(keep, "wd_pl_first", N, U8, 1, MOVING_SCALES)
         wd_pl_rest = placed(keep, "wd_pl_rest", D - N, U8, 1, MOVING_SCALES)
-        pt_raw = keep.tile([P, 2, 2 * M], U8, name="pt_raw", align_bytes=64)
-        pt_sb = placed(keep, "pt_sb", 4 * M, U8, 1, STILL_CODES).rearrange("p (g w) -> p g w", g=2)
-        pt_plraw = keep.tile([P, 2, M], U8, name="pt_plraw", align_bytes=64)
-        pt_pl = placed(keep, "pt_pl", 2 * M, U8, 1, STILL_SCALES).rearrange("p (g w) -> p g w", g=2)
+        pt_raw = keep.tile([P, GROUPS, 2 * M], U8, name="pt_raw", align_bytes=64)
+        pt_sb = placed(keep, "pt_sb", 4 * M, U8, 1, STILL_CODES).rearrange("p (g w) -> p g w", g=GROUPS)
+        pt_plraw = keep.tile([P, GROUPS, M], U8, name="pt_plraw", align_bytes=64)
+        pt_pl = placed(keep, "pt_pl", 2 * M, U8, 1, STILL_SCALES).rearrange("p (g w) -> p g w", g=GROUPS)
         wb_sb = placed(keep, "wb_sb", CHUNKS * 2 * H, U8, 1, MOVING_CODES).rearrange("p (g w) -> p g w", g=CHUNKS)
         wb_pl = placed(keep, "wb_pl", CHUNKS * H, U8, 1, MOVING_SCALES).rearrange("p (g w) -> p g w", g=CHUNKS)
-        a_sb = keep.tile([P, 2, SLOTS], BF16, name="a_sb")
+        a_sb = keep.tile([P, GROUPS, SLOTS], BF16, name="a_sb")
         rate_sb = keep.tile([P, H], BF16, name="rate_sb")
-        f_codes = [placed(keep, "f_codes%d" % h, N, U32, 4, STILL_CODES) for h in range(HALVES)]
-        f_planes = [placed(keep, "f_planes%d" % h, N, U8, 1, STILL_SCALES) for h in range(HALVES)]
+        f_codes = [placed(keep, "f_codes%d" % h, N, U32, 4, STILL_CODES) for h in range(PARTS)]
+        f_planes = [placed(keep, "f_planes%d" % h, N, U8, 1, STILL_SCALES) for h in range(PARTS)]
 
         c_view = c.rearrange("(g p t) k -> g p t k", p=P, t=SLOTS)
         x_view = x.rearrange("(g p t) d -> g p t d", p=P, t=SLOTS)
@@ -69,14 +74,15 @@ def tile_tied_autoencoder_code_step_t2_kernel(
         def load_c(k):
             nc.sync.dma_start(out=c_raw[k][:], in_=c_view[k // 2][:, 2 * (k % 2) : 2 * (k % 2) + 2, :])
 
-        def load_x(s):
-            nc.sync.dma_start(out=x_all[s][:], in_=x_view[s % 2][:, :, N * (s // 2) : N * (s // 2 + 1)])
-
         def load_x_first(j):
-            nc.sync.dma_start(out=x_sb[0][j][:], in_=x_view[0][:, 2 * j : 2 * j + 2, 0:N])
+            nc.sync.dma_start(out=x_first[j][:], in_=x_view[0][:, 2 * j : 2 * j + 2, 0:N])
 
-        def x_row(s, t):
-            return x_sb[0][t // 2][:, t % 2, :] if s == 0 else x_all[s][:, t, :]
+        def load_x(s):
+            chunk, g = divmod(s, GROUPS)
+            nc.sync.dma_start(out=x_rest[s][:], in_=x_view[g][:, :, N * chunk : N * (chunk + 1)])
+
+        def x_slot(s, t):
+            return x_first[t // 2][:, t % 2, :] if s == 0 else x_rest[s][:, t, :]
 
         def load_wd(lo, hi):
             nc.sync.dma_start(
@@ -85,8 +91,13 @@ def tile_tied_autoencoder_code_step_t2_kernel(
 
         def load_wd_scales(plane, lo, hi):
             for r in range(4):
+                nc.sync.dma_start(out=plane[r:P:32, :].bitcast(I32), in_=wd_scales[0][r:16:4, lo:hi].bitcast(I32))
+
+        def load_scales(planes, rows):
+            for r in range(4):
                 nc.sync.dma_start(
-                    out=plane[r:P:32, :].bitcast(I32), in_=wd_scales[0][r:16:4, lo:hi].bitcast(I32)
+                    out=planes[r:P:32, :, :].bitcast(I32),
+                    in_=rows[:, r:16:4, :].rearrange("g q n -> q g n").bitcast(I32),
                 )
 
         nc.vector.memset(wd_pl_first[:].bitcast(I32), 0)
@@ -100,50 +111,48 @@ def tile_tied_autoencoder_code_step_t2_kernel(
         load_wd(0, N)
         load_wd_scales(wd_pl_first, 0, N)
         nc.sync.dma_start(out=pt_raw[:].bitcast(I32), in_=pt_words.rearrange("g p w -> p g w").bitcast(I32))
-        load_c(2)
-        load_x_first(0)
-        load_c(3)
-        load_x_first(1)
-        for r in range(4):
-            nc.sync.dma_start(
-                out=pt_plraw[r:P:32, :, :].bitcast(I32),
-                in_=pt_scales[:, r:16:4, :].rearrange("g q n -> q g n").bitcast(I32),
-            )
+        for j in range(2):
+            load_c(2 + j)
+            load_x_first(j)
+        load_scales(pt_plraw, pt_scales)
         load_x(1)
         load_wd(N, D)
         load_wd_scales(wd_pl_rest, N, D)
         load_x(2)
         nc.sync.dma_start(out=a_sb[:], in_=a.rearrange("(g p t) -> p g t", p=P, t=SLOTS))
         load_x(3)
-        for r in range(4):
-            nc.sync.dma_start(
-                out=wb_pl[r:P:32, :, :].bitcast(I32),
-                in_=wb_scales[:, r:16:4, :].rearrange("g q n -> q g n").bitcast(I32),
-            )
+        load_scales(wb_pl, wb_scales)
         nc.sync.dma_start(out=wb_sb[:].bitcast(I32), in_=wb_words.rearrange("g p w -> p g w").bitcast(I32))
-        for s in range(4, HALVES):
+        for s in range(4, PARTS):
             load_x(s)
         nc.sync.dma_start(out=rate_sb[:], in_=rate.partition_broadcast(P))
 
-        ring = {"size": 5, "next": 0}
+        free = list(range(8))
+        held = {}
 
-        def bank():
-            k = ring["next"] % ring["size"]
-            ring["next"] = k + 1
-            b = psum.tile([P, N], F32, name="ring%d" % k, tag="bank%d" % k)
-            return b
+        def take_bank(key):
+            k = free.pop(0)
+            bank = psum.tile([P, N], F32, name="bank%d" % k, tag="bank%d" % k)
+            held[key] = (k, bank)
+            return bank
 
-        def turn_c(first, count, tag):
-            turned = psum.tile([P, N], F32, name="turned_c", tag=tag)
+        def read_bank(key):
+            k, bank = held.pop(key)
+            free.append(k)
+            return bank
+
+        def turn_c(first, count):
+            turned = take_bank("c")
             for i in range(count):
                 k, j = divmod(first + i, 2)
                 for u in range(2):
-                    lo = P * (2 * i + u)
                     words = c_raw[k][:, j, :].bitcast(F32)[:, u : 2 * P : 2]
+                    lo = P * (2 * i + u)
                     nc.tensor.transpose(turned[:, lo : lo + P], words, ident[:])
+            grouped = c_grp[:, N * first : N * (first + count)].bitcast(F32)
             nc.scalar.copy(
-                out=c_grp[:, N * first : N * (first + count)].bitcast(F32).rearrange("p (i r u) -> p i r u", i=count, u=2),
-                in_=turned[:, : 2 * P * count].rearrange("p (i u r) -> p i r u", i=count, u=2),
+                out=grouped.rearrange("p (i r u) -> p i r u", i=count, u=2),
+                in_=read_bank("c")[:, : 2 * P * count].rearrange("p (i u r) -> p i r u", i=count, u=2),
             )
 
         def quantize_c(first, count):
@@ -154,103 +163,76 @@ def tile_tied_autoencoder_code_step_t2_kernel(
                 in_=c_grp[:, N * first : N * (first + count)],
             )
 
-        def permute_pt(g):
+        def sort_pt(k):
             nc.vector.tensor_copy(
-                out=pt_sb[:, g, :].bitcast(U16).rearrange("p (j t m) -> p j t m", j=2, t=4),
-                in_=pt_raw[:, g, :].bitcast(U16).rearrange("p (j m t) -> p j t m", j=2, t=4),
+                out=pt_sb[:, k, :].bitcast(U16).rearrange("p (j t m) -> p j t m", j=GROUPS, t=SLOTS),
+                in_=pt_raw[:, k, :].bitcast(U16).rearrange("p (j m t) -> p j t m", j=GROUPS, t=SLOTS),
             )
 
-        def permute_pt_scales(g):
+        def sort_pt_scales(k):
             nc.vector.tensor_copy(
-                out=pt_pl[:, g, :].rearrange("p (j t m) -> p j t m", j=2, t=4),
-                in_=pt_plraw[:, g, :].rearrange("p (j m t) -> p j t m", j=2, t=4),
+                out=pt_pl[:, k, :].rearrange("p (j t m) -> p j t m", j=GROUPS, t=SLOTS),
+                in_=pt_plraw[:, k, :].rearrange("p (j m t) -> p j t m", j=GROUPS, t=SLOTS),
             )
 
-        e32 = {}
-        e_codes = {}
-        e_planes = {}
-        e_grp = {}
-        f_sb = {}
-        f_grp = {}
-        e_bank = {}
+        e32, e_grp, e_codes, e_planes = {}, {}, {}, {}
 
-        def e_matmul(s, t):
-            ch, g = divmod(s, 2)
-            b = bank()
-            e_bank[(s, t)] = b
-            rows = slice(P * (4 * g + t), P * (4 * g + t + 1))
+        def as_stored(ap):
+            return ap.rearrange("p (u m e) -> p u m e", u=2, e=2)
+
+        def into_stored(ap):
+            return ap.rearrange("p (m u e) -> p u m e", u=2, e=2)
+
+        def e_slot(s, t):
+            if s not in e32:
+                e32[s] = work.tile([P, SLOTS, N], F32, name="e32", bufs=6)
+            return e32[s][:, t, :]
+
+        def r_matmul(s, t):
+            chunk, g = divmod(s, GROUPS)
+            rows = slice(P * (SLOTS * g + t), P * (SLOTS * g + t + 1))
             nc.tensor.matmul_mx(
-                out=b[:],
+                out=take_bank(("r", s, t))[:],
                 lhsT=c_codes[:, rows].bitcast(E4M3X4),
                 lhsT_scale=c_planes[:, rows],
-                rhs=wd_sb[:, 2 * N * ch : 2 * N * (ch + 1)].bitcast(E2M1X4),
-                rhs_scale=wd_pl_first[:] if ch == 0 else wd_pl_rest[:, N * (ch - 1) : N * ch],
+                rhs=wd_sb[:, 2 * N * chunk : 2 * N * (chunk + 1)].bitcast(E2M1X4),
+                rhs_scale=wd_pl_first[:] if chunk == 0 else wd_pl_rest[:, N * (chunk - 1) : N * chunk],
                 start=True,
                 stop=True,
             )
 
         def e_subtract(s, t):
-            if s not in e32:
-                e32[s] = work.tile([P, SLOTS, N], F32, name="e32", bufs=6)
-            b = e_bank.pop((s, t))
             nc.vector.tensor_tensor(
-                out=e32[s][:, t, :].rearrange("p (u m e) -> p u m e", u=2, e=2),
-                in0=x_row(s, t).rearrange("p (m u e) -> p u m e", u=2, e=2),
-                in1=b[:].rearrange("p (m u e) -> p u m e", u=2, e=2),
+                out=as_stored(e_slot(s, t)),
+                in0=into_stored(x_slot(s, t)),
+                in1=into_stored(read_bank(("r", s, t))[:]),
                 op=ALU.subtract,
             )
 
-        def e_subtract_aside(s, t):
-            if s not in e32:
-                e32[s] = work.tile([P, SLOTS, N], F32, name="e32", bufs=6)
-            b = e_bank.pop((s, t))
-            dst = e32[s][:, t, :].rearrange("p (u m e) -> p u m e", u=2, e=2)
-            nc.scalar.copy(out=dst, in_=b[:].rearrange("p (m u e) -> p u m e", u=2, e=2))
+        def r_copy(s):
+            nc.scalar.copy(out=as_stored(e_slot(s, 0)), in_=into_stored(read_bank(("r", s, 0))[:]))
 
-        def e_subtract_pool(s, t):
-            dst = e32[s][:, t, :].rearrange("p (u m e) -> p u m e", u=2, e=2)
-            nc.gpsimd.tensor_tensor(
-                out=dst,
-                in0=x_row(s, t).rearrange("p (m u e) -> p u m e", u=2, e=2),
-                in1=dst,
-                op=ALU.subtract,
-            )
+        def e_subtract_gpsimd(s):
+            dst = as_stored(e_slot(s, 0))
+            nc.gpsimd.tensor_tensor(out=dst, in0=into_stored(x_slot(s, 0)), in1=dst, op=ALU.subtract)
 
-        def e_group_half(s, k):
-            if k == 0:
-                e_grp[s] = work.tile([P, N, SLOTS], BF16, name="e_grp", bufs=2, align_bytes=64)
-            cols = slice(N // 2 * k, N // 2 * (k + 1))
-            nc.scalar.copy(out=e_grp[s][:, cols, :], in_=e32[s][:, :, cols].rearrange("p t n -> p n t"))
-
-        def e_group_shared(s, split):
-            e_group_scalar(s, split)
-            e_group_pool(s, split)
-
-        def e_group_scalar(s, split):
+        def e_group_scalar(s, share):
             e_grp[s] = work.tile([P, N, SLOTS], BF16, name="e_grp", bufs=2, align_bytes=64)
-            nc.scalar.copy(out=e_grp[s][:, :split, :], in_=e32[s][:, :, :split].rearrange("p t n -> p n t"))
+            nc.scalar.copy(out=e_grp[s][:, :share, :], in_=e32[s][:, :, :share].rearrange("p t n -> p n t"))
 
-        def e_group_vector(s, split):
-            nc.vector.tensor_copy(out=e_grp[s][:, split:, :], in_=e32[s][:, :, split:].rearrange("p t n -> p n t"))
+        def e_group_vector(s, share):
+            nc.vector.tensor_copy(out=e_grp[s][:, share:, :], in_=e32[s][:, :, share:].rearrange("p t n -> p n t"))
 
-        def e_group_pool(s, split):
+        def e_group(s, share):
+            e_group_scalar(s, share)
             nc.gpsimd.tensor_scalar(
-                out=e_grp[s][:, split:, :],
-                in0=e32[s][:, :, split:].rearrange("p t n -> p n t"),
+                out=e_grp[s][:, share:, :],
+                in0=e32[s][:, :, share:].rearrange("p t n -> p n t"),
                 scalar1=1.0,
                 scalar2=0.0,
                 op0=ALU.mult,
                 op1=ALU.add,
             )
-
-        def e_group(s):
-            e_grp[s] = work.tile([P, N, SLOTS], BF16, name="e_grp", bufs=2, align_bytes=64)
-            for k in range(2):
-                cols = slice(N // 2 * k, N // 2 * (k + 1))
-                nc.scalar.copy(
-                    out=e_grp[s][:, cols, :],
-                    in_=e32[s][:, :, cols].rearrange("p t n -> p n t"),
-                )
 
         def e_quantize(s):
             e_codes[s] = placed(work, "e_codes", N, U32, 4, MOVING_CODES, bufs=4)
@@ -261,230 +243,235 @@ def tile_tied_autoencoder_code_step_t2_kernel(
                 in_=e_grp[s][:].rearrange("p n t -> p (n t)"),
             )
 
+        f_sb, f_grp = {}, {}
+
         def g_pass(h, t, k):
-            ch, g = divmod(h, 2)
+            chunk, g = divmod(h, GROUPS)
             if k == 0:
-                e_bank[("g", h, t)] = bank() if h > 1 or t == 3 or (h == 1 and t >= EARLY) else psum.tile([P, N], F32, name="first_g", tag="bank%d" % (5 + t))
-            tile_no = 4 * g + t
+                take_bank(("g", h, t))
+            n = SLOTS * g + t
             nc.tensor.matmul_mx(
-                out=e_bank[("g", h, t)][:],
-                lhsT=pt_sb[:, k, 2 * P * tile_no : 2 * P * (tile_no + 1)].bitcast(E2M1X4),
-                lhsT_scale=pt_pl[:, k, P * tile_no : P * (tile_no + 1)],
-                rhs=e_codes[2 * ch + k][:].bitcast(E4M3X4),
-                rhs_scale=e_planes[2 * ch + k][:],
+                out=held[("g", h, t)][1][:],
+                lhsT=pt_sb[:, k, 2 * P * n : 2 * P * (n + 1)].bitcast(E2M1X4),
+                lhsT_scale=pt_pl[:, k, P * n : P * (n + 1)],
+                rhs=e_codes[GROUPS * chunk + k][:].bitcast(E4M3X4),
+                rhs_scale=e_planes[GROUPS * chunk + k][:],
                 start=(k == 0),
-                stop=(k == 1),
+                stop=(k == GROUPS - 1),
             )
 
         def g_matmul(h, t):
-            g_pass(h, t, 0)
-            g_pass(h, t, 1)
+            for k in range(GROUPS):
+                g_pass(h, t, k)
 
         def f_add(h, t):
-            g = h % 2
             if t == 0:
-                f_sb[h] = work.tile([P, SLOTS, N], BF16, name="f_sb", bufs=2)
-            b = e_bank.pop(("g", h, t))
+                f_sb[h] = work.tile([P, SLOTS, N], BF16, name="f_sb", bufs=3)
             nc.vector.scalar_tensor_tensor(
                 out=f_sb[h][:, t, :],
                 in0=e32[h][:, t, :],
-                scalar=a_sb[:, g, t : t + 1],
-                in1=b[:],
+                scalar=a_sb[:, h % GROUPS, t : t + 1],
+                in1=read_bank(("g", h, t))[:],
                 op0=ALU.mult,
                 op1=ALU.add,
             )
 
-        def f_turn(h, pair):
-            if pair == 0:
-                f_grp[h] = work.tile([P, SLOTS * P * 4], BF16, name="f_grp", bufs=5, align_bytes=64)
-            turned = bank()
-            for i in range(2):
-                words = f_sb[h][:, 2 * pair + i, :].bitcast(F32)
-                for u in range(2):
-                    lo = P * (2 * i + u)
-                    nc.tensor.transpose(turned[:, lo : lo + P], words[:, P * u : P * (u + 1)], ident[:])
-            half = slice(1024 * pair, 1024 * (pair + 1))
-            nc.scalar.copy(
-                out=f_grp[h][:, half].bitcast(F32).rearrange("p (i r u) -> p i r u", i=2, u=2),
-                in_=turned[:].rearrange("p (i u r) -> p i r u", i=2, u=2),
-            )
+        def f_turn(h):
+            for pair in range(2):
+                turned = take_bank(("t", h, pair))
+                for i in range(2):
+                    words = f_sb[h][:, 2 * pair + i, :].bitcast(F32)
+                    for u in range(2):
+                        lo = P * (2 * i + u)
+                        nc.tensor.transpose(turned[:, lo : lo + P], words[:, P * u : P * (u + 1)], ident[:])
 
-        def f_quantize(h, lo, hi):
+        def f_group(h):
+            f_grp[h] = work.tile([P, SLOTS * N], BF16, name="f_grp", bufs=8, align_bytes=64)
+            for pair in range(2):
+                grouped = f_grp[h][:, 2 * N * pair : 2 * N * (pair + 1)].bitcast(F32)
+                nc.scalar.copy(
+                    out=grouped.rearrange("p (i r u) -> p i r u", i=2, u=2),
+                    in_=read_bank(("t", h, pair))[:].rearrange("p (i u r) -> p i r u", i=2, u=2),
+                )
+
+        def f_quantize(h, lo=0, hi=SLOTS):
             nc.vector.quantize_mx(
                 out=f_codes[h][:, P * lo : P * hi].bitcast(E4M3X4),
                 scales=f_planes[h][:, P * lo : P * hi],
-                in_=f_grp[h][:, 4 * P * lo : 4 * P * hi],
+                in_=f_grp[h][:, N * lo : N * hi],
             )
 
-        o_bank = {}
+        def o_passes(slots, chunks):
+            for n in slots:
+                g, t = divmod(n, SLOTS)
+                for chunk in chunks:
+                    if chunk == 0:
+                        take_bank(("o", n))
+                    h = GROUPS * chunk + g
+                    nc.tensor.matmul_mx(
+                        out=held[("o", n)][1][:],
+                        lhsT=f_codes[h][:, P * t : P * (t + 1)].bitcast(E4M3X4),
+                        lhsT_scale=f_planes[h][:, P * t : P * (t + 1)],
+                        rhs=wb_sb[:, chunk, :].bitcast(E2M1X4),
+                        rhs_scale=wb_pl[:, chunk, :],
+                        start=(chunk == 0),
+                        stop=(chunk == CHUNKS - 1),
+                    )
 
-        def o_pass(n, ch, tag):
-            if ch == 0:
-                o_new = psum.tile([P, N], F32, name="o", tag=tag)
-                o_bank[n] = o_new
-            g, t = divmod(n, 4)
-            h = 2 * ch + g
-            nc.tensor.matmul_mx(
-                out=o_bank[n][:],
-                lhsT=f_codes[h][:, P * t : P * (t + 1)].bitcast(E4M3X4),
-                lhsT_scale=f_planes[h][:, P * t : P * (t + 1)],
-                rhs=wb_sb[:, ch, :].bitcast(E2M1X4),
-                rhs_scale=wb_pl[:, ch, :],
-                start=(ch == 0),
-                stop=(ch == CHUNKS - 1),
-            )
+        def o_store(n):
+            g, t = divmod(n, SLOTS)
+            o_sb = work.tile([P, H], F32, name="o_sb", bufs=8)
+            nc.vector.tensor_tensor(out=o_sb[:], in0=read_bank(("o", n))[:], in1=rate_sb[:], op=ALU.mult)
+            nc.sync.dma_start(out=out_view[g][:, t, :], in_=o_sb[:])
 
-        def o_store_last(n):
-            g, t = divmod(n, 4)
+        def o_store_in_halves(n):
+            g, t = divmod(n, SLOTS)
+            bank = read_bank(("o", n))
             for k in range(2):
                 cols = slice(H // 2 * k, H // 2 * (k + 1))
                 o_half = work.tile([P, H // 2], F32, name="o_half", bufs=2)
-                nc.vector.tensor_tensor(out=o_half[:], in0=o_bank[n][:, cols], in1=rate_sb[:, cols], op=ALU.mult)
+                nc.vector.tensor_tensor(out=o_half[:], in0=bank[:, cols], in1=rate_sb[:, cols], op=ALU.mult)
                 nc.sync.dma_start(out=out_view[g][:, t, cols], in_=o_half[:])
 
-        def o_store(n):
-            g, t = divmod(n, 4)
-            o_sb = work.tile([P, H], F32, name="o_sb", bufs=8)
-            nc.vector.tensor_tensor(out=o_sb[:], in0=o_bank[n][:], in1=rate_sb[:], op=ALU.mult)
-            nc.sync.dma_start(out=out_view[g][:, t, :], in_=o_sb[:])
-
-        def e_tile(s, t):
-            e_matmul(s, t)
-            e_subtract(s, t)
-
-        def f_tile(h, t):
-            g_matmul(h, t)
-            f_add(h, t)
-
-        def o_passes(tiles, chunks):
-            for n in tiles:
-                for ch in chunks:
-                    o_pass(n, ch, "bank%d" % (4 + (n + 1) % 4))
-
-        turn_c(0, 1, "bank7")
-        turn_c(1, 1, "bank5")
-        turn_c(2, 2, "bank6")
+        turn_c(0, 1)
+        turn_c(1, 1)
+        turn_c(2, 2)
         quantize_c(0, 1)
         quantize_c(1, 1)
-        permute_pt(0)
-        permute_pt(1)
-        e_matmul(0, 0)
-        e_matmul(0, 1)
-        turn_c(4, 2, "bank7")
+        sort_pt(0)
+        sort_pt(1)
+        r_matmul(0, 0)
+        r_matmul(0, 1)
+        turn_c(4, 2)
         quantize_c(2, 2)
         e_subtract(0, 0)
         e_subtract(0, 1)
-        e_matmul(0, 2)
-        turn_c(6, 2, "bank5")
-        e_matmul(0, 3)
+        r_matmul(0, 2)
+        turn_c(6, 2)
+        r_matmul(0, 3)
         quantize_c(4, 2)
         e_subtract(0, 2)
-        permute_pt_scales(0)
+        sort_pt_scales(0)
         e_subtract(0, 3)
         quantize_c(6, 2)
-        e_group_shared(0, 256)
-        for t in range(4):
-            e_tile(1, t)
-        e_group_scalar(1, 320)
-        for t in range(4):
-            e_matmul(2, t)
-        e_subtract_aside(2, 0)
+        e_group(0, SCALAR_SHARE_PART0)
+        for t in range(SLOTS):
+            r_matmul(1, t)
+            e_subtract(1, t)
+        e_group_scalar(1, SCALAR_SHARE_PART1)
+
+        for t in range(SLOTS):
+            r_matmul(2, t)
+        r_copy(2)
         e_quantize(0)
-        for t in range(4):
+        for t in range(SLOTS):
             g_pass(0, t, 0)
-        permute_pt_scales(1)
-        e_group_vector(1, 320)
+        sort_pt_scales(1)
+        e_group_vector(1, SCALAR_SHARE_PART1)
         e_subtract(2, 1)
         e_quantize(1)
-        e_subtract_pool(2, 0)
-        e_matmul(3, 0)
-        e_subtract_aside(3, 0)
-        for t in range(4):
+        e_subtract_gpsimd(2)
+        r_matmul(3, 0)
+        r_copy(3)
+        for t in range(SLOTS):
             g_pass(0, t, 1)
         e_subtract(2, 2)
         e_subtract(2, 3)
-        e_group_shared(2, SPLIT)
-        e_subtract_pool(3, 0)
-        for t in range(4):
+        e_group(2, SCALAR_SHARE)
+        e_subtract_gpsimd(3)
+        for t in range(SLOTS):
             f_add(0, t)
 
-        for s in range(3, HALVES):
-            h = s - 2
-            e_matmul(s, 1)
-            if s + 1 < HALVES:
-                e_matmul(s + 1, 0)
-                e_subtract_aside(s + 1, 0)
-            e_matmul(s, 2)
-            if h == 1:
-                for t in range(EARLY):
-                    g_matmul(h, t)
-            e_matmul(s, 3)
-            if h >= 3:
-                o_passes(range(2) if h % 2 == 1 else [2], [(h - 1) // 2 - 1])
-            e_subtract(s, 1)
-            f_turn(h - 1, 0)
-            f_turn(h - 1, 1)
-            if s % 2 == 0:
+        for s in range(LAG + 1, PARTS):
+            h = s - LAG
+            even = s % 2 == 0
+            more = s + 1 < PARTS
+            if not even:
+                r_matmul(s, 1)
+            if more:
+                r_matmul(s + 1, 0)
+                r_copy(s + 1)
+            r_matmul(s, 2)
+            r_matmul(s, 3)
+            ahead = whole = 0
+            if even:
+                ahead = 3 if s == 4 else 2
+                for t in range(ahead):
+                    g_pass(h, t, 0)
+                if s == 6 and False:
+                    f_turn(h - 2)
+                    f_group(h - 2)
+                f_turn(h - 1)
+                f_group(h - 1)
                 e_quantize(s - 1)
-            e_subtract(s, 2)
-            if s % 2 == 1:
+                e_subtract(s, 2)
+            else:
+                if s != 5 or not False:
+                    whole = 2 if s == 3 else 0
+                    for t in range(whole):
+                        g_matmul(h, t)
+                    f_turn(h - 1)
+                    f_group(h - 1)
+                e_subtract(s, 1)
+                e_subtract(s, 2)
                 e_quantize(s - 1)
             e_subtract(s, 3)
-            e_group_shared(s, SPLIT)
-            if h % 2 == 0:
-                f_quantize(h - 2, 0, 4)
-            if s + 1 < HALVES:
-                e_subtract_pool(s + 1, 0)
-            for t in range(4):
-                if h > 1 or t >= EARLY:
-                    g_matmul(h, t)
+            e_group(s, SCALAR_SHARE)
+            if more:
+                e_subtract_gpsimd(s + 1)
+            else:
+                f_quantize(0)
+            for t in range(whole, SLOTS):
+                if t >= ahead:
+                    g_pass(h, t, 0)
+                g_pass(h, t, 1)
+            for t in range(SLOTS):
+                if t == SLOTS - 1 and more and not even:
+                    r_matmul(s + 1, 1)
+                    e_subtract(s + 1, 1)
                 f_add(h, t)
-        ring["size"] = 4
-        o_passes([2], [1])
-        g_pass(6, 0, 0)
-        o_passes([3], [0, 1])
-        f_quantize(4, 0, 4)
-        e_quantize(7)
-        f_quantize(1, 0, 4)
-        f_quantize(3, 0, 4)
-        f_turn(5, 0)
-        f_turn(5, 1)
-        o_passes(range(2), [2])
-        g_pass(6, 0, 1)
-        g_matmul(6, 1)
-        o_passes(range(2, 4), [2])
-        f_add(6, 0)
-        g_matmul(6, 2)
-        f_add(6, 1)
-        f_quantize(5, 0, 4)
-        g_matmul(6, 3)
-        f_add(6, 2)
-        f_add(6, 3)
-        g_matmul(7, 0)
-        g_matmul(7, 1)
-        f_turn(6, 0)
-        f_turn(6, 1)
-        f_add(7, 0)
-        f_add(7, 1)
-        g_matmul(7, 2)
-        g_matmul(7, 3)
-        f_quantize(6, 0, 2)
-        f_add(7, 2)
-        f_quantize(6, 2, 4)
-        o_passes(range(4), [3])
-        f_add(7, 3)
+                if t == 1 and not more:
+                    f_quantize(2)
+
+        last_a, last_b = PARTS - 2, PARTS - 1
+        o_passes(range(SLOTS), [0])
+        for pair in ([0, 1], [2, 3]):
+            for t in pair:
+                g_pass(last_a, t, 0)
+            o_passes(pair, [1])
+        e_quantize(last_b)
+        f_quantize(4)
+        f_quantize(1)
+        for t in range(SLOTS):
+            g_pass(last_a, t, 1)
+        o_passes(range(SLOTS), [2])
+        for t in range(SLOTS):
+            f_add(last_a, t)
+        f_quantize(3)
+        f_turn(5)
+        f_turn(last_a)
+        f_group(5)
+        f_group(last_a)
+        for t in range(SLOTS):
+            g_matmul(last_b, t)
+        f_quantize(5)
+        f_add(last_b, 0)
+        f_quantize(last_a)
+        for t in range(1, SLOTS):
+            f_add(last_b, t)
+        o_passes(range(SLOTS), [CHUNKS - 1])
+        f_turn(last_b)
+        f_group(last_b)
         o_store(0)
-        f_turn(7, 0)
-        f_turn(7, 1)
         o_store(1)
-        o_passes([4], range(3))
+        o_passes([4], range(CHUNKS - 1))
         o_store(2)
-        f_quantize(7, 0, 2)
-        o_passes([5], range(4))
-        o_passes([4], [3])
+        f_quantize(last_b, 0, 2)
+        o_passes([5], range(CHUNKS))
+        o_passes([4], [CHUNKS - 1])
         o_store(3)
-        f_quantize(7, 2, 4)
-        o_passes([6, 7], range(4))
+        f_quantize(last_b, 2, 4)
+        o_passes([6, 7], range(CHUNKS))
         for n in (5, 4, 6):
             o_store(n)
-        o_store_last(7)
+        o_store_in_halves(7)

@@ -203,18 +203,18 @@ def tile_tied_autoencoder_code_step_t2_kernel(
 
         def e_subtract(s, t):
             nc.vector.tensor_tensor(
-                out=as_stored(e_slot(s, t)),
-                in0=into_stored(x_slot(s, t)),
-                in1=into_stored(read_bank(("r", s, t))[:]),
+                out=e_slot(s, t).rearrange("p (u m e) -> p m u e", u=2, e=2),
+                in0=x_slot(s, t).rearrange("p (m u e) -> p m u e", u=2, e=2),
+                in1=read_bank(("r", s, t))[:].rearrange("p (m u e) -> p m u e", u=2, e=2),
                 op=ALU.subtract,
             )
 
-        def r_copy(s):
-            nc.scalar.copy(out=as_stored(e_slot(s, 0)), in_=into_stored(read_bank(("r", s, 0))[:]))
+        def r_copy(s, t=0):
+            nc.scalar.copy(out=as_stored(e_slot(s, t)), in_=into_stored(read_bank(("r", s, t))[:]))
 
-        def e_subtract_gpsimd(s):
-            dst = as_stored(e_slot(s, 0))
-            nc.gpsimd.tensor_tensor(out=dst, in0=into_stored(x_slot(s, 0)), in1=dst, op=ALU.subtract)
+        def e_subtract_gpsimd(s, t=0):
+            dst = as_stored(e_slot(s, t))
+            nc.gpsimd.tensor_tensor(out=dst, in0=into_stored(x_slot(s, t)), in1=dst, op=ALU.subtract)
 
         def e_group_scalar(s, share):
             e_grp[s] = work.tile([P, N, SLOTS], BF16, name="e_grp", bufs=2, align_bytes=64)
@@ -386,39 +386,42 @@ def tile_tied_autoencoder_code_step_t2_kernel(
             h = s - LAG
             even = s % 2 == 0
             more = s + 1 < PARTS
-            if not even:
+            two = s + 1 in (5, 7)
+            if not even and s not in (5, 7):
                 r_matmul(s, 1)
             if more:
-                r_matmul(s + 1, 0)
-                r_copy(s + 1)
+                r_matmul(s + 1, 1 if two else 0)
+                r_copy(s + 1, 1 if two else 0)
             r_matmul(s, 2)
             r_matmul(s, 3)
+            if two:
+                r_matmul(s + 1, 0)
+                r_copy(s + 1, 0)
             ahead = whole = 0
             if even:
                 ahead = 3 if s == 4 else 2
                 for t in range(ahead):
                     g_pass(h, t, 0)
-                if s == 6 and False:
-                    f_turn(h - 2)
-                    f_group(h - 2)
                 f_turn(h - 1)
                 f_group(h - 1)
                 e_quantize(s - 1)
+                if two:
+                    e_subtract_gpsimd(s + 1, 0)
                 e_subtract(s, 2)
             else:
-                if s != 5 or not False:
-                    whole = 2 if s == 3 else 0
-                    for t in range(whole):
-                        g_matmul(h, t)
-                    f_turn(h - 1)
-                    f_group(h - 1)
-                e_subtract(s, 1)
+                whole = 2 if s == 3 else 0
+                for t in range(whole):
+                    g_matmul(h, t)
+                f_turn(h - 1)
+                f_group(h - 1)
+                if s not in (5, 7):
+                    e_subtract(s, 1)
                 e_subtract(s, 2)
                 e_quantize(s - 1)
             e_subtract(s, 3)
             e_group(s, SCALAR_SHARE)
             if more:
-                e_subtract_gpsimd(s + 1)
+                e_subtract_gpsimd(s + 1, 1 if two else 0)
             else:
                 f_quantize(0)
             for t in range(whole, SLOTS):

@@ -22,13 +22,8 @@ SLOTS = 4
 GROUPS = M // (P * SLOTS)
 CHUNKS = D // N
 PARTS = GROUPS * CHUNKS
-LAG = 2
 
 MOVING_CODES, MOVING_SCALES, STILL_CODES, STILL_SCALES = 0, 64, 128, 192
-
-SCALAR_SHARE = 384
-SCALAR_SHARE_PART0 = 256
-SCALAR_SHARE_PART1 = 320
 
 
 def tile_tied_autoencoder_code_step_t2_kernel(
@@ -51,15 +46,15 @@ def tile_tied_autoencoder_code_step_t2_kernel(
         c_grp = keep.tile([P, 4 * M], BF16, name="c_grp", align_bytes=64)
         c_codes = placed(keep, "c_codes", M, U32, 4, STILL_CODES)
         c_planes = placed(keep, "c_planes", M, U8, 1, STILL_SCALES)
-        x_first = [keep.tile([P, 2, N], BF16, name="x_sb0_%d" % j) for j in range(2)]
-        x_rest = {s: keep.tile([P, SLOTS, N], BF16, name="x_sb%d" % s) for s in range(1, PARTS)}
+        x_half = {(s, j): keep.tile([P, 2, N], BF16, name="x_sb%d_%d" % (s, j)) for s in range(2) for j in range(2)}
+        x_rest = {s: keep.tile([P, SLOTS, N], BF16, name="x_sb%d" % s) for s in range(2, PARTS)}
         wd_sb = placed(keep, "wd_sb", 2 * D, U8, 1, MOVING_CODES)
         wd_pl_first = placed(keep, "wd_pl_first", N, U8, 1, MOVING_SCALES)
         wd_pl_rest = placed(keep, "wd_pl_rest", D - N, U8, 1, MOVING_SCALES)
-        pt_raw = keep.tile([P, GROUPS, 2 * M], U8, name="pt_raw", align_bytes=64)
-        pt_sb = placed(keep, "pt_sb", 4 * M, U8, 1, STILL_CODES).rearrange("p (g w) -> p g w", g=GROUPS)
-        pt_plraw = keep.tile([P, GROUPS, M], U8, name="pt_plraw", align_bytes=64)
-        pt_pl = placed(keep, "pt_pl", 2 * M, U8, 1, STILL_SCALES).rearrange("p (g w) -> p g w", g=GROUPS)
+        pt_raw = [keep.tile([P, GROUPS, 2 * N], U8, name="pt_raw%d" % j, align_bytes=64) for j in range(GROUPS)]
+        pt_sb = {(k, j): placed(keep, "pt_sb%d_%d" % (k, j), 2 * N, U8, 1, STILL_CODES) for k in range(2) for j in range(2)}
+        pt_plraw = [keep.tile([P, GROUPS, N], U8, name="pt_plraw%d" % j, align_bytes=64) for j in range(GROUPS)]
+        pt_pl = {(k, j): placed(keep, "pt_pl%d_%d" % (k, j), N, U8, 1, STILL_SCALES) for k in range(2) for j in range(2)}
         wb_sb = placed(keep, "wb_sb", CHUNKS * 2 * H, U8, 1, MOVING_CODES).rearrange("p (g w) -> p g w", g=CHUNKS)
         wb_pl = placed(keep, "wb_pl", CHUNKS * H, U8, 1, MOVING_SCALES).rearrange("p (g w) -> p g w", g=CHUNKS)
         a_sb = keep.tile([P, GROUPS, SLOTS], BF16, name="a_sb")
@@ -74,15 +69,15 @@ def tile_tied_autoencoder_code_step_t2_kernel(
         def load_c(k):
             nc.sync.dma_start(out=c_raw[k][:], in_=c_view[k // 2][:, 2 * (k % 2) : 2 * (k % 2) + 2, :])
 
-        def load_x_first(j):
-            nc.sync.dma_start(out=x_first[j][:], in_=x_view[0][:, 2 * j : 2 * j + 2, 0:N])
+        def load_x_half(s, j):
+            nc.sync.dma_start(out=x_half[s, j][:], in_=x_view[s][:, 2 * j : 2 * j + 2, 0:N])
 
         def load_x(s):
             chunk, g = divmod(s, GROUPS)
             nc.sync.dma_start(out=x_rest[s][:], in_=x_view[g][:, :, N * chunk : N * (chunk + 1)])
 
         def x_slot(s, t):
-            return x_first[t // 2][:, t % 2, :] if s == 0 else x_rest[s][:, t, :]
+            return x_half[s, t // 2][:, t % 2, :] if s < 2 else x_rest[s][:, t, :]
 
         def load_wd(lo, hi):
             nc.sync.dma_start(
@@ -100,32 +95,47 @@ def tile_tied_autoencoder_code_step_t2_kernel(
                     in_=rows[:, r:16:4, :].rearrange("g q n -> q g n").bitcast(I32),
                 )
 
+        def load_pt(j):
+            cols = pt_words[:, :, 2 * N * j : 2 * N * (j + 1)]
+            nc.sync.dma_start(out=pt_raw[j][:].bitcast(I32), in_=cols.rearrange("g p w -> p g w").bitcast(I32))
+
+        def load_pt_scales(j):
+            load_scales(pt_plraw[j], pt_scales[:, :, N * j : N * (j + 1)])
+
+        nc.vector.memset(pt_plraw[0][:].rearrange("p g n -> p (g n)").bitcast(I32), 0)
         nc.vector.memset(wd_pl_first[:].bitcast(I32), 0)
-        nc.vector.memset(pt_plraw[:].rearrange("p g n -> p (g n)").bitcast(I32), 0)
         nc.vector.memset(wd_pl_rest[:].bitcast(I32), 0)
+        nc.vector.memset(pt_plraw[1][:].rearrange("p g n -> p (g n)").bitcast(I32), 0)
         nc.vector.memset(wb_pl[:].rearrange("p g n -> p (g n)").bitcast(I32), 0)
         make_identity(nc, ident[:])
 
         load_c(0)
         load_c(1)
-        load_wd(0, N)
+        load_pt_scales(0)
+        load_c(2)
+        load_c(3)
+        load_wd(0 * N, 1 * N)
         load_wd_scales(wd_pl_first, 0, N)
-        nc.sync.dma_start(out=pt_raw[:].bitcast(I32), in_=pt_words.rearrange("g p w -> p g w").bitcast(I32))
-        for j in range(2):
-            load_c(2 + j)
-            load_x_first(j)
-        load_scales(pt_plraw, pt_scales)
-        load_x(1)
-        load_wd(N, D)
+        load_pt(0)
+        load_x_half(0, 0)
+        load_x_half(0, 1)
+        load_x_half(1, 0)
+        load_wd(1 * N, 4 * N)
         load_wd_scales(wd_pl_rest, N, D)
+        load_x_half(1, 1)
+        load_pt(1)
+        load_pt_scales(1)
         load_x(2)
-        nc.sync.dma_start(out=a_sb[:], in_=a.rearrange("(g p t) -> p g t", p=P, t=SLOTS))
         load_x(3)
+        nc.sync.dma_start(out=a_sb[:], in_=a.rearrange("(g p t) -> p g t", p=P, t=SLOTS))
+        load_x(4)
+        load_x(5)
+        load_x(6)
+        load_x(7)
         load_scales(wb_pl, wb_scales)
         nc.sync.dma_start(out=wb_sb[:].bitcast(I32), in_=wb_words.rearrange("g p w -> p g w").bitcast(I32))
-        for s in range(4, PARTS):
-            load_x(s)
         nc.sync.dma_start(out=rate_sb[:], in_=rate.partition_broadcast(P))
+
 
         free = list(range(8))
         held = {}
@@ -141,12 +151,23 @@ def tile_tied_autoencoder_code_step_t2_kernel(
             free.append(k)
             return bank
 
+        c_sorted = {}
+
+        def sort_c(k):
+            c_sorted[k] = keep.tile([P, 2, 2, P], F32, name="c_sorted%d" % k)
+            nc.vector.tensor_copy(
+                out=c_sorted[k][:], in_=c_raw[k][:].bitcast(F32).rearrange("p j (m u) -> p j u m", u=2)
+            )
+
         def turn_c(first, count):
             turned = take_bank("c")
             for i in range(count):
                 k, j = divmod(first + i, 2)
                 for u in range(2):
-                    words = c_raw[k][:, j, :].bitcast(F32)[:, u : 2 * P : 2]
+                    if k in c_sorted:
+                        words = c_sorted[k][:, j, u, :]
+                    else:
+                        words = c_raw[k][:, j, :].bitcast(F32)[:, u : 2 * P : 2]
                     lo = P * (2 * i + u)
                     nc.tensor.transpose(turned[:, lo : lo + P], words, ident[:])
             grouped = c_grp[:, N * first : N * (first + count)].bitcast(F32)
@@ -163,16 +184,16 @@ def tile_tied_autoencoder_code_step_t2_kernel(
                 in_=c_grp[:, N * first : N * (first + count)],
             )
 
-        def sort_pt(k):
+        def sort_pt(k, j):
             nc.vector.tensor_copy(
-                out=pt_sb[:, k, :].bitcast(U16).rearrange("p (j t m) -> p j t m", j=GROUPS, t=SLOTS),
-                in_=pt_raw[:, k, :].bitcast(U16).rearrange("p (j m t) -> p j t m", j=GROUPS, t=SLOTS),
+                out=pt_sb[k, j][:].bitcast(U16).rearrange("p (t m) -> p t m", t=SLOTS),
+                in_=pt_raw[j][:, k, :].bitcast(U16).rearrange("p (m t) -> p t m", t=SLOTS),
             )
 
-        def sort_pt_scales(k):
+        def sort_pt_scales(k, j):
             nc.vector.tensor_copy(
-                out=pt_pl[:, k, :].rearrange("p (j t m) -> p j t m", j=GROUPS, t=SLOTS),
-                in_=pt_plraw[:, k, :].rearrange("p (j m t) -> p j t m", j=GROUPS, t=SLOTS),
+                out=pt_pl[k, j][:].rearrange("p (t m) -> p t m", t=SLOTS),
+                in_=pt_plraw[j][:, k, :].rearrange("p (m t) -> p t m", t=SLOTS),
             )
 
         e32, e_grp, e_codes, e_planes = {}, {}, {}, {}
@@ -209,25 +230,31 @@ def tile_tied_autoencoder_code_step_t2_kernel(
                 op=ALU.subtract,
             )
 
-        def r_copy(s, t=0):
+        def r_copy(s, t):
             nc.scalar.copy(out=as_stored(e_slot(s, t)), in_=into_stored(read_bank(("r", s, t))[:]))
 
-        def e_subtract_gpsimd(s, t=0):
+        def e_subtract_gpsimd(s, t):
             dst = as_stored(e_slot(s, t))
             nc.gpsimd.tensor_tensor(out=dst, in0=into_stored(x_slot(s, t)), in1=dst, op=ALU.subtract)
 
-        def e_group_scalar(s, share):
-            e_grp[s] = work.tile([P, N, SLOTS], BF16, name="e_grp", bufs=2, align_bytes=64)
-            nc.scalar.copy(out=e_grp[s][:, :share, :], in_=e32[s][:, :, :share].rearrange("p t n -> p n t"))
+        def grouped_e(s, lo, hi):
+            if s not in e_grp:
+                e_grp[s] = work.tile([P, N, SLOTS], BF16, name="e_grp", bufs=2, align_bytes=64)
+            return e_grp[s][:, lo:hi, :]
 
-        def e_group_vector(s, share):
-            nc.vector.tensor_copy(out=e_grp[s][:, share:, :], in_=e32[s][:, :, share:].rearrange("p t n -> p n t"))
+        def e_group_scalar(s, hi=N):
+            nc.scalar.copy(
+                out=grouped_e(s, 0, hi).rearrange("p (c i) (w e) -> p c w i e", i=2, e=2),
+                in_=e32[s][:, :, :hi].rearrange("p (w e) (c i) -> p c w i e", i=2, e=2),
+            )
 
-        def e_group(s, share):
-            e_group_scalar(s, share)
+        def e_group_vector(s, lo):
+            nc.vector.tensor_copy(out=grouped_e(s, lo, N), in_=e32[s][:, :, lo:].rearrange("p t n -> p n t"))
+
+        def e_group_gpsimd(s, lo):
             nc.gpsimd.tensor_scalar(
-                out=e_grp[s][:, share:, :],
-                in0=e32[s][:, :, share:].rearrange("p t n -> p n t"),
+                out=grouped_e(s, lo, N),
+                in0=e32[s][:, :, lo:].rearrange("p t n -> p n t"),
                 scalar1=1.0,
                 scalar2=0.0,
                 op0=ALU.mult,
@@ -249,11 +276,10 @@ def tile_tied_autoencoder_code_step_t2_kernel(
             chunk, g = divmod(h, GROUPS)
             if k == 0:
                 take_bank(("g", h, t))
-            n = SLOTS * g + t
             nc.tensor.matmul_mx(
                 out=held[("g", h, t)][1][:],
-                lhsT=pt_sb[:, k, 2 * P * n : 2 * P * (n + 1)].bitcast(E2M1X4),
-                lhsT_scale=pt_pl[:, k, P * n : P * (n + 1)],
+                lhsT=pt_sb[k, g][:, 2 * P * t : 2 * P * (t + 1)].bitcast(E2M1X4),
+                lhsT_scale=pt_pl[k, g][:, P * t : P * (t + 1)],
                 rhs=e_codes[GROUPS * chunk + k][:].bitcast(E4M3X4),
                 rhs_scale=e_planes[GROUPS * chunk + k][:],
                 start=(k == 0),
@@ -265,8 +291,8 @@ def tile_tied_autoencoder_code_step_t2_kernel(
                 g_pass(h, t, k)
 
         def f_add(h, t):
-            if t == 0:
-                f_sb[h] = work.tile([P, SLOTS, N], BF16, name="f_sb", bufs=3)
+            if h not in f_sb:
+                f_sb[h] = work.tile([P, SLOTS, N], BF16, name="f_sb", bufs=4)
             nc.vector.scalar_tensor_tensor(
                 out=f_sb[h][:, t, :],
                 in0=e32[h][:, t, :],
@@ -276,23 +302,22 @@ def tile_tied_autoencoder_code_step_t2_kernel(
                 op1=ALU.add,
             )
 
-        def f_turn(h):
-            for pair in range(2):
-                turned = take_bank(("t", h, pair))
-                for i in range(2):
-                    words = f_sb[h][:, 2 * pair + i, :].bitcast(F32)
-                    for u in range(2):
-                        lo = P * (2 * i + u)
-                        nc.tensor.transpose(turned[:, lo : lo + P], words[:, P * u : P * (u + 1)], ident[:])
+        def f_turn(h, pair):
+            turned = take_bank(("t", h, pair))
+            for i in range(2):
+                words = f_sb[h][:, 2 * pair + i, :].bitcast(F32)
+                for u in range(2):
+                    lo = P * (2 * i + u)
+                    nc.tensor.transpose(turned[:, lo : lo + P], words[:, P * u : P * (u + 1)], ident[:])
 
-        def f_group(h):
-            f_grp[h] = work.tile([P, SLOTS * N], BF16, name="f_grp", bufs=8, align_bytes=64)
-            for pair in range(2):
-                grouped = f_grp[h][:, 2 * N * pair : 2 * N * (pair + 1)].bitcast(F32)
-                nc.scalar.copy(
-                    out=grouped.rearrange("p (i r u) -> p i r u", i=2, u=2),
-                    in_=read_bank(("t", h, pair))[:].rearrange("p (i u r) -> p i r u", i=2, u=2),
-                )
+        def f_group(h, pair):
+            if h not in f_grp:
+                f_grp[h] = work.tile([P, SLOTS * N], BF16, name="f_grp", bufs=6, align_bytes=64)
+            grouped = f_grp[h][:, 2 * N * pair : 2 * N * (pair + 1)].bitcast(F32)
+            nc.scalar.copy(
+                out=grouped.rearrange("p (i r u) -> p i r u", i=2, u=2),
+                in_=read_bank(("t", h, pair))[:].rearrange("p (i u r) -> p i r u", i=2, u=2),
+            )
 
         def f_quantize(h, lo=0, hi=SLOTS):
             nc.vector.quantize_mx(
@@ -320,7 +345,7 @@ def tile_tied_autoencoder_code_step_t2_kernel(
 
         def o_store(n):
             g, t = divmod(n, SLOTS)
-            o_sb = work.tile([P, H], F32, name="o_sb", bufs=8)
+            o_sb = work.tile([P, H], F32, name="o_sb", bufs=5)
             nc.vector.tensor_tensor(out=o_sb[:], in0=read_bank(("o", n))[:], in1=rate_sb[:], op=ALU.mult)
             nc.sync.dma_start(out=out_view[g][:, t, :], in_=o_sb[:])
 
@@ -336,145 +361,292 @@ def tile_tied_autoencoder_code_step_t2_kernel(
         turn_c(0, 1)
         turn_c(1, 1)
         turn_c(2, 2)
+        sort_pt_scales(0, 0)
         quantize_c(0, 1)
+        sort_c(2)
         quantize_c(1, 1)
-        sort_pt(0)
-        sort_pt(1)
+        sort_c(3)
+        turn_c(4, 2)
+        turn_c(6, 2)
+        quantize_c(2, 2)
+        sort_pt_scales(1, 0)
+        sort_pt(0, 0)
+        quantize_c(4, 2)
+        sort_pt(1, 0)
         r_matmul(0, 0)
         r_matmul(0, 1)
-        turn_c(4, 2)
-        quantize_c(2, 2)
-        e_subtract(0, 0)
-        e_subtract(0, 1)
         r_matmul(0, 2)
-        turn_c(6, 2)
         r_matmul(0, 3)
-        quantize_c(4, 2)
-        e_subtract(0, 2)
-        sort_pt_scales(0)
-        e_subtract(0, 3)
         quantize_c(6, 2)
-        e_group(0, SCALAR_SHARE_PART0)
-        for t in range(SLOTS):
-            r_matmul(1, t)
-            e_subtract(1, t)
-        e_group_scalar(1, SCALAR_SHARE_PART1)
-
-        for t in range(SLOTS):
-            r_matmul(2, t)
-        r_copy(2)
-        e_quantize(0)
-        for t in range(SLOTS):
-            g_pass(0, t, 0)
-        sort_pt_scales(1)
-        e_group_vector(1, SCALAR_SHARE_PART1)
-        e_subtract(2, 1)
-        e_quantize(1)
-        e_subtract_gpsimd(2)
+        r_matmul(1, 0)
+        r_matmul(1, 1)
+        r_matmul(1, 2)
+        r_matmul(1, 3)
+        r_copy(0, 0)
+        e_subtract(0, 1)
+        e_subtract_gpsimd(0, 0)
+        e_subtract(0, 2)
+        e_subtract(0, 3)
+        e_group_scalar(0, 256)
+        e_group_gpsimd(0, 256)
+        e_subtract(1, 0)
+        e_subtract(1, 1)
+        e_subtract(1, 2)
+        e_subtract(1, 3)
         r_matmul(3, 0)
-        r_copy(3)
-        for t in range(SLOTS):
-            g_pass(0, t, 1)
+        r_matmul(4, 0)
+        r_matmul(2, 0)
+        r_matmul(2, 1)
+        r_copy(3, 0)
+        r_copy(4, 0)
+        r_matmul(2, 2)
+        r_matmul(2, 3)
+        r_matmul(4, 1)
+        e_quantize(0)
+        e_group_scalar(1, 384)
+        g_pass(0, 0, 0)
+        g_pass(0, 1, 0)
+        g_pass(0, 2, 0)
+        sort_pt(0, 1)
+        sort_pt(1, 1)
+        e_group_vector(1, 384)
+        r_copy(4, 1)
+        r_matmul(5, 0)
+        r_copy(2, 0)
+        sort_pt_scales(0, 1)
+        sort_pt_scales(1, 1)
+        r_copy(5, 0)
+        e_quantize(1)
+        e_subtract_gpsimd(2, 0)
+        g_pass(0, 0, 1)
+        g_pass(0, 1, 1)
+        g_pass(0, 2, 1)
+        r_matmul(3, 1)
+        e_subtract(2, 1)
+        r_matmul(3, 2)
         e_subtract(2, 2)
+        r_matmul(3, 3)
         e_subtract(2, 3)
-        e_group(2, SCALAR_SHARE)
-        e_subtract_gpsimd(3)
-        for t in range(SLOTS):
-            f_add(0, t)
-
-        for s in range(LAG + 1, PARTS):
-            h = s - LAG
-            even = s % 2 == 0
-            more = s + 1 < PARTS
-            two = s + 1 in (5, 7)
-            if not even and s not in (5, 7):
-                r_matmul(s, 1)
-            if more:
-                r_matmul(s + 1, 1 if two else 0)
-                r_copy(s + 1, 1 if two else 0)
-            r_matmul(s, 2)
-            r_matmul(s, 3)
-            if two:
-                r_matmul(s + 1, 0)
-                r_copy(s + 1, 0)
-            ahead = whole = 0
-            if even:
-                ahead = 3 if s == 4 else 2
-                for t in range(ahead):
-                    g_pass(h, t, 0)
-                f_turn(h - 1)
-                f_group(h - 1)
-                e_quantize(s - 1)
-                if two:
-                    e_subtract_gpsimd(s + 1, 0)
-                e_subtract(s, 2)
-            else:
-                whole = 2 if s == 3 else 0
-                for t in range(whole):
-                    g_matmul(h, t)
-                f_turn(h - 1)
-                f_group(h - 1)
-                if s not in (5, 7):
-                    e_subtract(s, 1)
-                e_subtract(s, 2)
-                e_quantize(s - 1)
-            e_subtract(s, 3)
-            e_group(s, SCALAR_SHARE)
-            if more:
-                e_subtract_gpsimd(s + 1, 1 if two else 0)
-            else:
-                f_quantize(0)
-            for t in range(whole, SLOTS):
-                if t >= ahead:
-                    g_pass(h, t, 0)
-                g_pass(h, t, 1)
-            for t in range(SLOTS):
-                if t == SLOTS - 1 and more and not even:
-                    r_matmul(s + 1, 1)
-                    e_subtract(s + 1, 1)
-                f_add(h, t)
-                if t == 1 and not more:
-                    f_quantize(2)
-
-        last_a, last_b = PARTS - 2, PARTS - 1
-        o_passes(range(SLOTS), [0])
-        for pair in ([0, 1], [2, 3]):
-            for t in pair:
-                g_pass(last_a, t, 0)
-            o_passes(pair, [1])
-        e_quantize(last_b)
+        e_subtract_gpsimd(3, 0)
+        g_pass(0, 3, 0)
+        g_pass(0, 3, 1)
+        e_subtract(3, 1)
+        e_group_scalar(2)
+        g_pass(1, 0, 0)
+        g_pass(1, 0, 1)
+        e_subtract(3, 2)
+        e_subtract(3, 3)
+        e_subtract_gpsimd(4, 0)
+        f_add(0, 0)
+        g_pass(1, 1, 0)
+        g_pass(1, 1, 1)
+        f_add(0, 1)
+        e_subtract_gpsimd(4, 1)
+        g_pass(1, 2, 0)
+        g_pass(1, 2, 1)
+        f_add(0, 2)
+        e_group_scalar(3)
+        g_pass(1, 3, 0)
+        g_pass(1, 3, 1)
+        f_add(0, 3)
+        r_matmul(5, 1)
+        r_matmul(6, 0)
+        f_add(1, 0)
+        f_turn(0, 0)
+        f_turn(0, 1)
+        f_add(1, 1)
+        r_matmul(4, 2)
+        r_matmul(4, 3)
+        e_quantize(2)
+        f_group(0, 0)
+        r_copy(5, 1)
+        g_pass(2, 0, 0)
+        e_quantize(3)
+        e_subtract_gpsimd(5, 1)
+        r_copy(6, 0)
+        f_group(0, 1)
+        f_add(1, 2)
+        g_pass(2, 0, 1)
+        r_matmul(6, 1)
+        f_add(1, 3)
+        g_pass(2, 1, 0)
+        g_pass(2, 1, 1)
+        e_subtract(4, 2)
+        e_subtract_gpsimd(5, 0)
+        r_copy(6, 1)
+        r_matmul(5, 2)
+        e_subtract(4, 3)
+        r_matmul(5, 3)
+        f_add(2, 0)
+        e_group_scalar(4)
+        g_pass(2, 2, 0)
+        g_pass(2, 2, 1)
+        e_subtract(5, 2)
+        e_subtract_gpsimd(6, 0)
+        g_pass(2, 3, 0)
+        g_pass(2, 3, 1)
+        f_add(2, 1)
+        g_pass(3, 0, 0)
+        g_pass(3, 0, 1)
+        e_subtract(5, 3)
+        e_subtract_gpsimd(6, 1)
+        g_pass(3, 1, 0)
+        g_pass(3, 1, 1)
+        f_add(2, 2)
+        e_group_scalar(5)
+        g_pass(3, 2, 0)
+        g_pass(3, 2, 1)
+        f_add(2, 3)
+        g_pass(3, 3, 0)
+        g_pass(3, 3, 1)
+        f_add(3, 0)
+        r_matmul(7, 0)
+        r_matmul(7, 1)
+        f_add(3, 1)
+        f_turn(1, 0)
+        f_turn(1, 1)
+        f_add(3, 2)
+        r_matmul(6, 2)
+        r_matmul(6, 3)
+        e_quantize(4)
+        f_group(1, 0)
+        r_copy(7, 0)
+        g_pass(4, 0, 0)
+        e_quantize(5)
+        e_subtract_gpsimd(7, 0)
+        r_copy(7, 1)
+        f_group(1, 1)
+        f_add(3, 3)
+        g_pass(4, 0, 1)
+        e_subtract_gpsimd(7, 1)
+        r_matmul(7, 2)
+        e_subtract(6, 2)
+        r_matmul(7, 3)
+        e_subtract(6, 3)
+        g_pass(4, 1, 0)
+        g_pass(4, 1, 1)
+        e_subtract(7, 2)
+        e_group_gpsimd(6, 384)
+        e_group_scalar(6, 384)
+        g_pass(4, 2, 0)
+        g_pass(4, 2, 1)
+        e_subtract(7, 3)
+        g_pass(4, 3, 0)
+        g_pass(4, 3, 1)
+        f_add(4, 0)
+        e_group_gpsimd(7, 256)
+        g_pass(5, 0, 0)
+        g_pass(5, 0, 1)
+        e_group_scalar(7, 256)
+        f_add(4, 1)
+        g_pass(5, 1, 0)
+        g_pass(5, 1, 1)
+        f_add(4, 2)
+        f_turn(2, 0)
+        f_turn(2, 1)
+        f_turn(3, 0)
+        f_add(4, 3)
+        g_pass(5, 2, 0)
+        g_pass(5, 2, 1)
+        e_quantize(6)
+        f_group(2, 0)
+        f_group(2, 1)
+        f_group(3, 0)
+        e_quantize(7)
+        g_pass(5, 3, 0)
+        g_pass(5, 3, 1)
+        f_turn(3, 1)
+        f_turn(4, 0)
+        f_turn(4, 1)
+        f_add(5, 0)
+        g_pass(6, 0, 0)
+        g_pass(6, 0, 1)
+        f_group(3, 1)
+        f_group(4, 0)
+        f_group(4, 1)
+        f_add(5, 1)
+        g_pass(6, 1, 0)
+        g_pass(6, 1, 1)
+        f_add(5, 2)
+        g_pass(6, 2, 0)
+        g_pass(6, 2, 1)
+        f_add(5, 3)
+        g_pass(6, 3, 0)
+        g_pass(6, 3, 1)
+        f_quantize(0)
+        f_add(6, 0)
+        g_pass(7, 0, 0)
+        g_pass(7, 0, 1)
+        f_add(6, 1)
+        g_pass(7, 1, 0)
+        g_pass(7, 1, 1)
+        f_quantize(2)
+        f_add(6, 2)
+        g_pass(7, 2, 0)
+        g_pass(7, 2, 1)
+        f_add(6, 3)
+        g_pass(7, 3, 0)
+        g_pass(7, 3, 1)
+        o_passes([0], [0])
+        o_passes([0], [1])
+        f_add(7, 0)
+        f_turn(5, 0)
+        f_turn(5, 1)
+        f_turn(6, 0)
+        f_turn(6, 1)
+        f_add(7, 1)
         f_quantize(4)
+        f_add(7, 2)
+        f_add(7, 3)
+        f_group(6, 0)
+        f_group(6, 1)
+        f_group(5, 0)
+        f_group(5, 1)
+        o_passes([1], [0])
+        o_passes([1], [1])
+        o_passes([0], [2])
+        o_passes([1], [2])
+        o_passes([2], [0])
+        o_passes([2], [1])
+        o_passes([2], [2])
+        o_passes([3], [0])
+        o_passes([3], [1])
+        o_passes([3], [2])
         f_quantize(1)
-        for t in range(SLOTS):
-            g_pass(last_a, t, 1)
-        o_passes(range(SLOTS), [2])
-        for t in range(SLOTS):
-            f_add(last_a, t)
+        f_quantize(6)
+        f_turn(7, 0)
+        f_turn(7, 1)
+        f_group(7, 0)
+        f_group(7, 1)
+        o_passes([0], [3])
+        o_passes([1], [3])
+        o_passes([2], [3])
+        o_passes([3], [3])
         f_quantize(3)
-        f_turn(5)
-        f_turn(last_a)
-        f_group(5)
-        f_group(last_a)
-        for t in range(SLOTS):
-            g_matmul(last_b, t)
         f_quantize(5)
-        f_add(last_b, 0)
-        f_quantize(last_a)
-        for t in range(1, SLOTS):
-            f_add(last_b, t)
-        o_passes(range(SLOTS), [CHUNKS - 1])
-        f_turn(last_b)
-        f_group(last_b)
         o_store(0)
+        o_passes([4], [0])
+        o_passes([4], [1])
+        o_passes([4], [2])
         o_store(1)
-        o_passes([4], range(CHUNKS - 1))
+        o_passes([5], [0])
+        o_passes([5], [1])
+        o_passes([5], [2])
+        f_quantize(7, 0, 2)
         o_store(2)
-        f_quantize(last_b, 0, 2)
-        o_passes([5], range(CHUNKS))
-        o_passes([4], [CHUNKS - 1])
+        o_passes([4], [3])
+        o_passes([5], [3])
+        f_quantize(7, 2, 4)
         o_store(3)
-        f_quantize(last_b, 2, 4)
-        o_passes([6, 7], range(CHUNKS))
-        for n in (5, 4, 6):
-            o_store(n)
+        o_passes([6], [0])
+        o_passes([6], [1])
+        o_passes([6], [2])
+        o_passes([6], [3])
+        o_store(4)
+        o_store(5)
+        o_passes([7], [0])
+        o_passes([7], [1])
+        o_passes([7], [2])
+        o_passes([7], [3])
+        o_store(6)
         o_store_in_halves(7)

@@ -22,6 +22,7 @@ SLOTS = 4
 GROUPS = M // (P * SLOTS)
 CHUNKS = D // N
 PARTS = GROUPS * CHUNKS
+E_BUFFER = [0, 1, 2, 3, 4, 5, 0, 1]
 
 MOVING_CODES, MOVING_SCALES, STILL_CODES, STILL_SCALES = 0, 64, 128, 192
 
@@ -140,8 +141,8 @@ def tile_tied_autoencoder_code_step_t2_kernel(
         free = list(range(8))
         held = {}
 
-        def take_bank(key):
-            k = free.pop(0)
+        def take_bank(key, newest=False):
+            k = free.pop(-1 if newest else 0)
             bank = psum.tile([P, N], F32, name="bank%d" % k, tag="bank%d" % k)
             held[key] = (k, bank)
             return bank
@@ -206,14 +207,14 @@ def tile_tied_autoencoder_code_step_t2_kernel(
 
         def e_slot(s, t):
             if s not in e32:
-                e32[s] = work.tile([P, SLOTS, N], F32, name="e32", bufs=6)
+                e32[s] = work.tile([P, SLOTS, N], F32, name="e32_%d" % E_BUFFER[s], bufs=1)
             return e32[s][:, t, :]
 
-        def r_matmul(s, t):
+        def r_matmul(s, t, newest=False):
             chunk, g = divmod(s, GROUPS)
             rows = slice(P * (SLOTS * g + t), P * (SLOTS * g + t + 1))
             nc.tensor.matmul_mx(
-                out=take_bank(("r", s, t))[:],
+                out=take_bank(("r", s, t), newest)[:],
                 lhsT=c_codes[:, rows].bitcast(E4M3X4),
                 lhsT_scale=c_planes[:, rows],
                 rhs=wd_sb[:, 2 * N * chunk : 2 * N * (chunk + 1)].bitcast(E2M1X4),
@@ -406,22 +407,24 @@ def tile_tied_autoencoder_code_step_t2_kernel(
         e_group_scalar(1, 384)
         g_pass(0, 0, 0)
         g_pass(0, 1, 0)
-        g_pass(0, 2, 0)
+        r_matmul(5, 0)
         sort_pt(0, 1)
         sort_pt(1, 1)
         e_group_vector(1, 384)
         r_copy(4, 1)
-        r_matmul(5, 0)
+        r_matmul(5, 1)
         r_copy(2, 0)
         sort_pt_scales(0, 1)
         sort_pt_scales(1, 1)
         r_copy(5, 0)
+        r_copy(5, 1)
         e_quantize(1)
         e_subtract_gpsimd(2, 0)
         g_pass(0, 0, 1)
         g_pass(0, 1, 1)
-        g_pass(0, 2, 1)
         r_matmul(3, 1)
+        g_pass(0, 2, 0)
+        g_pass(0, 2, 1)
         e_subtract(2, 1)
         r_matmul(3, 2)
         e_subtract(2, 2)
@@ -449,8 +452,8 @@ def tile_tied_autoencoder_code_step_t2_kernel(
         g_pass(1, 3, 0)
         g_pass(1, 3, 1)
         f_add(0, 3)
-        r_matmul(5, 1)
         r_matmul(6, 0)
+        r_matmul(6, 1)
         f_add(1, 0)
         f_turn(0, 0)
         f_turn(0, 1)
@@ -459,75 +462,76 @@ def tile_tied_autoencoder_code_step_t2_kernel(
         r_matmul(4, 3)
         e_quantize(2)
         f_group(0, 0)
-        r_copy(5, 1)
+        r_copy(6, 0)
         g_pass(2, 0, 0)
         e_quantize(3)
-        e_subtract_gpsimd(5, 1)
-        r_copy(6, 0)
-        f_group(0, 1)
-        f_add(1, 2)
-        g_pass(2, 0, 1)
-        r_matmul(6, 1)
-        f_add(1, 3)
-        g_pass(2, 1, 0)
-        g_pass(2, 1, 1)
-        e_subtract(4, 2)
-        e_subtract_gpsimd(5, 0)
+        e_subtract_gpsimd(6, 0)
         r_copy(6, 1)
-        r_matmul(5, 2)
+        f_group(0, 1)
+        e_subtract(4, 2)
+        g_pass(2, 0, 1)
+        g_pass(2, 1, 0)
         e_subtract(4, 3)
-        r_matmul(5, 3)
-        f_add(2, 0)
+        g_pass(2, 1, 1)
+        r_matmul(5, 2)
+        f_add(1, 2)
+        e_subtract_gpsimd(5, 0)
         e_group_scalar(4)
+        r_matmul(5, 3)
+        f_add(1, 3)
         g_pass(2, 2, 0)
         g_pass(2, 2, 1)
         e_subtract(5, 2)
-        e_subtract_gpsimd(6, 0)
+        f_turn(1, 0)
+        f_turn(1, 1)
+        e_subtract_gpsimd(5, 1)
         g_pass(2, 3, 0)
         g_pass(2, 3, 1)
-        f_add(2, 1)
+        e_subtract(5, 3)
+        f_group(1, 0)
+        f_group(1, 1)
         g_pass(3, 0, 0)
         g_pass(3, 0, 1)
-        e_subtract(5, 3)
+        f_add(2, 0)
         e_subtract_gpsimd(6, 1)
         g_pass(3, 1, 0)
         g_pass(3, 1, 1)
-        f_add(2, 2)
+        f_add(2, 1)
         e_group_scalar(5)
         g_pass(3, 2, 0)
         g_pass(3, 2, 1)
-        f_add(2, 3)
+        f_add(2, 2)
         g_pass(3, 3, 0)
         g_pass(3, 3, 1)
-        f_add(3, 0)
+        f_add(2, 3)
         r_matmul(7, 0)
         r_matmul(7, 1)
+        f_add(3, 0)
+        f_turn(2, 0)
+        f_turn(2, 1)
         f_add(3, 1)
-        f_turn(1, 0)
-        f_turn(1, 1)
-        f_add(3, 2)
         r_matmul(6, 2)
+        f_add(3, 2)
         r_matmul(6, 3)
         e_quantize(4)
-        f_group(1, 0)
+        f_group(2, 0)
         r_copy(7, 0)
         g_pass(4, 0, 0)
         e_quantize(5)
         e_subtract_gpsimd(7, 0)
         r_copy(7, 1)
-        f_group(1, 1)
-        f_add(3, 3)
+        f_group(2, 1)
+        e_subtract(6, 2)
         g_pass(4, 0, 1)
         e_subtract_gpsimd(7, 1)
         r_matmul(7, 2)
-        e_subtract(6, 2)
-        r_matmul(7, 3)
         e_subtract(6, 3)
+        r_matmul(7, 3)
+        f_add(3, 3)
         g_pass(4, 1, 0)
         g_pass(4, 1, 1)
         e_subtract(7, 2)
-        e_group_gpsimd(6, 384)
-        e_group_scalar(6, 384)
+        e_group_scalar(6)
         g_pass(4, 2, 0)
         g_pass(4, 2, 1)
         e_subtract(7, 3)
@@ -542,28 +546,22 @@ def tile_tied_autoencoder_code_step_t2_kernel(
         g_pass(5, 1, 0)
         g_pass(5, 1, 1)
         f_add(4, 2)
-        f_turn(2, 0)
-        f_turn(2, 1)
         f_turn(3, 0)
+        f_turn(3, 1)
+        f_turn(4, 0)
         f_add(4, 3)
         g_pass(5, 2, 0)
         g_pass(5, 2, 1)
         e_quantize(6)
-        f_group(2, 0)
-        f_group(2, 1)
         f_group(3, 0)
+        f_group(3, 1)
+        f_group(4, 0)
         e_quantize(7)
         g_pass(5, 3, 0)
         g_pass(5, 3, 1)
-        f_turn(3, 1)
-        f_turn(4, 0)
-        f_turn(4, 1)
         f_add(5, 0)
         g_pass(6, 0, 0)
         g_pass(6, 0, 1)
-        f_group(3, 1)
-        f_group(4, 0)
-        f_group(4, 1)
         f_add(5, 1)
         g_pass(6, 1, 0)
         g_pass(6, 1, 1)
@@ -573,6 +571,12 @@ def tile_tied_autoencoder_code_step_t2_kernel(
         f_add(5, 3)
         g_pass(6, 3, 0)
         g_pass(6, 3, 1)
+        f_turn(4, 1)
+        f_turn(5, 0)
+        f_turn(5, 1)
+        f_group(4, 1)
+        f_group(5, 0)
+        f_group(5, 1)
         f_quantize(0)
         f_add(6, 0)
         g_pass(7, 0, 0)
@@ -590,8 +594,6 @@ def tile_tied_autoencoder_code_step_t2_kernel(
         o_passes([0], [0])
         o_passes([0], [1])
         f_add(7, 0)
-        f_turn(5, 0)
-        f_turn(5, 1)
         f_turn(6, 0)
         f_turn(6, 1)
         f_add(7, 1)
@@ -600,8 +602,6 @@ def tile_tied_autoencoder_code_step_t2_kernel(
         f_add(7, 3)
         f_group(6, 0)
         f_group(6, 1)
-        f_group(5, 0)
-        f_group(5, 1)
         o_passes([1], [0])
         o_passes([1], [1])
         o_passes([0], [2])
@@ -609,11 +609,8 @@ def tile_tied_autoencoder_code_step_t2_kernel(
         o_passes([2], [0])
         o_passes([2], [1])
         o_passes([2], [2])
-        o_passes([3], [0])
-        o_passes([3], [1])
-        o_passes([3], [2])
-        f_quantize(1)
         f_quantize(6)
+        f_quantize(1)
         f_turn(7, 0)
         f_turn(7, 1)
         f_group(7, 0)
@@ -621,6 +618,9 @@ def tile_tied_autoencoder_code_step_t2_kernel(
         o_passes([0], [3])
         o_passes([1], [3])
         o_passes([2], [3])
+        o_passes([3], [0])
+        o_passes([3], [1])
+        o_passes([3], [2])
         o_passes([3], [3])
         f_quantize(3)
         f_quantize(5)

@@ -115,9 +115,9 @@ def tile_tied_autoencoder_code_step_t2_kernel(
         load_pt_scales(0)
         load_c(2)
         load_c(3)
+        load_pt(0)
         load_wd(0 * N, 1 * N)
         load_wd_scales(wd_pl_first, 0, N)
-        load_pt(0)
         load_x_half(0, 0)
         load_x_half(0, 1)
         load_x_half(1, 0)
@@ -350,6 +350,28 @@ def tile_tied_autoencoder_code_step_t2_kernel(
             nc.vector.tensor_tensor(out=o_sb[:], in0=read_bank(("o", n))[:], in1=rate_sb[:], op=ALU.mult)
             nc.sync.dma_start(out=out_view[g][:, t, :], in_=o_sb[:])
 
+        def o_quarter(n, q):
+            g, t = divmod(n, SLOTS)
+            bank = take_bank(("q", q))
+            for chunk in range(CHUNKS):
+                h = GROUPS * chunk + g
+                nc.tensor.matmul_mx(
+                    out=bank[:, :P],
+                    lhsT=f_codes[h][:, P * t : P * (t + 1)].bitcast(E4M3X4),
+                    lhsT_scale=f_planes[h][:, P * t : P * (t + 1)],
+                    rhs=wb_sb[:, chunk, 2 * P * q : 2 * P * (q + 1)].bitcast(E2M1X4),
+                    rhs_scale=wb_pl[:, chunk, P * q : P * (q + 1)],
+                    start=(chunk == 0),
+                    stop=(chunk == CHUNKS - 1),
+                )
+
+        def o_store_quarter(n, q):
+            g, t = divmod(n, SLOTS)
+            cols = slice(P * q, P * (q + 1))
+            o_part = work.tile([P, P], F32, name="o_part", bufs=4)
+            nc.vector.tensor_tensor(out=o_part[:], in0=read_bank(("q", q))[:, :P], in1=rate_sb[:, cols], op=ALU.mult)
+            nc.sync.dma_start(out=out_view[g][:, t, cols], in_=o_part[:])
+
         def o_store_in_halves(n):
             g, t = divmod(n, SLOTS)
             bank = read_bank(("o", n))
@@ -364,16 +386,14 @@ def tile_tied_autoencoder_code_step_t2_kernel(
         turn_c(2, 2)
         sort_pt_scales(0, 0)
         quantize_c(0, 1)
-        sort_c(2)
         quantize_c(1, 1)
-        sort_c(3)
+        sort_pt_scales(1, 0)
         turn_c(4, 2)
         turn_c(6, 2)
         quantize_c(2, 2)
-        sort_pt_scales(1, 0)
         sort_pt(0, 0)
-        quantize_c(4, 2)
         sort_pt(1, 0)
+        quantize_c(4, 2)
         r_matmul(0, 0)
         r_matmul(0, 1)
         r_matmul(0, 2)
@@ -452,28 +472,27 @@ def tile_tied_autoencoder_code_step_t2_kernel(
         g_pass(1, 3, 0)
         g_pass(1, 3, 1)
         f_add(0, 3)
-        r_matmul(6, 0)
-        r_matmul(6, 1)
-        f_add(1, 0)
+        r_matmul(5, 2)
         f_turn(0, 0)
         f_turn(0, 1)
-        f_add(1, 1)
+        f_add(1, 0)
         r_matmul(4, 2)
         r_matmul(4, 3)
         e_quantize(2)
         f_group(0, 0)
-        r_copy(6, 0)
+        r_matmul(6, 0)
+        f_add(1, 1)
         g_pass(2, 0, 0)
+        r_copy(5, 2)
         e_quantize(3)
-        e_subtract_gpsimd(6, 0)
-        r_copy(6, 1)
+        e_subtract_gpsimd(5, 2)
+        r_copy(6, 0)
         f_group(0, 1)
         e_subtract(4, 2)
         g_pass(2, 0, 1)
         g_pass(2, 1, 0)
-        e_subtract(4, 3)
         g_pass(2, 1, 1)
-        r_matmul(5, 2)
+        e_subtract(4, 3)
         f_add(1, 2)
         e_subtract_gpsimd(5, 0)
         e_group_scalar(4)
@@ -481,19 +500,16 @@ def tile_tied_autoencoder_code_step_t2_kernel(
         f_add(1, 3)
         g_pass(2, 2, 0)
         g_pass(2, 2, 1)
-        e_subtract(5, 2)
-        f_turn(1, 0)
-        f_turn(1, 1)
+        r_matmul(6, 1)
+        e_subtract(5, 3)
         e_subtract_gpsimd(5, 1)
         g_pass(2, 3, 0)
         g_pass(2, 3, 1)
-        e_subtract(5, 3)
-        f_group(1, 0)
-        f_group(1, 1)
         g_pass(3, 0, 0)
         g_pass(3, 0, 1)
         f_add(2, 0)
-        e_subtract_gpsimd(6, 1)
+        r_copy(6, 1)
+        e_subtract_gpsimd(6, 0)
         g_pass(3, 1, 0)
         g_pass(3, 1, 1)
         f_add(2, 1)
@@ -501,35 +517,38 @@ def tile_tied_autoencoder_code_step_t2_kernel(
         g_pass(3, 2, 0)
         g_pass(3, 2, 1)
         f_add(2, 2)
+        e_subtract_gpsimd(6, 1)
         g_pass(3, 3, 0)
         g_pass(3, 3, 1)
         f_add(2, 3)
         r_matmul(7, 0)
-        r_matmul(7, 1)
         f_add(3, 0)
+        f_turn(1, 0)
+        f_turn(1, 1)
         f_turn(2, 0)
-        f_turn(2, 1)
         f_add(3, 1)
         r_matmul(6, 2)
-        f_add(3, 2)
+        f_group(1, 0)
+        f_group(1, 1)
         r_matmul(6, 3)
+        r_matmul(7, 1)
+        f_add(3, 2)
+        r_matmul(7, 2)
+        f_add(3, 3)
         e_quantize(4)
-        f_group(2, 0)
-        r_copy(7, 0)
         g_pass(4, 0, 0)
+        r_copy(7, 0)
         e_quantize(5)
         e_subtract_gpsimd(7, 0)
+        f_group(2, 0)
         r_copy(7, 1)
-        f_group(2, 1)
         e_subtract(6, 2)
         g_pass(4, 0, 1)
-        e_subtract_gpsimd(7, 1)
-        r_matmul(7, 2)
-        e_subtract(6, 3)
-        r_matmul(7, 3)
-        f_add(3, 3)
         g_pass(4, 1, 0)
         g_pass(4, 1, 1)
+        e_subtract_gpsimd(7, 1)
+        e_subtract(6, 3)
+        r_matmul(7, 3)
         e_subtract(7, 2)
         e_group_scalar(6)
         g_pass(4, 2, 0)
@@ -543,19 +562,19 @@ def tile_tied_autoencoder_code_step_t2_kernel(
         g_pass(5, 0, 1)
         e_group_scalar(7, 256)
         f_add(4, 1)
-        g_pass(5, 1, 0)
-        g_pass(5, 1, 1)
-        f_add(4, 2)
+        f_turn(2, 1)
         f_turn(3, 0)
         f_turn(3, 1)
-        f_turn(4, 0)
+        f_add(4, 2)
+        g_pass(5, 1, 0)
+        g_pass(5, 1, 1)
         f_add(4, 3)
         g_pass(5, 2, 0)
         g_pass(5, 2, 1)
         e_quantize(6)
+        f_group(2, 1)
         f_group(3, 0)
         f_group(3, 1)
-        f_group(4, 0)
         e_quantize(7)
         g_pass(5, 3, 0)
         g_pass(5, 3, 1)
@@ -566,18 +585,18 @@ def tile_tied_autoencoder_code_step_t2_kernel(
         g_pass(6, 1, 0)
         g_pass(6, 1, 1)
         f_add(5, 2)
-        g_pass(6, 2, 0)
-        g_pass(6, 2, 1)
-        f_add(5, 3)
-        g_pass(6, 3, 0)
-        g_pass(6, 3, 1)
+        f_turn(4, 0)
         f_turn(4, 1)
         f_turn(5, 0)
-        f_turn(5, 1)
+        f_add(5, 3)
+        g_pass(6, 2, 0)
+        g_pass(6, 2, 1)
+        f_group(4, 0)
         f_group(4, 1)
         f_group(5, 0)
-        f_group(5, 1)
         f_quantize(0)
+        g_pass(6, 3, 0)
+        g_pass(6, 3, 1)
         f_add(6, 0)
         g_pass(7, 0, 0)
         g_pass(7, 0, 1)
@@ -594,6 +613,7 @@ def tile_tied_autoencoder_code_step_t2_kernel(
         o_passes([0], [0])
         o_passes([0], [1])
         f_add(7, 0)
+        f_turn(5, 1)
         f_turn(6, 0)
         f_turn(6, 1)
         f_add(7, 1)
@@ -602,6 +622,7 @@ def tile_tied_autoencoder_code_step_t2_kernel(
         f_add(7, 3)
         f_group(6, 0)
         f_group(6, 1)
+        f_group(5, 1)
         o_passes([1], [0])
         o_passes([1], [1])
         o_passes([0], [2])

@@ -21,8 +21,10 @@ N = 512
 SLOTS = 4
 GROUPS = M // (P * SLOTS)
 CHUNKS = D // N
-PARTS = GROUPS * CHUNKS
-E_BUFFER = [0, 1, 2, 3, 4, 5, 0, 1]
+SHARE = 320
+SHARE0 = 128
+EARLY = 2
+SHARE_LAST = 224
 
 MOVING_CODES, MOVING_SCALES, STILL_CODES, STILL_SCALES = 0, 64, 128, 192
 
@@ -44,24 +46,29 @@ def tile_tied_autoencoder_code_step_t2_kernel(
 
         ident = keep.tile([P, P], F32, name="ident")
         c_raw = [keep.tile([P, 2, H], BF16, name="c_raw%d" % k) for k in range(4)]
+        c_sorted = {k: keep.tile([P, 2, 2, P], F32, name="c_sorted%d" % k) for k in range(2, 4)}
         c_grp = keep.tile([P, 4 * M], BF16, name="c_grp", align_bytes=64)
         c_codes = placed(keep, "c_codes", M, U32, 4, STILL_CODES)
         c_planes = placed(keep, "c_planes", M, U8, 1, STILL_SCALES)
-        x_half = {(s, j): keep.tile([P, 2, N], BF16, name="x_sb%d_%d" % (s, j)) for s in range(2) for j in range(2)}
-        x_rest = {s: keep.tile([P, SLOTS, N], BF16, name="x_sb%d" % s) for s in range(2, PARTS)}
-        wd_sb = placed(keep, "wd_sb", 2 * D, U8, 1, MOVING_CODES)
+        x_half = {(g, j): keep.tile([P, 2, N], BF16, name="x_first%d_%d" % (g, j)) for g in range(2) for j in range(2)}
+        x_rest = {
+            (n, g): keep.tile([P, SLOTS, N], BF16, name="x_sb%d_%d" % (n, g)) for n in range(1, CHUNKS) for g in range(2)
+        }
+        wd_first = placed(keep, "wd_first", 2 * N, U8, 1, MOVING_CODES)
+        wd_second = placed(keep, "wd_second", 2 * N, U8, 1, MOVING_CODES)
+        wd_rest = placed(keep, "wd_rest", 2 * (D - 2 * N), U8, 1, MOVING_CODES)
         wd_pl_first = placed(keep, "wd_pl_first", N, U8, 1, MOVING_SCALES)
         wd_pl_rest = placed(keep, "wd_pl_rest", D - N, U8, 1, MOVING_SCALES)
         pt_raw = [keep.tile([P, GROUPS, 2 * N], U8, name="pt_raw%d" % j, align_bytes=64) for j in range(GROUPS)]
         pt_sb = {(k, j): placed(keep, "pt_sb%d_%d" % (k, j), 2 * N, U8, 1, STILL_CODES) for k in range(2) for j in range(2)}
-        pt_plraw = [keep.tile([P, GROUPS, N], U8, name="pt_plraw%d" % j, align_bytes=64) for j in range(GROUPS)]
+        pt_plraw = keep.tile([P, GROUPS, M], U8, name="pt_plraw", align_bytes=64)
         pt_pl = {(k, j): placed(keep, "pt_pl%d_%d" % (k, j), N, U8, 1, STILL_SCALES) for k in range(2) for j in range(2)}
         wb_sb = placed(keep, "wb_sb", CHUNKS * 2 * H, U8, 1, MOVING_CODES).rearrange("p (g w) -> p g w", g=CHUNKS)
         wb_pl = placed(keep, "wb_pl", CHUNKS * H, U8, 1, MOVING_SCALES).rearrange("p (g w) -> p g w", g=CHUNKS)
         a_sb = keep.tile([P, GROUPS, SLOTS], BF16, name="a_sb")
         rate_sb = keep.tile([P, H], BF16, name="rate_sb")
-        f_codes = [placed(keep, "f_codes%d" % h, N, U32, 4, STILL_CODES) for h in range(PARTS)]
-        f_planes = [placed(keep, "f_planes%d" % h, N, U8, 1, STILL_SCALES) for h in range(PARTS)]
+        f_codes = {(n, g): placed(keep, "f_codes%d_%d" % (n, g), N, U32, 4, STILL_CODES) for n in range(CHUNKS) for g in range(2)}
+        f_planes = {(n, g): placed(keep, "f_planes%d_%d" % (n, g), N, U8, 1, STILL_SCALES) for n in range(CHUNKS) for g in range(2)}
 
         c_view = c.rearrange("(g p t) k -> g p t k", p=P, t=SLOTS)
         x_view = x.rearrange("(g p t) d -> g p t d", p=P, t=SLOTS)
@@ -70,20 +77,17 @@ def tile_tied_autoencoder_code_step_t2_kernel(
         def load_c(k):
             nc.sync.dma_start(out=c_raw[k][:], in_=c_view[k // 2][:, 2 * (k % 2) : 2 * (k % 2) + 2, :])
 
-        def load_x_half(s, j):
-            nc.sync.dma_start(out=x_half[s, j][:], in_=x_view[s][:, 2 * j : 2 * j + 2, 0:N])
+        def load_x_half(g, j):
+            nc.sync.dma_start(out=x_half[g, j][:], in_=x_view[g][:, 2 * j : 2 * j + 2, 0:N])
 
-        def load_x(s):
-            chunk, g = divmod(s, GROUPS)
-            nc.sync.dma_start(out=x_rest[s][:], in_=x_view[g][:, :, N * chunk : N * (chunk + 1)])
+        def load_x(n, g):
+            nc.sync.dma_start(out=x_rest[n, g][:], in_=x_view[g][:, :, N * n : N * (n + 1)])
 
-        def x_slot(s, t):
-            return x_half[s, t // 2][:, t % 2, :] if s < 2 else x_rest[s][:, t, :]
+        def x_slot(n, g, t):
+            return x_half[g, t // 2][:, t % 2, :] if n == 0 else x_rest[n, g][:, t, :]
 
-        def load_wd(lo, hi):
-            nc.sync.dma_start(
-                out=wd_sb[:, 2 * lo : 2 * hi].bitcast(I32), in_=wd_words[0][:, 2 * lo : 2 * hi].bitcast(I32)
-            )
+        def load_wd(tile, lo, hi):
+            nc.sync.dma_start(out=tile[:].bitcast(I32), in_=wd_words[0][:, 2 * lo : 2 * hi].bitcast(I32))
 
         def load_wd_scales(plane, lo, hi):
             for r in range(4):
@@ -100,49 +104,22 @@ def tile_tied_autoencoder_code_step_t2_kernel(
             cols = pt_words[:, :, 2 * N * j : 2 * N * (j + 1)]
             nc.sync.dma_start(out=pt_raw[j][:].bitcast(I32), in_=cols.rearrange("g p w -> p g w").bitcast(I32))
 
-        def load_pt_scales(j):
-            load_scales(pt_plraw[j], pt_scales[:, :, N * j : N * (j + 1)])
+        def load_pt_scales():
+            load_scales(pt_plraw, pt_scales)
 
-        nc.vector.memset(pt_plraw[0][:].rearrange("p g n -> p (g n)").bitcast(I32), 0)
-        nc.vector.memset(wd_pl_first[:].bitcast(I32), 0)
-        nc.vector.memset(wd_pl_rest[:].bitcast(I32), 0)
-        nc.vector.memset(pt_plraw[1][:].rearrange("p g n -> p (g n)").bitcast(I32), 0)
-        nc.vector.memset(wb_pl[:].rearrange("p g n -> p (g n)").bitcast(I32), 0)
-        make_identity(nc, ident[:])
+        def load_a():
+            nc.sync.dma_start(out=a_sb[:], in_=a.rearrange("(g p t) -> p g t", p=P, t=SLOTS))
 
-        load_c(0)
-        load_c(1)
-        load_pt_scales(0)
-        load_c(2)
-        load_c(3)
-        load_pt(0)
-        load_wd(0 * N, 1 * N)
-        load_wd_scales(wd_pl_first, 0, N)
-        load_x_half(0, 0)
-        load_x_half(0, 1)
-        load_x_half(1, 0)
-        load_wd(1 * N, 4 * N)
-        load_wd_scales(wd_pl_rest, N, D)
-        load_x_half(1, 1)
-        load_pt(1)
-        load_pt_scales(1)
-        load_x(2)
-        load_x(3)
-        nc.sync.dma_start(out=a_sb[:], in_=a.rearrange("(g p t) -> p g t", p=P, t=SLOTS))
-        load_x(4)
-        load_x(5)
-        load_x(6)
-        load_x(7)
-        load_scales(wb_pl, wb_scales)
-        nc.sync.dma_start(out=wb_sb[:].bitcast(I32), in_=wb_words.rearrange("g p w -> p g w").bitcast(I32))
-        nc.sync.dma_start(out=rate_sb[:], in_=rate.partition_broadcast(P))
-
+        def load_wb():
+            load_scales(wb_pl, wb_scales)
+            nc.sync.dma_start(out=wb_sb[:].bitcast(I32), in_=wb_words.rearrange("g p w -> p g w").bitcast(I32))
+            nc.sync.dma_start(out=rate_sb[:], in_=rate.partition_broadcast(P))
 
         free = list(range(8))
         held = {}
 
-        def take_bank(key, newest=False):
-            k = free.pop(-1 if newest else 0)
+        def take_bank(key):
+            k = free.pop(0)
             bank = psum.tile([P, N], F32, name="bank%d" % k, tag="bank%d" % k)
             held[key] = (k, bank)
             return bank
@@ -152,37 +129,30 @@ def tile_tied_autoencoder_code_step_t2_kernel(
             free.append(k)
             return bank
 
-        c_sorted = {}
-
         def sort_c(k):
-            c_sorted[k] = keep.tile([P, 2, 2, P], F32, name="c_sorted%d" % k)
             nc.vector.tensor_copy(
                 out=c_sorted[k][:], in_=c_raw[k][:].bitcast(F32).rearrange("p j (m u) -> p j u m", u=2)
             )
 
-        def turn_c(first, count):
-            turned = take_bank("c")
-            for i in range(count):
-                k, j = divmod(first + i, 2)
+        def turn_c(k, is_sorted=True, lo_j=0, hi_j=2):
+            turned = take_bank(("c", k, lo_j))
+            for j in range(lo_j, hi_j):
                 for u in range(2):
-                    if k in c_sorted:
-                        words = c_sorted[k][:, j, u, :]
-                    else:
-                        words = c_raw[k][:, j, :].bitcast(F32)[:, u : 2 * P : 2]
-                    lo = P * (2 * i + u)
+                    words = c_sorted[k][:, j, u, :] if is_sorted else c_raw[k][:, j, :].bitcast(F32)[:, u : 2 * P : 2]
+                    lo = P * (2 * j + u)
                     nc.tensor.transpose(turned[:, lo : lo + P], words, ident[:])
-            grouped = c_grp[:, N * first : N * (first + count)].bitcast(F32)
+
+        def group_c(k, lo_j=0, hi_j=2):
+            grouped = c_grp[:, N * (2 * k + lo_j) : N * (2 * k + hi_j)].bitcast(F32)
             nc.scalar.copy(
-                out=grouped.rearrange("p (i r u) -> p i r u", i=count, u=2),
-                in_=read_bank("c")[:, : 2 * P * count].rearrange("p (i u r) -> p i r u", i=count, u=2),
+                out=grouped.rearrange("p (i r u) -> p i r u", i=hi_j - lo_j, u=2),
+                in_=read_bank(("c", k, lo_j))[:, 2 * P * lo_j : 2 * P * hi_j].rearrange("p (i u r) -> p i r u", i=hi_j - lo_j, u=2),
             )
 
-        def quantize_c(first, count):
-            cols = slice(P * first, P * (first + count))
+        def quantize_c(k, lo_j=0, hi_j=2):
+            lo, hi = 2 * k + lo_j, 2 * k + hi_j
             nc.vector.quantize_mx(
-                out=c_codes[:, cols].bitcast(E4M3X4),
-                scales=c_planes[:, cols],
-                in_=c_grp[:, N * first : N * (first + count)],
+                out=c_codes[:, P * lo : P * hi].bitcast(E4M3X4), scales=c_planes[:, P * lo : P * hi], in_=c_grp[:, N * lo : N * hi]
             )
 
         def sort_pt(k, j):
@@ -191,13 +161,19 @@ def tile_tied_autoencoder_code_step_t2_kernel(
                 in_=pt_raw[j][:, k, :].bitcast(U16).rearrange("p (m t) -> p t m", t=SLOTS),
             )
 
+        def sort_pt_scalar(k, j):
+            nc.scalar.copy(
+                out=pt_sb[k, j][:].bitcast(U16).rearrange("p (t m) -> p t m", t=SLOTS),
+                in_=pt_raw[j][:, k, :].bitcast(U16).rearrange("p (m t) -> p t m", t=SLOTS),
+            )
+
         def sort_pt_scales(k, j):
             nc.vector.tensor_copy(
                 out=pt_pl[k, j][:].rearrange("p (t m) -> p t m", t=SLOTS),
-                in_=pt_plraw[j][:, k, :].rearrange("p (m t) -> p t m", t=SLOTS),
+                in_=pt_plraw[:, k, N * j : N * (j + 1)].rearrange("p (m t) -> p t m", t=SLOTS),
             )
 
-        e32, e_grp, e_codes, e_planes = {}, {}, {}, {}
+        e32, e_grp, e_codes, e_planes, r_aside = {}, {}, {}, {}, {}
 
         def as_stored(ap):
             return ap.rearrange("p (u m e) -> p u m e", u=2, e=2)
@@ -205,469 +181,391 @@ def tile_tied_autoencoder_code_step_t2_kernel(
         def into_stored(ap):
             return ap.rearrange("p (m u e) -> p u m e", u=2, e=2)
 
-        def e_slot(s, t):
-            if s not in e32:
-                e32[s] = work.tile([P, SLOTS, N], F32, name="e32_%d" % E_BUFFER[s], bufs=1)
-            return e32[s][:, t, :]
+        def e_part(n, g):
+            if (n, g) not in e32:
+                e32[n, g] = work.tile([P, SLOTS, N], F32, name="e32_%d" % g, bufs=3 - g)
+            return e32[n, g]
 
-        def r_matmul(s, t, newest=False):
-            chunk, g = divmod(s, GROUPS)
+        def r_matmul(n, g, t):
             rows = slice(P * (SLOTS * g + t), P * (SLOTS * g + t + 1))
+            words = [wd_first[:], wd_second[:], wd_rest[:, : 2 * N], wd_rest[:, 2 * N :]][n]
             nc.tensor.matmul_mx(
-                out=take_bank(("r", s, t), newest)[:],
+                out=take_bank(("r", n, g, t))[:],
                 lhsT=c_codes[:, rows].bitcast(E4M3X4),
                 lhsT_scale=c_planes[:, rows],
-                rhs=wd_sb[:, 2 * N * chunk : 2 * N * (chunk + 1)].bitcast(E2M1X4),
-                rhs_scale=wd_pl_first[:] if chunk == 0 else wd_pl_rest[:, N * (chunk - 1) : N * chunk],
+                rhs=words.bitcast(E2M1X4),
+                rhs_scale=wd_pl_first[:] if n == 0 else wd_pl_rest[:, N * (n - 1) : N * n],
                 start=True,
                 stop=True,
             )
 
-        def e_subtract(s, t):
+        def e_subtract(n, g, t):
             nc.vector.tensor_tensor(
-                out=e_slot(s, t).rearrange("p (u m e) -> p m u e", u=2, e=2),
-                in0=x_slot(s, t).rearrange("p (m u e) -> p m u e", u=2, e=2),
-                in1=read_bank(("r", s, t))[:].rearrange("p (m u e) -> p m u e", u=2, e=2),
+                out=e_part(n, g)[:, t, :].rearrange("p (u m e) -> p m u e", u=2, e=2),
+                in0=x_slot(n, g, t).rearrange("p (m u e) -> p m u e", u=2, e=2),
+                in1=read_bank(("r", n, g, t))[:].rearrange("p (m u e) -> p m u e", u=2, e=2),
                 op=ALU.subtract,
             )
 
-        def r_copy(s, t):
-            nc.scalar.copy(out=as_stored(e_slot(s, t)), in_=into_stored(read_bank(("r", s, t))[:]))
+        def r_copy(n, g, t):
+            r_aside[n, g, t] = work.tile([P, N], F32, name="r_aside", bufs=4)
+            nc.scalar.copy(out=as_stored(r_aside[n, g, t][:]), in_=into_stored(read_bank(("r", n, g, t))[:]))
 
-        def e_subtract_gpsimd(s, t):
-            dst = as_stored(e_slot(s, t))
-            nc.gpsimd.tensor_tensor(out=dst, in0=into_stored(x_slot(s, t)), in1=dst, op=ALU.subtract)
-
-        def grouped_e(s, lo, hi):
-            if s not in e_grp:
-                e_grp[s] = work.tile([P, N, SLOTS], BF16, name="e_grp", bufs=2, align_bytes=64)
-            return e_grp[s][:, lo:hi, :]
-
-        def e_group_scalar(s, hi=N):
-            nc.scalar.copy(
-                out=grouped_e(s, 0, hi).rearrange("p (c i) (w e) -> p c w i e", i=2, e=2),
-                in_=e32[s][:, :, :hi].rearrange("p (w e) (c i) -> p c w i e", i=2, e=2),
+        def e_subtract_gpsimd(n, g, t):
+            nc.gpsimd.tensor_tensor(
+                out=as_stored(e_part(n, g)[:, t, :]),
+                in0=into_stored(x_slot(n, g, t)),
+                in1=as_stored(r_aside[n, g, t][:]),
+                op=ALU.subtract,
             )
 
-        def e_group_vector(s, lo):
-            nc.vector.tensor_copy(out=grouped_e(s, lo, N), in_=e32[s][:, :, lo:].rearrange("p t n -> p n t"))
+        def grouped_e(n, g, lo, hi):
+            if n not in e_grp:
+                e_grp[n] = work.tile([P, GROUPS, N, SLOTS], BF16, name="e_grp", bufs=1, align_bytes=64)
+            return e_grp[n][:, g, lo:hi, :]
 
-        def e_group_gpsimd(s, lo):
+        def e_group_scalar(n, g, lo=0, hi=N):
+            nc.scalar.copy(
+                out=grouped_e(n, g, lo, hi).rearrange("p (c i) (w e) -> p c w i e", i=2, e=2),
+                in_=e32[n, g][:, :, lo:hi].rearrange("p (w e) (c i) -> p c w i e", i=2, e=2),
+            )
+
+        def e_group_vector(n, g, lo, hi=N):
+            nc.vector.tensor_copy(out=grouped_e(n, g, lo, hi), in_=e32[n, g][:, :, lo:hi].rearrange("p t n -> p n t"))
+
+        def e_group_gpsimd(n, g, lo, hi=N):
             nc.gpsimd.tensor_scalar(
-                out=grouped_e(s, lo, N),
-                in0=e32[s][:, :, lo:].rearrange("p t n -> p n t"),
+                out=grouped_e(n, g, lo, hi),
+                in0=e32[n, g][:, :, lo:hi].rearrange("p t n -> p n t"),
                 scalar1=1.0,
                 scalar2=0.0,
                 op0=ALU.mult,
                 op1=ALU.add,
             )
 
-        def e_quantize(s):
-            e_codes[s] = placed(work, "e_codes", N, U32, 4, MOVING_CODES, bufs=4)
-            e_planes[s] = placed(work, "e_planes", N, U8, 1, MOVING_SCALES, bufs=4)
+        def e_quantize(n, lo=0, hi=GROUPS):
+            if n not in e_codes:
+                e_codes[n] = placed(work, "e_codes", GROUPS * N, U32, 4, MOVING_CODES, bufs=2)
+                e_planes[n] = placed(work, "e_planes", GROUPS * N, U8, 1, MOVING_SCALES, bufs=2)
             nc.vector.quantize_mx(
-                out=e_codes[s][:].bitcast(E4M3X4),
-                scales=e_planes[s][:],
-                in_=e_grp[s][:].rearrange("p n t -> p (n t)"),
+                out=e_codes[n][:, N * lo : N * hi].bitcast(E4M3X4),
+                scales=e_planes[n][:, N * lo : N * hi],
+                in_=e_grp[n][:, lo:hi, :, :].rearrange("p g n t -> p (g n t)"),
             )
 
         f_sb, f_grp = {}, {}
 
-        def g_pass(h, t, k):
-            chunk, g = divmod(h, GROUPS)
+        def g_pass(n, g, t, k):
             if k == 0:
-                take_bank(("g", h, t))
+                take_bank(("g", n, g, t))
             nc.tensor.matmul_mx(
-                out=held[("g", h, t)][1][:],
+                out=held[("g", n, g, t)][1][:],
                 lhsT=pt_sb[k, g][:, 2 * P * t : 2 * P * (t + 1)].bitcast(E2M1X4),
                 lhsT_scale=pt_pl[k, g][:, P * t : P * (t + 1)],
-                rhs=e_codes[GROUPS * chunk + k][:].bitcast(E4M3X4),
-                rhs_scale=e_planes[GROUPS * chunk + k][:],
+                rhs=e_codes[n][:, N * k : N * (k + 1)].bitcast(E4M3X4),
+                rhs_scale=e_planes[n][:, N * k : N * (k + 1)],
                 start=(k == 0),
                 stop=(k == GROUPS - 1),
             )
 
-        def g_matmul(h, t):
+        def g_matmul(n, g, t):
             for k in range(GROUPS):
-                g_pass(h, t, k)
+                g_pass(n, g, t, k)
 
-        def f_add(h, t):
-            if h not in f_sb:
-                f_sb[h] = work.tile([P, SLOTS, N], BF16, name="f_sb", bufs=4)
+        def f_add(n, g, t):
+            if (n, g) not in f_sb:
+                f_sb[n, g] = work.tile([P, SLOTS, N], BF16, name="f_sb", bufs=3)
             nc.vector.scalar_tensor_tensor(
-                out=f_sb[h][:, t, :],
-                in0=e32[h][:, t, :],
-                scalar=a_sb[:, h % GROUPS, t : t + 1],
-                in1=read_bank(("g", h, t))[:],
+                out=f_sb[n, g][:, t, :],
+                in0=e32[n, g][:, t, :],
+                scalar=a_sb[:, g, t : t + 1],
+                in1=read_bank(("g", n, g, t))[:],
                 op0=ALU.mult,
                 op1=ALU.add,
             )
 
-        def f_turn(h, pair):
-            turned = take_bank(("t", h, pair))
+        def f_turn(n, g, pair):
+            turned = take_bank(("t", n, g, pair))
             for i in range(2):
-                words = f_sb[h][:, 2 * pair + i, :].bitcast(F32)
+                words = f_sb[n, g][:, 2 * pair + i, :].bitcast(F32)
                 for u in range(2):
                     lo = P * (2 * i + u)
                     nc.tensor.transpose(turned[:, lo : lo + P], words[:, P * u : P * (u + 1)], ident[:])
 
-        def f_group(h, pair):
-            if h not in f_grp:
-                f_grp[h] = work.tile([P, SLOTS * N], BF16, name="f_grp", bufs=6, align_bytes=64)
-            grouped = f_grp[h][:, 2 * N * pair : 2 * N * (pair + 1)].bitcast(F32)
+        def f_group(n, g, pair):
+            if (n, g) not in f_grp:
+                f_grp[n, g] = work.tile([P, SLOTS * N], BF16, name="f_grp", bufs=6, align_bytes=64)
+            grouped = f_grp[n, g][:, 2 * N * pair : 2 * N * (pair + 1)].bitcast(F32)
             nc.scalar.copy(
                 out=grouped.rearrange("p (i r u) -> p i r u", i=2, u=2),
-                in_=read_bank(("t", h, pair))[:].rearrange("p (i u r) -> p i r u", i=2, u=2),
+                in_=read_bank(("t", n, g, pair))[:].rearrange("p (i u r) -> p i r u", i=2, u=2),
             )
 
-        def f_quantize(h, lo=0, hi=SLOTS):
+        def f_quantize(n, g, lo=0, hi=SLOTS):
             nc.vector.quantize_mx(
-                out=f_codes[h][:, P * lo : P * hi].bitcast(E4M3X4),
-                scales=f_planes[h][:, P * lo : P * hi],
-                in_=f_grp[h][:, N * lo : N * hi],
+                out=f_codes[n, g][:, P * lo : P * hi].bitcast(E4M3X4),
+                scales=f_planes[n, g][:, P * lo : P * hi],
+                in_=f_grp[n, g][:, N * lo : N * hi],
             )
 
-        def o_passes(slots, chunks):
-            for n in slots:
-                g, t = divmod(n, SLOTS)
-                for chunk in chunks:
-                    if chunk == 0:
-                        take_bank(("o", n))
-                    h = GROUPS * chunk + g
-                    nc.tensor.matmul_mx(
-                        out=held[("o", n)][1][:],
-                        lhsT=f_codes[h][:, P * t : P * (t + 1)].bitcast(E4M3X4),
-                        lhsT_scale=f_planes[h][:, P * t : P * (t + 1)],
-                        rhs=wb_sb[:, chunk, :].bitcast(E2M1X4),
-                        rhs_scale=wb_pl[:, chunk, :],
-                        start=(chunk == 0),
-                        stop=(chunk == CHUNKS - 1),
-                    )
+        def o_pass(g, t, n):
+            if n == 0:
+                take_bank(("o", g, t))
+            nc.tensor.matmul_mx(
+                out=held[("o", g, t)][1][:],
+                lhsT=f_codes[n, g][:, P * t : P * (t + 1)].bitcast(E4M3X4),
+                lhsT_scale=f_planes[n, g][:, P * t : P * (t + 1)],
+                rhs=wb_sb[:, n, :].bitcast(E2M1X4),
+                rhs_scale=wb_pl[:, n, :],
+                start=(n == 0),
+                stop=(n == CHUNKS - 1),
+            )
 
-        def o_store(n):
-            g, t = divmod(n, SLOTS)
-            o_sb = work.tile([P, H], F32, name="o_sb", bufs=5)
-            nc.vector.tensor_tensor(out=o_sb[:], in0=read_bank(("o", n))[:], in1=rate_sb[:], op=ALU.mult)
+        def o_passes(g, t, lo, hi):
+            for n in range(lo, hi):
+                o_pass(g, t, n)
+
+        def o_store(g, t, pieces=1):
+            bank = read_bank(("o", g, t))
+            width = H // pieces
+            for k in range(pieces):
+                cols = slice(width * k, width * (k + 1))
+                o_sb = work.tile([P, width], F32, name="o_sb", bufs=6)
+                nc.vector.tensor_tensor(out=o_sb[:], in0=bank[:, cols], in1=rate_sb[:, cols], op=ALU.mult)
+                nc.sync.dma_start(out=out_view[g][:, t, cols], in_=o_sb[:])
+
+        def o_store_aside(g, t):
+            o_raw = work.tile([P, H], F32, name="o_raw", bufs=2)
+            nc.scalar.copy(out=o_raw[:], in_=read_bank(("o", g, t))[:])
+            o_sb = work.tile([P, H], F32, name="o_sb", bufs=6)
+            nc.gpsimd.tensor_tensor(out=o_sb[:], in0=o_raw[:], in1=rate_sb[:], op=ALU.mult)
             nc.sync.dma_start(out=out_view[g][:, t, :], in_=o_sb[:])
 
-        def o_quarter(n, q):
-            g, t = divmod(n, SLOTS)
-            bank = take_bank(("q", q))
-            for chunk in range(CHUNKS):
-                h = GROUPS * chunk + g
-                nc.tensor.matmul_mx(
-                    out=bank[:, :P],
-                    lhsT=f_codes[h][:, P * t : P * (t + 1)].bitcast(E4M3X4),
-                    lhsT_scale=f_planes[h][:, P * t : P * (t + 1)],
-                    rhs=wb_sb[:, chunk, 2 * P * q : 2 * P * (q + 1)].bitcast(E2M1X4),
-                    rhs_scale=wb_pl[:, chunk, P * q : P * (q + 1)],
-                    start=(chunk == 0),
-                    stop=(chunk == CHUNKS - 1),
-                )
+        nc.vector.memset(pt_plraw[:].rearrange("p g n -> p (g n)").bitcast(I32), 0)
+        nc.vector.memset(wd_pl_first[:].bitcast(I32), 0)
+        nc.vector.memset(wd_pl_rest[:].bitcast(I32), 0)
+        nc.vector.memset(wb_pl[:].rearrange("p g n -> p (g n)").bitcast(I32), 0)
+        make_identity(nc, ident[:])
 
-        def o_store_quarter(n, q):
-            g, t = divmod(n, SLOTS)
-            cols = slice(P * q, P * (q + 1))
-            o_part = work.tile([P, P], F32, name="o_part", bufs=4)
-            nc.vector.tensor_tensor(out=o_part[:], in0=read_bank(("q", q))[:, :P], in1=rate_sb[:, cols], op=ALU.mult)
-            nc.sync.dma_start(out=out_view[g][:, t, cols], in_=o_part[:])
 
-        def o_store_in_halves(n):
-            g, t = divmod(n, SLOTS)
-            bank = read_bank(("o", n))
-            for k in range(2):
-                cols = slice(H // 2 * k, H // 2 * (k + 1))
-                o_half = work.tile([P, H // 2], F32, name="o_half", bufs=2)
-                nc.vector.tensor_tensor(out=o_half[:], in0=bank[:, cols], in1=rate_sb[:, cols], op=ALU.mult)
-                nc.sync.dma_start(out=out_view[g][:, t, cols], in_=o_half[:])
+        load_c(0)
+        load_c(1)
+        load_pt_scales()
+        load_c(2)
+        load_c(3)
+        load_wd(wd_first, 0, N)
+        load_wd_scales(wd_pl_first, 0, N)
+        load_x_half(0, 0)
+        load_x_half(0, 1)
+        load_x_half(1, 0)
+        load_x_half(1, 1)
+        load_pt(0)
+        load_wd(wd_second, N, 2 * N)
+        load_wd_scales(wd_pl_rest, N, D)
+        load_x(1, 0)
+        load_pt(1)
+        load_wd(wd_rest, 2 * N, D)
+        load_x(1, 1)
+        load_a()
+        for n in range(2, CHUNKS):
+            for g in range(GROUPS):
+                load_x(n, g)
+        load_wb()
 
-        turn_c(0, 1)
-        turn_c(1, 1)
-        turn_c(2, 2)
+        turn_c(0, False)
+        turn_c(1, False)
+        group_c(0)
         sort_pt_scales(0, 0)
-        quantize_c(0, 1)
-        quantize_c(1, 1)
+        sort_c(2)
+        turn_c(2)
+        quantize_c(0)
+        sort_c(3)
+        turn_c(3)
+        group_c(1)
+        group_c(2)
+        group_c(3)
         sort_pt_scales(1, 0)
-        turn_c(4, 2)
-        turn_c(6, 2)
-        quantize_c(2, 2)
-        sort_pt(0, 0)
-        sort_pt(1, 0)
-        quantize_c(4, 2)
-        r_matmul(0, 0)
-        r_matmul(0, 1)
-        r_matmul(0, 2)
-        r_matmul(0, 3)
-        quantize_c(6, 2)
-        r_matmul(1, 0)
-        r_matmul(1, 1)
-        r_matmul(1, 2)
-        r_matmul(1, 3)
-        r_copy(0, 0)
-        e_subtract(0, 1)
-        e_subtract_gpsimd(0, 0)
-        e_subtract(0, 2)
-        e_subtract(0, 3)
-        e_group_scalar(0, 256)
-        e_group_gpsimd(0, 256)
-        e_subtract(1, 0)
-        e_subtract(1, 1)
-        e_subtract(1, 2)
-        e_subtract(1, 3)
-        r_matmul(3, 0)
-        r_matmul(4, 0)
-        r_matmul(2, 0)
-        r_matmul(2, 1)
-        r_copy(3, 0)
-        r_copy(4, 0)
-        r_matmul(2, 2)
-        r_matmul(2, 3)
-        r_matmul(4, 1)
-        e_quantize(0)
-        e_group_scalar(1, 384)
-        g_pass(0, 0, 0)
-        g_pass(0, 1, 0)
-        r_matmul(5, 0)
-        sort_pt(0, 1)
-        sort_pt(1, 1)
-        e_group_vector(1, 384)
-        r_copy(4, 1)
-        r_matmul(5, 1)
-        r_copy(2, 0)
+        quantize_c(1)
         sort_pt_scales(0, 1)
+        quantize_c(2)
         sort_pt_scales(1, 1)
-        r_copy(5, 0)
-        r_copy(5, 1)
-        e_quantize(1)
-        e_subtract_gpsimd(2, 0)
-        g_pass(0, 0, 1)
-        g_pass(0, 1, 1)
-        r_matmul(3, 1)
-        g_pass(0, 2, 0)
-        g_pass(0, 2, 1)
-        e_subtract(2, 1)
-        r_matmul(3, 2)
-        e_subtract(2, 2)
-        r_matmul(3, 3)
-        e_subtract(2, 3)
-        e_subtract_gpsimd(3, 0)
-        g_pass(0, 3, 0)
-        g_pass(0, 3, 1)
-        e_subtract(3, 1)
-        e_group_scalar(2)
-        g_pass(1, 0, 0)
-        g_pass(1, 0, 1)
-        e_subtract(3, 2)
-        e_subtract(3, 3)
-        e_subtract_gpsimd(4, 0)
-        f_add(0, 0)
-        g_pass(1, 1, 0)
-        g_pass(1, 1, 1)
-        f_add(0, 1)
-        e_subtract_gpsimd(4, 1)
-        g_pass(1, 2, 0)
-        g_pass(1, 2, 1)
-        f_add(0, 2)
-        e_group_scalar(3)
-        g_pass(1, 3, 0)
-        g_pass(1, 3, 1)
-        f_add(0, 3)
-        r_matmul(5, 2)
-        f_turn(0, 0)
-        f_turn(0, 1)
-        f_add(1, 0)
-        r_matmul(4, 2)
-        r_matmul(4, 3)
-        e_quantize(2)
-        f_group(0, 0)
-        r_matmul(6, 0)
-        f_add(1, 1)
-        g_pass(2, 0, 0)
-        r_copy(5, 2)
-        e_quantize(3)
-        e_subtract_gpsimd(5, 2)
-        r_copy(6, 0)
-        f_group(0, 1)
-        e_subtract(4, 2)
-        g_pass(2, 0, 1)
-        g_pass(2, 1, 0)
-        g_pass(2, 1, 1)
-        e_subtract(4, 3)
-        f_add(1, 2)
-        e_subtract_gpsimd(5, 0)
-        e_group_scalar(4)
-        r_matmul(5, 3)
-        f_add(1, 3)
-        g_pass(2, 2, 0)
-        g_pass(2, 2, 1)
-        r_matmul(6, 1)
-        e_subtract(5, 3)
-        e_subtract_gpsimd(5, 1)
-        g_pass(2, 3, 0)
-        g_pass(2, 3, 1)
-        g_pass(3, 0, 0)
-        g_pass(3, 0, 1)
-        f_add(2, 0)
-        r_copy(6, 1)
-        e_subtract_gpsimd(6, 0)
-        g_pass(3, 1, 0)
-        g_pass(3, 1, 1)
-        f_add(2, 1)
-        e_group_scalar(5)
-        g_pass(3, 2, 0)
-        g_pass(3, 2, 1)
-        f_add(2, 2)
-        e_subtract_gpsimd(6, 1)
-        g_pass(3, 3, 0)
-        g_pass(3, 3, 1)
-        f_add(2, 3)
-        r_matmul(7, 0)
-        f_add(3, 0)
-        f_turn(1, 0)
-        f_turn(1, 1)
-        f_turn(2, 0)
-        f_add(3, 1)
-        r_matmul(6, 2)
-        f_group(1, 0)
-        f_group(1, 1)
-        r_matmul(6, 3)
-        r_matmul(7, 1)
-        f_add(3, 2)
-        r_matmul(7, 2)
-        f_add(3, 3)
-        e_quantize(4)
-        g_pass(4, 0, 0)
-        r_copy(7, 0)
-        e_quantize(5)
-        e_subtract_gpsimd(7, 0)
-        f_group(2, 0)
-        r_copy(7, 1)
-        e_subtract(6, 2)
-        g_pass(4, 0, 1)
-        g_pass(4, 1, 0)
-        g_pass(4, 1, 1)
-        e_subtract_gpsimd(7, 1)
-        e_subtract(6, 3)
-        r_matmul(7, 3)
-        e_subtract(7, 2)
-        e_group_scalar(6)
-        g_pass(4, 2, 0)
-        g_pass(4, 2, 1)
-        e_subtract(7, 3)
-        g_pass(4, 3, 0)
-        g_pass(4, 3, 1)
-        f_add(4, 0)
-        e_group_gpsimd(7, 256)
-        g_pass(5, 0, 0)
-        g_pass(5, 0, 1)
-        e_group_scalar(7, 256)
-        f_add(4, 1)
-        f_turn(2, 1)
-        f_turn(3, 0)
-        f_turn(3, 1)
-        f_add(4, 2)
-        g_pass(5, 1, 0)
-        g_pass(5, 1, 1)
-        f_add(4, 3)
-        g_pass(5, 2, 0)
-        g_pass(5, 2, 1)
-        e_quantize(6)
-        f_group(2, 1)
-        f_group(3, 0)
-        f_group(3, 1)
-        e_quantize(7)
-        g_pass(5, 3, 0)
-        g_pass(5, 3, 1)
-        f_add(5, 0)
-        g_pass(6, 0, 0)
-        g_pass(6, 0, 1)
-        f_add(5, 1)
-        g_pass(6, 1, 0)
-        g_pass(6, 1, 1)
-        f_add(5, 2)
-        f_turn(4, 0)
-        f_turn(4, 1)
-        f_turn(5, 0)
-        f_add(5, 3)
-        g_pass(6, 2, 0)
-        g_pass(6, 2, 1)
-        f_group(4, 0)
-        f_group(4, 1)
-        f_group(5, 0)
-        f_quantize(0)
-        g_pass(6, 3, 0)
-        g_pass(6, 3, 1)
-        f_add(6, 0)
-        g_pass(7, 0, 0)
-        g_pass(7, 0, 1)
-        f_add(6, 1)
-        g_pass(7, 1, 0)
-        g_pass(7, 1, 1)
-        f_quantize(2)
-        f_add(6, 2)
-        g_pass(7, 2, 0)
-        g_pass(7, 2, 1)
-        f_add(6, 3)
-        g_pass(7, 3, 0)
-        g_pass(7, 3, 1)
-        o_passes([0], [0])
-        o_passes([0], [1])
-        f_add(7, 0)
-        f_turn(5, 1)
-        f_turn(6, 0)
-        f_turn(6, 1)
-        f_add(7, 1)
-        f_quantize(4)
-        f_add(7, 2)
-        f_add(7, 3)
-        f_group(6, 0)
-        f_group(6, 1)
-        f_group(5, 1)
-        o_passes([1], [0])
-        o_passes([1], [1])
-        o_passes([0], [2])
-        o_passes([1], [2])
-        o_passes([2], [0])
-        o_passes([2], [1])
-        o_passes([2], [2])
-        f_quantize(6)
-        f_quantize(1)
-        f_turn(7, 0)
-        f_turn(7, 1)
-        f_group(7, 0)
-        f_group(7, 1)
-        o_passes([0], [3])
-        o_passes([1], [3])
-        o_passes([2], [3])
-        o_passes([3], [0])
-        o_passes([3], [1])
-        o_passes([3], [2])
-        o_passes([3], [3])
-        f_quantize(3)
-        f_quantize(5)
-        o_store(0)
-        o_passes([4], [0])
-        o_passes([4], [1])
-        o_passes([4], [2])
-        o_store(1)
-        o_passes([5], [0])
-        o_passes([5], [1])
-        o_passes([5], [2])
-        f_quantize(7, 0, 2)
-        o_store(2)
-        o_passes([4], [3])
-        o_passes([5], [3])
-        f_quantize(7, 2, 4)
-        o_store(3)
-        o_passes([6], [0])
-        o_passes([6], [1])
-        o_passes([6], [2])
-        o_passes([6], [3])
-        o_store(4)
-        o_store(5)
-        o_passes([7], [0])
-        o_passes([7], [1])
-        o_passes([7], [2])
-        o_passes([7], [3])
-        o_store(6)
-        o_store_in_halves(7)
+        quantize_c(3)
+        for g in range(GROUPS):
+            for t in range(SLOTS):
+                r_matmul(0, g, t)
+        r_copy(0, 0, 0)
+        r_copy(0, 1, 0)
+        e_subtract_gpsimd(0, 0, 0)
+        e_subtract_gpsimd(0, 1, 0)
+        r_matmul(1, 0, 3)
+        for g in range(GROUPS):
+            for t in range(1, SLOTS):
+                e_subtract(0, g, t)
+                if g == 0 or t == 1:
+                    r_matmul(1, *[(1, 2), (0, 0), (0, 1), (0, 2)][3 * g + t - 1])
+        sort_pt_scalar(0, 0)
+        e_group_scalar(0, 0)
+        sort_pt(1, 0)
+        r_matmul(1, 1, 3)
+        r_matmul(1, 1, 0)
+        e_group_vector(0, 1, SHARE0)
+        e_group_scalar(0, 1, 0, SHARE0)
+        e_quantize(0, 0, 1)
+        e_quantize(0, 1, 2)
+        r_copy(1, 0, 3)
+        r_copy(1, 1, 2)
+        e_subtract_gpsimd(1, 0, 3)
+        e_subtract_gpsimd(1, 1, 2)
+        g_pass(0, 0, 0, 0)
+        e_subtract(1, 0, 0)
+        g_pass(0, 0, 0, 1)
+        r_matmul(1, 1, 1)
+        g_matmul(0, 0, 1)
+        e_subtract(1, 0, 1)
+        r_copy(1, 1, 3)
+        e_subtract(1, 0, 2)
+        e_subtract_gpsimd(1, 1, 3)
+        sort_pt_scalar(0, 1)
+        sort_pt_scalar(1, 1)
+        e_subtract(1, 1, 0)
+        e_subtract(1, 1, 1)
+        e_group_scalar(1, 0)
+        for n in range(CHUNKS - 1):
+            nxt = n + 1
+            after = nxt + 1 < CHUNKS
+            share = SHARE if after else SHARE_LAST
+            if n > 0:
+                e_subtract_gpsimd(nxt, 1, 2)
+                e_subtract_gpsimd(nxt, 1, 3)
+                e_subtract(nxt, 0, 0)
+                if after:
+                    r_copy(nxt + 1, 0, 2)
+                e_subtract(nxt, 0, 1)
+                g_matmul(n, 0, 0)
+                if after:
+                    r_copy(nxt + 1, 0, 3)
+                e_subtract(nxt, 1, 0)
+                g_matmul(n, 0, 1)
+                e_subtract(nxt, 1, 1)
+                e_group_scalar(nxt, 0)
+            e_group_gpsimd(nxt, 1, share)
+            if n == 1:
+                e_subtract_gpsimd(nxt + 1, 0, 2)
+                e_subtract_gpsimd(nxt + 1, 0, 3)
+            if n > 0:
+                e_group_scalar(nxt, 1, 0, share)
+            g_matmul(n, 0, 2)
+            f_add(n, 0, 0)
+            g_matmul(n, 0, 3)
+            f_add(n, 0, 1)
+            if n == 0:
+                r_matmul(2, 0, 2)
+                r_matmul(2, 0, 3)
+                r_copy(2, 0, 2)
+                r_copy(2, 0, 3)
+                e_subtract_gpsimd(2, 0, 2)
+                e_subtract_gpsimd(2, 0, 3)
+                e_group_scalar(nxt, 1, 0, share)
+            g_matmul(n, 1, 0)
+            f_add(n, 0, 2)
+            g_matmul(n, 1, 1)
+            f_add(n, 0, 3)
+            if not after:
+                break
+            r_matmul(nxt + 1, 1, 2)
+            g_matmul(n, 1, 2)
+            f_add(n, 1, 0)
+            r_matmul(nxt + 1, 1, 3)
+            r_copy(nxt + 1, 1, 2)
+            g_matmul(n, 1, 3)
+            f_add(n, 1, 1)
+            r_copy(nxt + 1, 1, 3)
+            if n > 0:
+                f_turn(n - 1, 1, 0)
+                f_turn(n - 1, 1, 1)
+            f_turn(n, 0, 0)
+            f_add(n, 1, 2)
+            f_turn(n, 0, 1)
+            f_add(n, 1, 3)
+            if n > 0:
+                f_group(n - 1, 1, 0)
+            r_matmul(nxt + 1, 0, 0)
+            if nxt + 2 < CHUNKS:
+                r_matmul(nxt + 2, 0, 2)
+            if n > 0:
+                f_group(n - 1, 1, 1)
+            r_matmul(nxt + 1, 0, 1)
+            f_group(n, 0, 0)
+            if nxt + 2 < CHUNKS:
+                r_matmul(nxt + 2, 0, 3)
+            f_group(n, 0, 1)
+            r_matmul(nxt + 1, 1, 0)
+            r_matmul(nxt + 1, 1, 1)
+            e_quantize(nxt)
+
+        last = CHUNKS - 1
+        g_matmul(2, 1, 2)
+        g_matmul(2, 1, 3)
+        f_quantize(0, 0, 0, EARLY)
+        f_quantize(1, 0, 0, EARLY)
+        e_quantize(last)
+        for g, n in ((1, 1), (0, 2)):
+            f_turn(n, g, 0)
+            f_turn(n, g, 1)
+        for g, n in ((1, 1), (0, 2)):
+            f_group(n, g, 0)
+            f_group(n, g, 1)
+        for t in range(EARLY):
+            o_passes(0, t, 0, 2)
+        for t in range(SLOTS):
+            f_add(2, 1, t)
+            g_matmul(last, 0, t)
+        last = CHUNKS - 1
+        f_quantize(2, 0)
+        for t in range(SLOTS):
+            f_add(last, 0, t)
+            g_matmul(last, 1, t)
+            if t < 2:
+                f_quantize(t, 0, EARLY, SLOTS)
+        f_add(last, 1, 0)
+        f_add(last, 1, 1)
+        f_turn(last - 1, 1, 0)
+        f_turn(last - 1, 1, 1)
+        f_turn(last, 0, 0)
+        f_turn(last, 0, 1)
+        f_add(last, 1, 2)
+        f_add(last, 1, 3)
+        f_group(last, 0, 0)
+        f_group(last, 0, 1)
+        f_group(last - 1, 1, 0)
+        f_group(last - 1, 1, 1)
+        for t in range(EARLY):
+            o_pass(0, t, 2)
+        for t in range(EARLY, SLOTS):
+            o_passes(0, t, 0, last)
+        f_quantize(0, 1)
+        f_quantize(last, 0)
+        f_turn(last, 1, 0)
+        f_turn(last, 1, 1)
+        f_group(last, 1, 0)
+        f_group(last, 1, 1)
+        f_quantize(1, 1)
+        f_quantize(2, 1)
+        for t in range(SLOTS):
+            o_pass(0, t, last)
+        o_store(0, 0)
+        o_passes(1, 0, 0, last)
+        f_quantize(last, 1, 0, 2)
+        o_store(0, 1)
+        o_passes(1, 1, 0, last)
+        f_quantize(last, 1, 2, 4)
+        o_pass(1, 0, last)
+        o_pass(1, 1, last)
+        o_store(0, 2)
+        o_store(0, 3)
+        o_passes(1, 2, 0, CHUNKS)
+        o_store(1, 0)
+        o_store(1, 1)
+        o_passes(1, 3, 0, CHUNKS)
+        o_store(1, 2)
+        o_store(1, 3, 2)

@@ -22,7 +22,8 @@ SLOTS = 4
 GROUPS = M // (P * SLOTS)
 CHUNKS = D // N
 SHARE = 320
-SHARE0 = 128
+SHARE0 = 192
+SHARE_A = 288
 EARLY = 2
 SHARE_LAST = 224
 
@@ -208,7 +209,7 @@ def tile_tied_autoencoder_code_step_t2_kernel(
             )
 
         def r_copy(n, g, t):
-            r_aside[n, g, t] = work.tile([P, N], F32, name="r_aside", bufs=4)
+            r_aside[n, g, t] = work.tile([P, N], F32, name="r_aside", bufs=5)
             nc.scalar.copy(out=as_stored(r_aside[n, g, t][:]), in_=into_stored(read_bank(("r", n, g, t))[:]))
 
         def e_subtract_gpsimd(n, g, t):
@@ -334,6 +335,26 @@ def tile_tied_autoencoder_code_step_t2_kernel(
                 nc.vector.tensor_tensor(out=o_sb[:], in0=bank[:, cols], in1=rate_sb[:, cols], op=ALU.mult)
                 nc.sync.dma_start(out=out_view[g][:, t, cols], in_=o_sb[:])
 
+        def o_half(g, t, k):
+            cols = slice(H // 2 * k, H // 2 * (k + 1))
+            bank = take_bank(("h", k))
+            for n in range(CHUNKS):
+                nc.tensor.matmul_mx(
+                    out=bank[:, : H // 2],
+                    lhsT=f_codes[n, g][:, P * t : P * (t + 1)].bitcast(E4M3X4),
+                    lhsT_scale=f_planes[n, g][:, P * t : P * (t + 1)],
+                    rhs=wb_sb[:, n, H * k : H * (k + 1)].bitcast(E2M1X4),
+                    rhs_scale=wb_pl[:, n, cols],
+                    start=(n == 0),
+                    stop=(n == CHUNKS - 1),
+                )
+
+        def o_store_half(g, t, k):
+            cols = slice(H // 2 * k, H // 2 * (k + 1))
+            o_sb = work.tile([P, H // 2], F32, name="o_sb", bufs=6)
+            nc.vector.tensor_tensor(out=o_sb[:], in0=read_bank(("h", k))[:, : H // 2], in1=rate_sb[:, cols], op=ALU.mult)
+            nc.sync.dma_start(out=out_view[g][:, t, cols], in_=o_sb[:])
+
         def o_store_aside(g, t):
             o_raw = work.tile([P, H], F32, name="o_raw", bufs=2)
             nc.scalar.copy(out=o_raw[:], in_=read_bank(("o", g, t))[:])
@@ -357,13 +378,13 @@ def tile_tied_autoencoder_code_step_t2_kernel(
         load_wd_scales(wd_pl_first, 0, N)
         load_x_half(0, 0)
         load_x_half(0, 1)
+        load_pt(0)
+        load_pt(1)
         load_x_half(1, 0)
         load_x_half(1, 1)
-        load_pt(0)
         load_wd(wd_second, N, 2 * N)
         load_wd_scales(wd_pl_rest, N, D)
         load_x(1, 0)
-        load_pt(1)
         load_wd(wd_rest, 2 * N, D)
         load_x(1, 1)
         load_a()
@@ -394,39 +415,41 @@ def tile_tied_autoencoder_code_step_t2_kernel(
             for t in range(SLOTS):
                 r_matmul(0, g, t)
         r_copy(0, 0, 0)
-        r_copy(0, 1, 0)
         e_subtract_gpsimd(0, 0, 0)
-        e_subtract_gpsimd(0, 1, 0)
-        r_matmul(1, 0, 3)
-        for g in range(GROUPS):
-            for t in range(1, SLOTS):
-                e_subtract(0, g, t)
-                if g == 0 or t == 1:
-                    r_matmul(1, *[(1, 2), (0, 0), (0, 1), (0, 2)][3 * g + t - 1])
+        r_matmul(1, 1, 2)
+        for t in range(1, SLOTS):
+            e_subtract(0, 0, t)
+            r_matmul(1, 0, t)
         sort_pt_scalar(0, 0)
-        e_group_scalar(0, 0)
-        sort_pt(1, 0)
+        sort_pt_scalar(1, 0)
+        sort_pt_scalar(0, 1)
+        e_group_scalar(0, 0, 0, SHARE_A)
+        e_group_gpsimd(0, 0, SHARE_A)
+        for t in range(SLOTS):
+            e_subtract(0, 1, t)
+        r_matmul(1, 0, 0)
         r_matmul(1, 1, 3)
         r_matmul(1, 1, 0)
-        e_group_vector(0, 1, SHARE0)
-        e_group_scalar(0, 1, 0, SHARE0)
+        sort_pt_scalar(1, 1)
+        r_copy(1, 1, 2)
         e_quantize(0, 0, 1)
+        e_group_scalar(0, 1, 0, SHARE0)
+        e_group_vector(0, 1, SHARE0)
+        g_pass(0, 0, 0, 0)
+        g_pass(0, 0, 1, 0)
         e_quantize(0, 1, 2)
         r_copy(1, 0, 3)
-        r_copy(1, 1, 2)
+        r_copy(1, 1, 3)
         e_subtract_gpsimd(1, 0, 3)
         e_subtract_gpsimd(1, 1, 2)
-        g_pass(0, 0, 0, 0)
-        e_subtract(1, 0, 0)
-        g_pass(0, 0, 0, 1)
-        r_matmul(1, 1, 1)
-        g_matmul(0, 0, 1)
-        e_subtract(1, 0, 1)
-        r_copy(1, 1, 3)
-        e_subtract(1, 0, 2)
         e_subtract_gpsimd(1, 1, 3)
-        sort_pt_scalar(0, 1)
-        sort_pt_scalar(1, 1)
+        r_matmul(1, 1, 1)
+        g_pass(0, 0, 0, 1)
+        g_pass(0, 0, 1, 1)
+        for t in range(3):
+            e_subtract(1, 0, t)
+        r_matmul(2, 0, 2)
+        r_copy(2, 0, 2)
         e_subtract(1, 1, 0)
         e_subtract(1, 1, 1)
         e_group_scalar(1, 0)
@@ -435,37 +458,28 @@ def tile_tied_autoencoder_code_step_t2_kernel(
             after = nxt + 1 < CHUNKS
             share = SHARE if after else SHARE_LAST
             if n > 0:
+                r_copy(nxt, 1, 3)
+                e_subtract_gpsimd(nxt, 0, 3)
                 e_subtract_gpsimd(nxt, 1, 2)
                 e_subtract_gpsimd(nxt, 1, 3)
                 e_subtract(nxt, 0, 0)
                 if after:
                     r_copy(nxt + 1, 0, 2)
                 e_subtract(nxt, 0, 1)
+                r_matmul(nxt, 1, 1)
                 g_matmul(n, 0, 0)
-                if after:
-                    r_copy(nxt + 1, 0, 3)
                 e_subtract(nxt, 1, 0)
                 g_matmul(n, 0, 1)
                 e_subtract(nxt, 1, 1)
                 e_group_scalar(nxt, 0)
             e_group_gpsimd(nxt, 1, share)
-            if n == 1:
+            if after:
                 e_subtract_gpsimd(nxt + 1, 0, 2)
-                e_subtract_gpsimd(nxt + 1, 0, 3)
-            if n > 0:
-                e_group_scalar(nxt, 1, 0, share)
+            e_group_scalar(nxt, 1, 0, share)
             g_matmul(n, 0, 2)
             f_add(n, 0, 0)
             g_matmul(n, 0, 3)
             f_add(n, 0, 1)
-            if n == 0:
-                r_matmul(2, 0, 2)
-                r_matmul(2, 0, 3)
-                r_copy(2, 0, 2)
-                r_copy(2, 0, 3)
-                e_subtract_gpsimd(2, 0, 2)
-                e_subtract_gpsimd(2, 0, 3)
-                e_group_scalar(nxt, 1, 0, share)
             g_matmul(n, 1, 0)
             f_add(n, 0, 2)
             g_matmul(n, 1, 1)
@@ -475,49 +489,50 @@ def tile_tied_autoencoder_code_step_t2_kernel(
             r_matmul(nxt + 1, 1, 2)
             g_matmul(n, 1, 2)
             f_add(n, 1, 0)
-            r_matmul(nxt + 1, 1, 3)
+            r_matmul(nxt + 1, 0, 3)
             r_copy(nxt + 1, 1, 2)
             g_matmul(n, 1, 3)
             f_add(n, 1, 1)
-            r_copy(nxt + 1, 1, 3)
+            r_copy(nxt + 1, 0, 3)
             if n > 0:
                 f_turn(n - 1, 1, 0)
                 f_turn(n - 1, 1, 1)
             f_turn(n, 0, 0)
             f_add(n, 1, 2)
             f_turn(n, 0, 1)
-            f_add(n, 1, 3)
+            e_quantize(nxt)
             if n > 0:
                 f_group(n - 1, 1, 0)
             r_matmul(nxt + 1, 0, 0)
-            if nxt + 2 < CHUNKS:
-                r_matmul(nxt + 2, 0, 2)
+            r_matmul(nxt + 1, 1, 3)
             if n > 0:
                 f_group(n - 1, 1, 1)
             r_matmul(nxt + 1, 0, 1)
             f_group(n, 0, 0)
             if nxt + 2 < CHUNKS:
-                r_matmul(nxt + 2, 0, 3)
+                r_matmul(nxt + 2, 0, 2)
             f_group(n, 0, 1)
             r_matmul(nxt + 1, 1, 0)
-            r_matmul(nxt + 1, 1, 1)
-            e_quantize(nxt)
+            f_add(n, 1, 3)
 
         last = CHUNKS - 1
         g_matmul(2, 1, 2)
         g_matmul(2, 1, 3)
+        f_add(2, 1, 0)
         f_quantize(0, 0, 0, EARLY)
         f_quantize(1, 0, 0, EARLY)
         e_quantize(last)
         for g, n in ((1, 1), (0, 2)):
             f_turn(n, g, 0)
             f_turn(n, g, 1)
+        o_passes(0, 0, 0, 2)
         for g, n in ((1, 1), (0, 2)):
             f_group(n, g, 0)
             f_group(n, g, 1)
-        for t in range(EARLY):
+        for t in range(1, EARLY):
             o_passes(0, t, 0, 2)
-        for t in range(SLOTS):
+        g_matmul(last, 0, 0)
+        for t in range(1, SLOTS):
             f_add(2, 1, t)
             g_matmul(last, 0, t)
         last = CHUNKS - 1
@@ -566,6 +581,8 @@ def tile_tied_autoencoder_code_step_t2_kernel(
         o_passes(1, 2, 0, CHUNKS)
         o_store(1, 0)
         o_store(1, 1)
-        o_passes(1, 3, 0, CHUNKS)
+        o_half(1, 3, 0)
+        o_half(1, 3, 1)
         o_store(1, 2)
-        o_store(1, 3, 2)
+        o_store_half(1, 3, 0)
+        o_store_half(1, 3, 1)

@@ -25,6 +25,7 @@ SHARE = 320
 SHARE0 = 192
 SHARE_A = 288
 EARLY = 2
+SHARE_1 = 416
 SHARE_LAST = 224
 
 MOVING_CODES, MOVING_SCALES, STILL_CODES, STILL_SCALES = 0, 64, 128, 192
@@ -379,11 +380,11 @@ def tile_tied_autoencoder_code_step_t2_kernel(
         load_x_half(0, 0)
         load_x_half(0, 1)
         load_pt(0)
-        load_pt(1)
         load_x_half(1, 0)
         load_x_half(1, 1)
         load_wd(wd_second, N, 2 * N)
         load_wd_scales(wd_pl_rest, N, D)
+        load_pt(1)
         load_x(1, 0)
         load_wd(wd_rest, 2 * N, D)
         load_x(1, 1)
@@ -422,7 +423,6 @@ def tile_tied_autoencoder_code_step_t2_kernel(
             r_matmul(1, 0, t)
         sort_pt_scalar(0, 0)
         sort_pt_scalar(1, 0)
-        sort_pt_scalar(0, 1)
         e_group_scalar(0, 0, 0, SHARE_A)
         e_group_gpsimd(0, 0, SHARE_A)
         for t in range(SLOTS):
@@ -430,7 +430,6 @@ def tile_tied_autoencoder_code_step_t2_kernel(
         r_matmul(1, 0, 0)
         r_matmul(1, 1, 3)
         r_matmul(1, 1, 0)
-        sort_pt_scalar(1, 1)
         r_copy(1, 1, 2)
         e_quantize(0, 0, 1)
         e_group_scalar(0, 1, 0, SHARE0)
@@ -438,48 +437,58 @@ def tile_tied_autoencoder_code_step_t2_kernel(
         g_pass(0, 0, 0, 0)
         g_pass(0, 0, 1, 0)
         e_quantize(0, 1, 2)
+        sort_pt_scalar(0, 1)
         r_copy(1, 0, 3)
         r_copy(1, 1, 3)
+        sort_pt_scalar(1, 1)
         e_subtract_gpsimd(1, 0, 3)
         e_subtract_gpsimd(1, 1, 2)
         e_subtract_gpsimd(1, 1, 3)
-        r_matmul(1, 1, 1)
         g_pass(0, 0, 0, 1)
         g_pass(0, 0, 1, 1)
+        r_matmul(1, 1, 1)
         for t in range(3):
             e_subtract(1, 0, t)
         r_matmul(2, 0, 2)
+        r_matmul(2, 0, 3)
         r_copy(2, 0, 2)
+        r_copy(2, 0, 3)
         e_subtract(1, 1, 0)
         e_subtract(1, 1, 1)
         e_group_scalar(1, 0)
         for n in range(CHUNKS - 1):
             nxt = n + 1
             after = nxt + 1 < CHUNKS
-            share = SHARE if after else SHARE_LAST
+            share = [SHARE_1, SHARE, SHARE_LAST][n]
             if n > 0:
-                r_copy(nxt, 1, 3)
-                e_subtract_gpsimd(nxt, 0, 3)
                 e_subtract_gpsimd(nxt, 1, 2)
                 e_subtract_gpsimd(nxt, 1, 3)
                 e_subtract(nxt, 0, 0)
                 if after:
                     r_copy(nxt + 1, 0, 2)
                 e_subtract(nxt, 0, 1)
-                r_matmul(nxt, 1, 1)
                 g_matmul(n, 0, 0)
+                if after:
+                    r_copy(nxt + 1, 0, 3)
                 e_subtract(nxt, 1, 0)
                 g_matmul(n, 0, 1)
                 e_subtract(nxt, 1, 1)
                 e_group_scalar(nxt, 0)
-            e_group_gpsimd(nxt, 1, share)
-            if after:
+            if share < N:
+                e_group_gpsimd(nxt, 1, share)
+            if n == 1:
                 e_subtract_gpsimd(nxt + 1, 0, 2)
-            e_group_scalar(nxt, 1, 0, share)
+                e_subtract_gpsimd(nxt + 1, 0, 3)
+            if n > 0:
+                e_group_scalar(nxt, 1, 0, share)
             g_matmul(n, 0, 2)
             f_add(n, 0, 0)
             g_matmul(n, 0, 3)
             f_add(n, 0, 1)
+            if n == 0:
+                e_subtract_gpsimd(2, 0, 2)
+                e_subtract_gpsimd(2, 0, 3)
+                e_group_scalar(nxt, 1, 0, share)
             g_matmul(n, 1, 0)
             f_add(n, 0, 2)
             g_matmul(n, 1, 1)
@@ -489,31 +498,36 @@ def tile_tied_autoencoder_code_step_t2_kernel(
             r_matmul(nxt + 1, 1, 2)
             g_matmul(n, 1, 2)
             f_add(n, 1, 0)
-            r_matmul(nxt + 1, 0, 3)
-            r_copy(nxt + 1, 1, 2)
+            r_matmul(nxt + 1, 1, 3)
             g_matmul(n, 1, 3)
             f_add(n, 1, 1)
-            r_copy(nxt + 1, 0, 3)
             if n > 0:
                 f_turn(n - 1, 1, 0)
                 f_turn(n - 1, 1, 1)
             f_turn(n, 0, 0)
+            if n > 0:
+                r_copy(nxt + 1, 1, 2)
             f_add(n, 1, 2)
             f_turn(n, 0, 1)
-            e_quantize(nxt)
+            if n == 0:
+                r_copy(nxt + 1, 1, 2)
+            f_add(n, 1, 3)
+            r_copy(nxt + 1, 1, 3)
             if n > 0:
                 f_group(n - 1, 1, 0)
             r_matmul(nxt + 1, 0, 0)
-            r_matmul(nxt + 1, 1, 3)
+            if nxt + 2 < CHUNKS:
+                r_matmul(nxt + 2, 0, 2)
             if n > 0:
                 f_group(n - 1, 1, 1)
             r_matmul(nxt + 1, 0, 1)
             f_group(n, 0, 0)
             if nxt + 2 < CHUNKS:
-                r_matmul(nxt + 2, 0, 2)
+                r_matmul(nxt + 2, 0, 3)
             f_group(n, 0, 1)
             r_matmul(nxt + 1, 1, 0)
-            f_add(n, 1, 3)
+            r_matmul(nxt + 1, 1, 1)
+            e_quantize(nxt)
 
         last = CHUNKS - 1
         g_matmul(2, 1, 2)
@@ -544,40 +558,38 @@ def tile_tied_autoencoder_code_step_t2_kernel(
                 f_quantize(t, 0, EARLY, SLOTS)
         f_add(last, 1, 0)
         f_add(last, 1, 1)
-        f_turn(last - 1, 1, 0)
-        f_turn(last - 1, 1, 1)
-        f_turn(last, 0, 0)
-        f_turn(last, 0, 1)
-        f_add(last, 1, 2)
-        f_add(last, 1, 3)
-        f_group(last, 0, 0)
-        f_group(last, 0, 1)
-        f_group(last - 1, 1, 0)
-        f_group(last - 1, 1, 1)
         for t in range(EARLY):
             o_pass(0, t, 2)
+        for n, g in ((last, 0), (last - 1, 1)):
+            f_turn(n, g, 0)
+            f_turn(n, g, 1)
+        f_add(last, 1, 2)
+        f_add(last, 1, 3)
         for t in range(EARLY, SLOTS):
             o_passes(0, t, 0, last)
+        for n, g in ((last, 0), (last - 1, 1)):
+            f_group(n, g, 0)
+            f_group(n, g, 1)
         f_quantize(0, 1)
         f_quantize(last, 0)
+        f_quantize(1, 1)
+        for t in range(SLOTS):
+            o_pass(0, t, last)
         f_turn(last, 1, 0)
         f_turn(last, 1, 1)
         f_group(last, 1, 0)
         f_group(last, 1, 1)
-        f_quantize(1, 1)
         f_quantize(2, 1)
-        for t in range(SLOTS):
-            o_pass(0, t, last)
         o_store(0, 0)
-        o_passes(1, 0, 0, last)
-        f_quantize(last, 1, 0, 2)
         o_store(0, 1)
+        o_passes(1, 0, 0, last)
         o_passes(1, 1, 0, last)
+        o_store(0, 2)
+        f_quantize(last, 1, 0, 2)
+        o_store(0, 3)
         f_quantize(last, 1, 2, 4)
         o_pass(1, 0, last)
         o_pass(1, 1, last)
-        o_store(0, 2)
-        o_store(0, 3)
         o_passes(1, 2, 0, CHUNKS)
         o_store(1, 0)
         o_store(1, 1)

@@ -15,6 +15,7 @@ U8 = mybir.dt.uint8
 E4M3X4 = mybir.dt.float8_e4m3fn_x4
 E2M1X4 = mybir.dt.float4_e2m1fn_x4
 ALU = mybir.AluOpType
+ACT = mybir.ActivationFunctionType
 
 P = 128
 N = 512
@@ -68,6 +69,7 @@ def tile_tied_autoencoder_code_step_t2_kernel(
         wb_sb = placed(keep, "wb_sb", CHUNKS * 2 * H, U8, 1, MOVING_CODES).rearrange("p (g w) -> p g w", g=CHUNKS)
         wb_pl = placed(keep, "wb_pl", CHUNKS * H, U8, 1, MOVING_SCALES).rearrange("p (g w) -> p g w", g=CHUNKS)
         a_sb = keep.tile([P, GROUPS, SLOTS], BF16, name="a_sb")
+        a_f32 = keep.tile([P, GROUPS, SLOTS], F32, name="a_f32")
         rate_sb = keep.tile([P, H], BF16, name="rate_sb")
         f_codes = {(n, g): placed(keep, "f_codes%d_%d" % (n, g), N, U32, 4, STILL_CODES) for n in range(CHUNKS) for g in range(2)}
         f_planes = {(n, g): placed(keep, "f_planes%d_%d" % (n, g), N, U8, 1, STILL_SCALES) for n in range(CHUNKS) for g in range(2)}
@@ -286,6 +288,22 @@ def tile_tied_autoencoder_code_step_t2_kernel(
                 op1=ALU.add,
             )
 
+        g_aside = {}
+
+        def e_scale(n, g, t):
+            nc.scalar.activation(
+                out=e32[n, g][:, t, :], in_=e32[n, g][:, t, :], func=ACT.Copy, scale=a_f32[:, g, t : t + 1]
+            )
+
+        def g_copy(n, g, t):
+            g_aside[n, g, t] = work.tile([P, N], F32, name="r_aside", bufs=5)
+            nc.scalar.copy(out=g_aside[n, g, t][:], in_=read_bank(("g", n, g, t))[:])
+
+        def f_add_gpsimd(n, g, t):
+            if (n, g) not in f_sb:
+                f_sb[n, g] = work.tile([P, SLOTS, N], BF16, name="f_sb", bufs=3)
+            nc.gpsimd.tensor_tensor(out=f_sb[n, g][:, t, :], in0=e32[n, g][:, t, :], in1=g_aside[n, g, t][:], op=ALU.add)
+
         def f_turn(n, g, pair):
             turned = take_bank(("t", n, g, pair))
             for i in range(2):
@@ -356,11 +374,15 @@ def tile_tied_autoencoder_code_step_t2_kernel(
             nc.vector.tensor_tensor(out=o_sb[:], in0=read_bank(("h", k))[:, : H // 2], in1=rate_sb[:, cols], op=ALU.mult)
             nc.sync.dma_start(out=out_view[g][:, t, cols], in_=o_sb[:])
 
-        def o_store_aside(g, t):
-            o_raw = work.tile([P, H], F32, name="o_raw", bufs=2)
-            nc.scalar.copy(out=o_raw[:], in_=read_bank(("o", g, t))[:])
+        o_raw = {}
+
+        def o_copy(g, t):
+            o_raw[g, t] = work.tile([P, H], F32, name="r_aside", bufs=5)
+            nc.scalar.copy(out=o_raw[g, t][:], in_=read_bank(("o", g, t))[:])
+
+        def o_store_gpsimd(g, t):
             o_sb = work.tile([P, H], F32, name="o_sb", bufs=6)
-            nc.gpsimd.tensor_tensor(out=o_sb[:], in0=o_raw[:], in1=rate_sb[:], op=ALU.mult)
+            nc.gpsimd.tensor_tensor(out=o_sb[:], in0=o_raw[g, t][:], in1=rate_sb[:], op=ALU.mult)
             nc.sync.dma_start(out=out_view[g][:, t, :], in_=o_sb[:])
 
         nc.vector.memset(pt_plraw[:].rearrange("p g n -> p (g n)").bitcast(I32), 0)
@@ -474,10 +496,10 @@ def tile_tied_autoencoder_code_step_t2_kernel(
                 g_matmul(n, 0, 1)
                 e_subtract(nxt, 1, 1)
                 e_group_scalar(nxt, 0)
-            if share < N:
-                e_group_gpsimd(nxt, 1, share)
-            if n == 1:
+            if after:
                 e_subtract_gpsimd(nxt + 1, 0, 2)
+            e_group_gpsimd(nxt, 1, share)
+            if after:
                 e_subtract_gpsimd(nxt + 1, 0, 3)
             if n > 0:
                 e_group_scalar(nxt, 1, 0, share)
@@ -486,8 +508,6 @@ def tile_tied_autoencoder_code_step_t2_kernel(
             g_matmul(n, 0, 3)
             f_add(n, 0, 1)
             if n == 0:
-                e_subtract_gpsimd(2, 0, 2)
-                e_subtract_gpsimd(2, 0, 3)
                 e_group_scalar(nxt, 1, 0, share)
             g_matmul(n, 1, 0)
             f_add(n, 0, 2)
@@ -536,6 +556,8 @@ def tile_tied_autoencoder_code_step_t2_kernel(
         f_quantize(0, 0, 0, EARLY)
         f_quantize(1, 0, 0, EARLY)
         e_quantize(last)
+        nc.scalar.copy(out=a_f32[:], in_=a_sb[:])
+        e_scale(2, 1, 3)
         for g, n in ((1, 1), (0, 2)):
             f_turn(n, g, 0)
             f_turn(n, g, 1)
@@ -546,52 +568,60 @@ def tile_tied_autoencoder_code_step_t2_kernel(
         for t in range(1, EARLY):
             o_passes(0, t, 0, 2)
         g_matmul(last, 0, 0)
-        for t in range(1, SLOTS):
-            f_add(2, 1, t)
-            g_matmul(last, 0, t)
-        last = CHUNKS - 1
-        f_quantize(2, 0)
-        for t in range(SLOTS):
-            f_add(last, 0, t)
-            g_matmul(last, 1, t)
-            if t < 2:
-                f_quantize(t, 0, EARLY, SLOTS)
-        f_add(last, 1, 0)
+        f_add(2, 1, 1)
+        g_copy(2, 1, 3)
+        g_matmul(last, 0, 1)
+        f_add(2, 1, 2)
+        f_quantize(2, 0, 0, EARLY)
+        f_add_gpsimd(2, 1, 3)
+        e_scale(last, 0, 1)
+        g_matmul(last, 0, 2)
+        f_add(last, 0, 0)
+        g_copy(last, 0, 1)
+        f_add_gpsimd(last, 0, 1)
+        g_matmul(last, 0, 3)
+        e_scale(last, 1, 0)
+        g_matmul(last, 1, 0)
+        f_add(last, 0, 2)
+        g_matmul(last, 1, 1)
+        f_add(last, 0, 3)
+        g_copy(last, 1, 0)
+        f_add_gpsimd(last, 1, 0)
+        g_matmul(last, 1, 2)
+        g_matmul(last, 1, 3)
         f_add(last, 1, 1)
+        f_turn(last, 0, 0)
+        f_turn(last, 0, 1)
         for t in range(EARLY):
             o_pass(0, t, 2)
-        for n, g in ((last, 0), (last - 1, 1)):
-            f_turn(n, g, 0)
-            f_turn(n, g, 1)
         f_add(last, 1, 2)
         f_add(last, 1, 3)
-        for t in range(EARLY, SLOTS):
-            o_passes(0, t, 0, last)
-        for n, g in ((last, 0), (last - 1, 1)):
-            f_group(n, g, 0)
-            f_group(n, g, 1)
-        f_quantize(0, 1)
+        f_group(last, 0, 0)
+        f_group(last, 0, 1)
+        for n in (last - 1, last):
+            f_turn(n, 1, 0)
+            f_turn(n, 1, 1)
+        for n in (last - 1, last):
+            f_group(n, 1, 0)
+            f_group(n, 1, 1)
+        for n in range(last):
+            f_quantize(n, 0, EARLY, SLOTS)
         f_quantize(last, 0)
-        f_quantize(1, 1)
-        for t in range(SLOTS):
+        o_passes(0, 2, 0, last)
+        for t in range(3):
             o_pass(0, t, last)
-        f_turn(last, 1, 0)
-        f_turn(last, 1, 1)
-        f_group(last, 1, 0)
-        f_group(last, 1, 1)
+        o_passes(0, 3, 0, CHUNKS)
+        f_quantize(0, 1)
+        f_quantize(1, 1)
         f_quantize(2, 1)
         o_store(0, 0)
-        o_store(0, 1)
-        o_passes(1, 0, 0, last)
-        o_passes(1, 1, 0, last)
-        o_store(0, 2)
-        f_quantize(last, 1, 0, 2)
-        o_store(0, 3)
-        f_quantize(last, 1, 2, 4)
-        o_pass(1, 0, last)
-        o_pass(1, 1, last)
-        o_passes(1, 2, 0, CHUNKS)
+        f_quantize(last, 1)
+        o_passes(1, 0, 0, CHUNKS)
+        for t in range(1, SLOTS):
+            o_store(0, t)
+        o_passes(1, 1, 0, CHUNKS)
         o_store(1, 0)
+        o_passes(1, 2, 0, CHUNKS)
         o_store(1, 1)
         o_half(1, 3, 0)
         o_half(1, 3, 1)

@@ -23,7 +23,7 @@ SLOTS = 4
 GROUPS = M // (P * SLOTS)
 CHUNKS = D // N
 SHARE = 320
-SHARE0 = 192
+SHARE0 = 128
 SHARE_A = 288
 EARLY = 2
 SHARE_1 = 416
@@ -401,13 +401,13 @@ def tile_tied_autoencoder_code_step_t2_kernel(
         load_wd_scales(wd_pl_first, 0, N)
         load_x_half(0, 0)
         load_x_half(0, 1)
-        load_pt(0)
         load_x_half(1, 0)
         load_x_half(1, 1)
+        load_pt(0)
         load_wd(wd_second, N, 2 * N)
         load_wd_scales(wd_pl_rest, N, D)
-        load_pt(1)
         load_x(1, 0)
+        load_pt(1)
         load_wd(wd_rest, 2 * N, D)
         load_x(1, 1)
         load_a()
@@ -438,41 +438,41 @@ def tile_tied_autoencoder_code_step_t2_kernel(
             for t in range(SLOTS):
                 r_matmul(0, g, t)
         r_copy(0, 0, 0)
+        r_copy(0, 1, 0)
         e_subtract_gpsimd(0, 0, 0)
-        r_matmul(1, 1, 2)
-        for t in range(1, SLOTS):
-            e_subtract(0, 0, t)
-            r_matmul(1, 0, t)
+        e_subtract_gpsimd(0, 1, 0)
+        r_matmul(1, 0, 3)
+        for g in range(GROUPS):
+            for t in range(1, SLOTS):
+                e_subtract(0, g, t)
+                if g == 0 or t == 1:
+                    r_matmul(1, *[(1, 2), (0, 0), (0, 1), (0, 2)][3 * g + t - 1])
         sort_pt_scalar(0, 0)
-        sort_pt_scalar(1, 0)
-        e_group_scalar(0, 0, 0, SHARE_A)
-        e_group_gpsimd(0, 0, SHARE_A)
-        for t in range(SLOTS):
-            e_subtract(0, 1, t)
-        r_matmul(1, 0, 0)
+        e_group_scalar(0, 0)
+        sort_pt(1, 0)
         r_matmul(1, 1, 3)
         r_matmul(1, 1, 0)
-        r_copy(1, 1, 2)
-        e_quantize(0, 0, 1)
-        e_group_scalar(0, 1, 0, SHARE0)
         e_group_vector(0, 1, SHARE0)
-        g_pass(0, 0, 0, 0)
-        g_pass(0, 0, 1, 0)
+        e_group_scalar(0, 1, 0, SHARE0)
+        e_quantize(0, 0, 1)
         e_quantize(0, 1, 2)
-        sort_pt_scalar(0, 1)
         r_copy(1, 0, 3)
-        r_copy(1, 1, 3)
-        sort_pt_scalar(1, 1)
+        r_copy(1, 1, 2)
         e_subtract_gpsimd(1, 0, 3)
         e_subtract_gpsimd(1, 1, 2)
-        e_subtract_gpsimd(1, 1, 3)
+        g_pass(0, 0, 0, 0)
+        e_subtract(1, 0, 0)
         g_pass(0, 0, 0, 1)
-        g_pass(0, 0, 1, 1)
         r_matmul(1, 1, 1)
-        for t in range(3):
-            e_subtract(1, 0, t)
+        g_matmul(0, 0, 1)
+        e_subtract(1, 0, 1)
+        r_copy(1, 1, 3)
+        e_subtract(1, 0, 2)
+        e_subtract_gpsimd(1, 1, 3)
         r_matmul(2, 0, 2)
         r_matmul(2, 0, 3)
+        sort_pt_scalar(0, 1)
+        sort_pt_scalar(1, 1)
         r_copy(2, 0, 2)
         r_copy(2, 0, 3)
         e_subtract(1, 1, 0)

@@ -350,13 +350,13 @@ def tile_tied_autoencoder_code_step_t2_kernel(
             width = H // pieces
             for k in range(pieces):
                 cols = slice(width * k, width * (k + 1))
-                o_sb = work.tile([P, width], F32, name="o_sb", bufs=6)
+                o_sb = work.tile([P, width], F32, name="o_sb", bufs=8)
                 nc.vector.tensor_tensor(out=o_sb[:], in0=bank[:, cols], in1=rate_sb[:, cols], op=ALU.mult)
                 nc.sync.dma_start(out=out_view[g][:, t, cols], in_=o_sb[:])
 
         def o_half(g, t, k):
             cols = slice(H // 2 * k, H // 2 * (k + 1))
-            bank = take_bank(("h", k))
+            bank = take_bank(("h", t, k))
             for n in range(CHUNKS):
                 nc.tensor.matmul_mx(
                     out=bank[:, : H // 2],
@@ -370,8 +370,8 @@ def tile_tied_autoencoder_code_step_t2_kernel(
 
         def o_store_half(g, t, k):
             cols = slice(H // 2 * k, H // 2 * (k + 1))
-            o_sb = work.tile([P, H // 2], F32, name="o_sb", bufs=6)
-            nc.vector.tensor_tensor(out=o_sb[:], in0=read_bank(("h", k))[:, : H // 2], in1=rate_sb[:, cols], op=ALU.mult)
+            o_sb = work.tile([P, H // 2], F32, name="o_sb", bufs=8)
+            nc.vector.tensor_tensor(out=o_sb[:], in0=read_bank(("h", t, k))[:, : H // 2], in1=rate_sb[:, cols], op=ALU.mult)
             nc.sync.dma_start(out=out_view[g][:, t, cols], in_=o_sb[:])
 
         o_raw = {}
@@ -381,7 +381,7 @@ def tile_tied_autoencoder_code_step_t2_kernel(
             nc.scalar.copy(out=o_raw[g, t][:], in_=read_bank(("o", g, t))[:])
 
         def o_store_gpsimd(g, t):
-            o_sb = work.tile([P, H], F32, name="o_sb", bufs=6)
+            o_sb = work.tile([P, H], F32, name="o_sb", bufs=8)
             nc.gpsimd.tensor_tensor(out=o_sb[:], in0=o_raw[g, t][:], in1=rate_sb[:], op=ALU.mult)
             nc.sync.dma_start(out=out_view[g][:, t, :], in_=o_sb[:])
 
@@ -604,27 +604,31 @@ def tile_tied_autoencoder_code_step_t2_kernel(
         for n in (last - 1, last):
             f_group(n, 1, 0)
             f_group(n, 1, 1)
-        for n in range(last):
-            f_quantize(n, 0, EARLY, SLOTS)
-        f_quantize(last, 0)
-        o_passes(0, 2, 0, last)
-        for t in range(3):
+        f_quantize(0, 0, EARLY, SLOTS)
+        f_quantize(1, 0, EARLY, SLOTS)
+        f_quantize(last, 0, 0, EARLY)
+        f_quantize(2, 0, EARLY, SLOTS)
+        f_quantize(last, 0, EARLY, SLOTS)
+        for t in range(EARLY):
             o_pass(0, t, last)
-        o_passes(0, 3, 0, CHUNKS)
+        for t in range(EARLY, SLOTS):
+            o_passes(0, t, 0, CHUNKS)
         f_quantize(0, 1)
         f_quantize(1, 1)
-        f_quantize(2, 1)
         o_store(0, 0)
-        f_quantize(last, 1)
+        o_store(0, 1)
+        f_quantize(2, 1)
+        f_quantize(last, 1, 0, 2)
         o_passes(1, 0, 0, CHUNKS)
-        for t in range(1, SLOTS):
-            o_store(0, t)
+        o_store(0, 2)
+        o_store(0, 3)
+        f_quantize(last, 1, 2, SLOTS)
         o_passes(1, 1, 0, CHUNKS)
         o_store(1, 0)
-        o_passes(1, 2, 0, CHUNKS)
+        for t in (2, 3):
+            for k in range(2):
+                o_half(1, t, k)
         o_store(1, 1)
-        o_half(1, 3, 0)
-        o_half(1, 3, 1)
-        o_store(1, 2)
-        o_store_half(1, 3, 0)
-        o_store_half(1, 3, 1)
+        for t in (2, 3):
+            for k in range(2):
+                o_store_half(1, t, k)

@@ -230,8 +230,8 @@ def tile_tied_autoencoder_code_step_t2_kernel(
 
         def e_group_scalar(n, g, lo=0, hi=N):
             nc.scalar.copy(
-                out=grouped_e(n, g, lo, hi).rearrange("p (c i) (w e) -> p c w i e", i=2, e=2),
-                in_=e32[n, g][:, :, lo:hi].rearrange("p (w e) (c i) -> p c w i e", i=2, e=2),
+                out=grouped_e(n, g, lo, hi).rearrange("p (c i) (w e) -> p c w i e", i=4, e=2),
+                in_=e32[n, g][:, :, lo:hi].rearrange("p (w e) (c i) -> p c w i e", i=4, e=2),
             )
 
         def e_group_vector(n, g, lo, hi=N):

@@ -149,8 +149,8 @@ def tile_tied_autoencoder_code_step_t2_kernel(
         def group_c(k, lo_j=0, hi_j=2):
             grouped = c_grp[:, N * (2 * k + lo_j) : N * (2 * k + hi_j)].bitcast(F32)
             nc.scalar.copy(
-                out=grouped.rearrange("p (i r u) -> p i r u", i=hi_j - lo_j, u=2),
-                in_=read_bank(("c", k, lo_j))[:, 2 * P * lo_j : 2 * P * hi_j].rearrange("p (i u r) -> p i r u", i=hi_j - lo_j, u=2),
+                out=grouped.rearrange("p (i r s u) -> p i r u s", i=hi_j - lo_j, s=2, u=2),
+                in_=read_bank(("c", k, lo_j))[:, 2 * P * lo_j : 2 * P * hi_j].rearrange("p (i u r s) -> p i r u s", i=hi_j - lo_j, u=2, s=2),
             )
 
         def quantize_c(k, lo_j=0, hi_j=2):
@@ -235,7 +235,10 @@ def tile_tied_autoencoder_code_step_t2_kernel(
             )
 
         def e_group_vector(n, g, lo, hi=N):
-            nc.vector.tensor_copy(out=grouped_e(n, g, lo, hi), in_=e32[n, g][:, :, lo:hi].rearrange("p t n -> p n t"))
+            nc.vector.tensor_copy(
+                out=grouped_e(n, g, lo, hi).rearrange("p (c i) (w e) -> p c w i e", i=4, e=2),
+                in_=e32[n, g][:, :, lo:hi].rearrange("p (w e) (c i) -> p c w i e", i=4, e=2),
+            )
 
         def e_group_gpsimd(n, g, lo, hi=N):
             nc.gpsimd.tensor_scalar(
@@ -317,8 +320,8 @@ def tile_tied_autoencoder_code_step_t2_kernel(
                 f_grp[n, g] = work.tile([P, SLOTS * N], BF16, name="f_grp", bufs=6, align_bytes=64)
             grouped = f_grp[n, g][:, 2 * N * pair : 2 * N * (pair + 1)].bitcast(F32)
             nc.scalar.copy(
-                out=grouped.rearrange("p (i r u) -> p i r u", i=2, u=2),
-                in_=read_bank(("t", n, g, pair))[:].rearrange("p (i u r) -> p i r u", i=2, u=2),
+                out=grouped.rearrange("p (i r s u) -> p i r u s", i=2, s=2, u=2),
+                in_=read_bank(("t", n, g, pair))[:].rearrange("p (i u r s) -> p i r u s", i=2, u=2, s=2),
             )
 
         def f_quantize(n, g, lo=0, hi=SLOTS):

from contextlib import ExitStack

import concourse.mybir as mybir
from concourse.masks import make_identity

M, D, H = 1024, 2048, 512
FLOPS = 2 * (M * H * D + M * M * D + M * D * H)

F32 = mybir.dt.float32
BF16 = mybir.dt.bfloat16
I32 = mybir.dt.int32
U32 = mybir.dt.uint32
U16 = mybir.dt.uint16
U8 = mybir.dt.uint8
E4M3X4 = mybir.dt.float8_e4m3fn_x4
E2M1X4 = mybir.dt.float4_e2m1fn_x4
ALU = mybir.AluOpType
ACT = mybir.ActivationFunctionType

P = 128
N = 512
SLOTS = 4
GROUPS = M // (P * SLOTS)
CHUNKS = D // N
SHARE = 320
SHARE0 = 128
SHARE_A = 288
EARLY = 2
SHARE_1 = 416
SHARE_LAST = 224

MOVING_CODES, MOVING_SCALES, STILL_CODES, STILL_SCALES = 0, 64, 128, 192


def tile_tied_autoencoder_code_step_t2_kernel(
    tc, x, c, wd_words, wd_scales, pt_words, pt_scales, wb_words, wb_scales, a, rate, out
):
    nc = tc.nc
    with ExitStack() as ctx:
        keep = ctx.enter_context(tc.tile_pool(name="keep", bufs=1))
        work = ctx.enter_context(tc.tile_pool(name="work", bufs=2))
        psum = ctx.enter_context(tc.psum_pool(name="psum", bufs=1))
        ctx.enter_context(tc.manual_schedule())

        def placed(pool, name, columns, dtype, item_bytes, start, bufs=1):
            lead = start // item_bytes
            whole = pool.tile([P, lead + columns], dtype, name=name, bufs=bufs, align_bytes=256)
            return whole[:, lead : lead + columns]

        ident = keep.tile([P, P], F32, name="ident")
        c_raw = [keep.tile([P, 2, H], BF16, name="c_raw%d" % k) for k in range(4)]
        c_sorted = {k: keep.tile([P, 2, 2, P], F32, name="c_sorted%d" % k) for k in range(2, 4)}
        c_grp = keep.tile([P, 4 * M], BF16, name="c_grp", align_bytes=64)
        c_codes = placed(keep, "c_codes", M, U32, 4, STILL_CODES)
        c_planes = placed(keep, "c_planes", M, U8, 1, STILL_SCALES)
        x_half = {(g, j): keep.tile([P, 2, N], BF16, name="x_first%d_%d" % (g, j)) for g in range(2) for j in range(2)}
        x_rest = {
            (n, g): keep.tile([P, SLOTS, N], BF16, name="x_sb%d_%d" % (n, g)) for n in range(1, CHUNKS) for g in range(2)
        }
        wd_first = placed(keep, "wd_first", 2 * N, U8, 1, MOVING_CODES)
        wd_second = placed(keep, "wd_second", 2 * N, U8, 1, MOVING_CODES)
        wd_rest = placed(keep, "wd_rest", 2 * (D - 2 * N), U8, 1, MOVING_CODES)
        wd_pl_first = placed(keep, "wd_pl_first", N, U8, 1, MOVING_SCALES)
        wd_pl_rest = placed(keep, "wd_pl_rest", D - N, U8, 1, MOVING_SCALES)
        pt_raw = [keep.tile([P, GROUPS, 2 * N], U8, name="pt_raw%d" % j, align_bytes=64) for j in range(GROUPS)]
        pt_sb = {(k, j): placed(keep, "pt_sb%d_%d" % (k, j), 2 * N, U8, 1, STILL_CODES) for k in range(2) for j in range(2)}
        pt_plraw = keep.tile([P, GROUPS, M], U8, name="pt_plraw", align_bytes=64)
        pt_pl = {(k, j): placed(keep, "pt_pl%d_%d" % (k, j), N, U8, 1, STILL_SCALES) for k in range(2) for j in range(2)}
        wb_sb = placed(keep, "wb_sb", CHUNKS * 2 * H, U8, 1, MOVING_CODES).rearrange("p (g w) -> p g w", g=CHUNKS)
        wb_pl = placed(keep, "wb_pl", CHUNKS * H, U8, 1, MOVING_SCALES).rearrange("p (g w) -> p g w", g=CHUNKS)
        a_sb = keep.tile([P, GROUPS, SLOTS], BF16, name="a_sb")
        a_f32 = keep.tile([P, GROUPS, SLOTS], F32, name="a_f32")
        rate_sb = keep.tile([P, H], BF16, name="rate_sb")
        f_codes = {(n, g): placed(keep, "f_codes%d_%d" % (n, g), N, U32, 4, STILL_CODES) for n in range(CHUNKS) for g in range(2)}
        f_planes = {(n, g): placed(keep, "f_planes%d_%d" % (n, g), N, U8, 1, STILL_SCALES) for n in range(CHUNKS) for g in range(2)}

        c_view = c.rearrange("(g p t) k -> g p t k", p=P, t=SLOTS)
        x_view = x.rearrange("(g p t) d -> g p t d", p=P, t=SLOTS)
        out_view = out.rearrange("(g p t) h -> g p t h", p=P, t=SLOTS)

        def load_c(k):
            nc.sync.dma_start(out=c_raw[k][:], in_=c_view[k // 2][:, 2 * (k % 2) : 2 * (k % 2) + 2, :])

        def load_x_half(g, j):
            nc.sync.dma_start(out=x_half[g, j][:], in_=x_view[g][:, 2 * j : 2 * j + 2, 0:N])

        def load_x(n, g):
            nc.sync.dma_start(out=x_rest[n, g][:], in_=x_view[g][:, :, N * n : N * (n + 1)])

        def x_slot(n, g, t):
            return x_half[g, t // 2][:, t % 2, :] if n == 0 else x_rest[n, g][:, t, :]

        def load_wd(tile, lo, hi):
            nc.sync.dma_start(out=tile[:].bitcast(I32), in_=wd_words[0][:, 2 * lo : 2 * hi].bitcast(I32))

        def load_wd_scales(plane, lo, hi):
            for r in range(4):
                nc.sync.dma_start(out=plane[r:P:32, :].bitcast(I32), in_=wd_scales[0][r:16:4, lo:hi].bitcast(I32))

        def load_scales(planes, rows):
            for r in range(4):
                nc.sync.dma_start(
                    out=planes[r:P:32, :, :].bitcast(I32),
                    in_=rows[:, r:16:4, :].rearrange("g q n -> q g n").bitcast(I32),
                )

        def load_pt(j):
            cols = pt_words[:, :, 2 * N * j : 2 * N * (j + 1)]
            nc.sync.dma_start(out=pt_raw[j][:].bitcast(I32), in_=cols.rearrange("g p w -> p g w").bitcast(I32))

        def load_pt_scales():
            load_scales(pt_plraw, pt_scales)

        def load_a():
            nc.sync.dma_start(out=a_sb[:], in_=a.rearrange("(g p t) -> p g t", p=P, t=SLOTS))

        def load_wb():
            load_scales(wb_pl, wb_scales)
            nc.sync.dma_start(out=wb_sb[:].bitcast(I32), in_=wb_words.rearrange("g p w -> p g w").bitcast(I32))
            nc.sync.dma_start(out=rate_sb[:], in_=rate.partition_broadcast(P))

        free = list(range(8))
        held = {}

        def take_bank(key):
            k = free.pop(0)
            bank = psum.tile([P, N], F32, name="bank%d" % k, tag="bank%d" % k)
            held[key] = (k, bank)
            return bank

        def read_bank(key):
            k, bank = held.pop(key)
            free.append(k)
            return bank

        def sort_c(k):
            nc.vector.tensor_copy(
                out=c_sorted[k][:], in_=c_raw[k][:].bitcast(F32).rearrange("p j (m u) -> p j u m", u=2)
            )

        def turn_c(k, is_sorted=True, lo_j=0, hi_j=2):
            turned = take_bank(("c", k, lo_j))
            for j in range(lo_j, hi_j):
                for u in range(2):
                    words = c_sorted[k][:, j, u, :] if is_sorted else c_raw[k][:, j, :].bitcast(F32)[:, u : 2 * P : 2]
                    lo = P * (2 * j + u)
                    nc.tensor.transpose(turned[:, lo : lo + P], words, ident[:])

        def group_c(k, lo_j=0, hi_j=2):
            grouped = c_grp[:, N * (2 * k + lo_j) : N * (2 * k + hi_j)].bitcast(F32)
            nc.scalar.copy(
                out=grouped.rearrange("p (i r s u) -> p i r u s", i=hi_j - lo_j, s=2, u=2),
                in_=read_bank(("c", k, lo_j))[:, 2 * P * lo_j : 2 * P * hi_j].rearrange("p (i u r s) -> p i r u s", i=hi_j - lo_j, u=2, s=2),
            )

        def quantize_c(k, lo_j=0, hi_j=2):
            lo, hi = 2 * k + lo_j, 2 * k + hi_j
            nc.vector.quantize_mx(
                out=c_codes[:, P * lo : P * hi].bitcast(E4M3X4), scales=c_planes[:, P * lo : P * hi], in_=c_grp[:, N * lo : N * hi]
            )

        def sort_pt(k, j):
            nc.vector.tensor_copy(
                out=pt_sb[k, j][:].bitcast(U16).rearrange("p (t m) -> p t m", t=SLOTS),
                in_=pt_raw[j][:, k, :].bitcast(U16).rearrange("p (m t) -> p t m", t=SLOTS),
            )

        def sort_pt_scalar(k, j):
            nc.scalar.copy(
                out=pt_sb[k, j][:].bitcast(U16).rearrange("p (t m) -> p t m", t=SLOTS),
                in_=pt_raw[j][:, k, :].bitcast(U16).rearrange("p (m t) -> p t m", t=SLOTS),
            )

        def sort_pt_scales(k, j):
            nc.vector.tensor_copy(
                out=pt_pl[k, j][:].rearrange("p (t m) -> p t m", t=SLOTS),
                in_=pt_plraw[:, k, N * j : N * (j + 1)].rearrange("p (m t) -> p t m", t=SLOTS),
            )

        e32, e_grp, e_codes, e_planes, r_aside = {}, {}, {}, {}, {}

        def as_stored(ap):
            return ap.rearrange("p (u m e) -> p u m e", u=2, e=2)

        def into_stored(ap):
            return ap.rearrange("p (m u e) -> p u m e", u=2, e=2)

        def e_part(n, g):
            if (n, g) not in e32:
                e32[n, g] = work.tile([P, SLOTS, N], F32, name="e32_%d" % g, bufs=3 - g)
            return e32[n, g]

        def r_matmul(n, g, t):
            rows = slice(P * (SLOTS * g + t), P * (SLOTS * g + t + 1))
            words = [wd_first[:], wd_second[:], wd_rest[:, : 2 * N], wd_rest[:, 2 * N :]][n]
            nc.tensor.matmul_mx(
                out=take_bank(("r", n, g, t))[:],
                lhsT=c_codes[:, rows].bitcast(E4M3X4),
                lhsT_scale=c_planes[:, rows],
                rhs=words.bitcast(E2M1X4),
                rhs_scale=wd_pl_first[:] if n == 0 else wd_pl_rest[:, N * (n - 1) : N * n],
                start=True,
                stop=True,
            )

        def e_subtract(n, g, t):
            nc.vector.tensor_tensor(
                out=e_part(n, g)[:, t, :].rearrange("p (u m e) -> p m u e", u=2, e=2),
                in0=x_slot(n, g, t).rearrange("p (m u e) -> p m u e", u=2, e=2),
                in1=read_bank(("r", n, g, t))[:].rearrange("p (m u e) -> p m u e", u=2, e=2),
                op=ALU.subtract,
            )

        def r_copy(n, g, t):
            r_aside[n, g, t] = work.tile([P, N], F32, name="r_aside", bufs=5)
            nc.scalar.copy(out=as_stored(r_aside[n, g, t][:]), in_=into_stored(read_bank(("r", n, g, t))[:]))

        def e_subtract_gpsimd(n, g, t):
            nc.gpsimd.tensor_tensor(
                out=as_stored(e_part(n, g)[:, t, :]),
                in0=into_stored(x_slot(n, g, t)),
                in1=as_stored(r_aside[n, g, t][:]),
                op=ALU.subtract,
            )

        def grouped_e(n, g, lo, hi):
            if n not in e_grp:
                e_grp[n] = work.tile([P, GROUPS, N, SLOTS], BF16, name="e_grp", bufs=1, align_bytes=64)
            return e_grp[n][:, g, lo:hi, :]

        def e_group_scalar(n, g, lo=0, hi=N):
            nc.scalar.copy(
                out=grouped_e(n, g, lo, hi).rearrange("p (c i) (w e) -> p c w i e", i=4, e=2),
                in_=e32[n, g][:, :, lo:hi].rearrange("p (w e) (c i) -> p c w i e", i=4, e=2),
            )

        def e_group_vector(n, g, lo, hi=N):
            nc.vector.tensor_copy(
                out=grouped_e(n, g, lo, hi).rearrange("p (c i) (w e) -> p c w i e", i=4, e=2),
                in_=e32[n, g][:, :, lo:hi].rearrange("p (w e) (c i) -> p c w i e", i=4, e=2),
            )

        def e_group_gpsimd(n, g, lo, hi=N):
            nc.gpsimd.tensor_scalar(
                out=grouped_e(n, g, lo, hi),
                in0=e32[n, g][:, :, lo:hi].rearrange("p t n -> p n t"),
                scalar1=1.0,
                scalar2=0.0,
                op0=ALU.mult,
                op1=ALU.add,
            )

        def e_quantize(n, lo=0, hi=GROUPS):
            if n not in e_codes:
                e_codes[n] = placed(work, "e_codes", GROUPS * N, U32, 4, MOVING_CODES, bufs=2)
                e_planes[n] = placed(work, "e_planes", GROUPS * N, U8, 1, MOVING_SCALES, bufs=2)
            nc.vector.quantize_mx(
                out=e_codes[n][:, N * lo : N * hi].bitcast(E4M3X4),
                scales=e_planes[n][:, N * lo : N * hi],
                in_=e_grp[n][:, lo:hi, :, :].rearrange("p g n t -> p (g n t)"),
            )

        f_sb, f_grp = {}, {}

        def g_pass(n, g, t, k):
            if k == 0:
                take_bank(("g", n, g, t))
            nc.tensor.matmul_mx(
                out=held[("g", n, g, t)][1][:],
                lhsT=pt_sb[k, g][:, 2 * P * t : 2 * P * (t + 1)].bitcast(E2M1X4),
                lhsT_scale=pt_pl[k, g][:, P * t : P * (t + 1)],
                rhs=e_codes[n][:, N * k : N * (k + 1)].bitcast(E4M3X4),
                rhs_scale=e_planes[n][:, N * k : N * (k + 1)],
                start=(k == 0),
                stop=(k == GROUPS - 1),
            )

        def g_matmul(n, g, t):
            for k in range(GROUPS):
                g_pass(n, g, t, k)

        def f_add(n, g, t):
            if (n, g) not in f_sb:
                f_sb[n, g] = work.tile([P, SLOTS, N], BF16, name="f_sb", bufs=3)
            nc.vector.scalar_tensor_tensor(
                out=f_sb[n, g][:, t, :],
                in0=e32[n, g][:, t, :],
                scalar=a_sb[:, g, t : t + 1],
                in1=read_bank(("g", n, g, t))[:],
                op0=ALU.mult,
                op1=ALU.add,
            )

        g_aside = {}

        def e_scale(n, g, t):
            nc.scalar.activation(
                out=e32[n, g][:, t, :], in_=e32[n, g][:, t, :], func=ACT.Copy, scale=a_f32[:, g, t : t + 1]
            )

        def g_copy(n, g, t):
            g_aside[n, g, t] = work.tile([P, N], F32, name="r_aside", bufs=5)
            nc.scalar.copy(out=g_aside[n, g, t][:], in_=read_bank(("g", n, g, t))[:])

        def f_add_gpsimd(n, g, t):
            if (n, g) not in f_sb:
                f_sb[n, g] = work.tile([P, SLOTS, N], BF16, name="f_sb", bufs=3)
            nc.gpsimd.tensor_tensor(out=f_sb[n, g][:, t, :], in0=e32[n, g][:, t, :], in1=g_aside[n, g, t][:], op=ALU.add)

        def f_turn(n, g, pair):
            turned = take_bank(("t", n, g, pair))
            for i in range(2):
                words = f_sb[n, g][:, 2 * pair + i, :].bitcast(F32)
                for u in range(2):
                    lo = P * (2 * i + u)
                    nc.tensor.transpose(turned[:, lo : lo + P], words[:, P * u : P * (u + 1)], ident[:])

        def f_group(n, g, pair):
            if (n, g) not in f_grp:
                f_grp[n, g] = work.tile([P, SLOTS * N], BF16, name="f_grp", bufs=6, align_bytes=64)
            grouped = f_grp[n, g][:, 2 * N * pair : 2 * N * (pair + 1)].bitcast(F32)
            nc.scalar.copy(
                out=grouped.rearrange("p (i r s u) -> p i r u s", i=2, s=2, u=2),
                in_=read_bank(("t", n, g, pair))[:].rearrange("p (i u r s) -> p i r u s", i=2, u=2, s=2),
            )

        def f_quantize(n, g, lo=0, hi=SLOTS):
            nc.vector.quantize_mx(
                out=f_codes[n, g][:, P * lo : P * hi].bitcast(E4M3X4),
                scales=f_planes[n, g][:, P * lo : P * hi],
                in_=f_grp[n, g][:, N * lo : N * hi],
            )

        def o_pass(g, t, n):
            if n == 0:
                take_bank(("o", g, t))
            nc.tensor.matmul_mx(
                out=held[("o", g, t)][1][:],
                lhsT=f_codes[n, g][:, P * t : P * (t + 1)].bitcast(E4M3X4),
                lhsT_scale=f_planes[n, g][:, P * t : P * (t + 1)],
                rhs=wb_sb[:, n, :].bitcast(E2M1X4),
                rhs_scale=wb_pl[:, n, :],
                start=(n == 0),
                stop=(n == CHUNKS - 1),
            )

        def o_passes(g, t, lo, hi):
            for n in range(lo, hi):
                o_pass(g, t, n)

        def o_store(g, t, pieces=1):
            bank = read_bank(("o", g, t))
            width = H // pieces
            for k in range(pieces):
                cols = slice(width * k, width * (k + 1))
                o_sb = work.tile([P, width], F32, name="o_sb", bufs=8)
                nc.vector.tensor_tensor(out=o_sb[:], in0=bank[:, cols], in1=rate_sb[:, cols], op=ALU.mult)
                nc.sync.dma_start(out=out_view[g][:, t, cols], in_=o_sb[:])

        def o_half(g, t, k):
            cols = slice(H // 2 * k, H // 2 * (k + 1))
            bank = take_bank(("h", t, k))
            for n in range(CHUNKS):
                nc.tensor.matmul_mx(
                    out=bank[:, : H // 2],
                    lhsT=f_codes[n, g][:, P * t : P * (t + 1)].bitcast(E4M3X4),
                    lhsT_scale=f_planes[n, g][:, P * t : P * (t + 1)],
                    rhs=wb_sb[:, n, H * k : H * (k + 1)].bitcast(E2M1X4),
                    rhs_scale=wb_pl[:, n, cols],
                    start=(n == 0),
                    stop=(n == CHUNKS - 1),
                )

        def o_store_half(g, t, k):
            cols = slice(H // 2 * k, H // 2 * (k + 1))
            o_sb = work.tile([P, H // 2], F32, name="o_sb", bufs=8)
            nc.vector.tensor_tensor(out=o_sb[:], in0=read_bank(("h", t, k))[:, : H // 2], in1=rate_sb[:, cols], op=ALU.mult)
            nc.sync.dma_start(out=out_view[g][:, t, cols], in_=o_sb[:])

        o_raw = {}

        def o_copy(g, t):
            o_raw[g, t] = work.tile([P, H], F32, name="r_aside", bufs=5)
            nc.scalar.copy(out=o_raw[g, t][:], in_=read_bank(("o", g, t))[:])

        def o_store_gpsimd(g, t):
            o_sb = work.tile([P, H], F32, name="o_sb", bufs=8)
            nc.gpsimd.tensor_tensor(out=o_sb[:], in0=o_raw[g, t][:], in1=rate_sb[:], op=ALU.mult)
            nc.sync.dma_start(out=out_view[g][:, t, :], in_=o_sb[:])

        nc.vector.memset(pt_plraw[:].rearrange("p g n -> p (g n)").bitcast(I32), 0)
        nc.vector.memset(wd_pl_first[:].bitcast(I32), 0)
        nc.vector.memset(wd_pl_rest[:].bitcast(I32), 0)
        nc.vector.memset(wb_pl[:].rearrange("p g n -> p (g n)").bitcast(I32), 0)
        make_identity(nc, ident[:])


        load_c(0)
        load_c(1)
        load_pt_scales()
        load_c(2)
        load_c(3)
        load_wd(wd_first, 0, N)
        load_wd_scales(wd_pl_first, 0, N)
        load_x_half(0, 0)
        load_x_half(0, 1)
        load_x_half(1, 0)
        load_x_half(1, 1)
        load_pt(0)
        load_wd(wd_second, N, 2 * N)
        load_wd_scales(wd_pl_rest, N, D)
        load_x(1, 0)
        load_pt(1)
        load_wd(wd_rest, 2 * N, D)
        load_x(1, 1)
        load_a()
        for n in range(2, CHUNKS):
            for g in range(GROUPS):
                load_x(n, g)
        load_wb()

        turn_c(0, False)
        turn_c(1, False)
        group_c(0)
        sort_pt_scales(0, 0)
        sort_c(2)
        turn_c(2)
        quantize_c(0)
        sort_c(3)
        turn_c(3)
        group_c(1)
        group_c(2)
        group_c(3)
        sort_pt_scales(1, 0)
        quantize_c(1)
        sort_pt_scales(0, 1)
        quantize_c(2)
        sort_pt_scales(1, 1)
        quantize_c(3)
        for g in range(GROUPS):
            for t in range(SLOTS):
                r_matmul(0, g, t)
        r_copy(0, 0, 0)
        r_copy(0, 1, 0)
        e_subtract_gpsimd(0, 0, 0)
        e_subtract_gpsimd(0, 1, 0)
        r_matmul(1, 0, 3)
        for g in range(GROUPS):
            for t in range(1, SLOTS):
                e_subtract(0, g, t)
                if g == 0 or t == 1:
                    r_matmul(1, *[(1, 2), (0, 0), (0, 1), (0, 2)][3 * g + t - 1])
        sort_pt_scalar(0, 0)
        e_group_scalar(0, 0)
        sort_pt(1, 0)
        r_matmul(1, 1, 3)
        r_matmul(1, 1, 0)
        e_group_vector(0, 1, SHARE0)
        e_group_scalar(0, 1, 0, SHARE0)
        e_quantize(0, 0, 1)
        e_quantize(0, 1, 2)
        r_copy(1, 0, 3)
        r_copy(1, 1, 2)
        e_subtract_gpsimd(1, 0, 3)
        e_subtract_gpsimd(1, 1, 2)
        g_pass(0, 0, 0, 0)
        e_subtract(1, 0, 0)
        g_pass(0, 0, 0, 1)
        r_matmul(1, 1, 1)
        g_matmul(0, 0, 1)
        e_subtract(1, 0, 1)
        r_copy(1, 1, 3)
        e_subtract(1, 0, 2)
        e_subtract_gpsimd(1, 1, 3)
        r_matmul(2, 0, 2)
        r_matmul(2, 0, 3)
        sort_pt_scalar(0, 1)
        sort_pt_scalar(1, 1)
        r_copy(2, 0, 2)
        r_copy(2, 0, 3)
        e_subtract(1, 1, 0)
        e_subtract(1, 1, 1)
        e_group_scalar(1, 0)
        for n in range(CHUNKS - 1):
            nxt = n + 1
            after = nxt + 1 < CHUNKS
            share = [SHARE_1, SHARE, SHARE_LAST][n]
            if n > 0:
                e_subtract_gpsimd(nxt, 1, 2)
                e_subtract_gpsimd(nxt, 1, 3)
                e_subtract(nxt, 0, 0)
                if after:
                    r_copy(nxt + 1, 0, 2)
                e_subtract(nxt, 0, 1)
                g_matmul(n, 0, 0)
                if after:
                    r_copy(nxt + 1, 0, 3)
                e_subtract(nxt, 1, 0)
                g_matmul(n, 0, 1)
                e_subtract(nxt, 1, 1)
                e_group_scalar(nxt, 0)
            if after:
                e_subtract_gpsimd(nxt + 1, 0, 2)
            e_group_gpsimd(nxt, 1, share)
            if after:
                e_subtract_gpsimd(nxt + 1, 0, 3)
            if n > 0:
                e_group_scalar(nxt, 1, 0, share)
            g_matmul(n, 0, 2)
            f_add(n, 0, 0)
            g_matmul(n, 0, 3)
            f_add(n, 0, 1)
            if n == 0:
                e_group_scalar(nxt, 1, 0, share)
            g_matmul(n, 1, 0)
            f_add(n, 0, 2)
            g_matmul(n, 1, 1)
            f_add(n, 0, 3)
            if not after:
                break
            r_matmul(nxt + 1, 1, 2)
            g_matmul(n, 1, 2)
            f_add(n, 1, 0)
            r_matmul(nxt + 1, 1, 3)
            g_matmul(n, 1, 3)
            f_add(n, 1, 1)
            if n > 0:
                f_turn(n - 1, 1, 0)
                f_turn(n - 1, 1, 1)
            f_turn(n, 0, 0)
            if n > 0:
                r_copy(nxt + 1, 1, 2)
            f_add(n, 1, 2)
            f_turn(n, 0, 1)
            if n == 0:
                r_copy(nxt + 1, 1, 2)
            f_add(n, 1, 3)
            r_copy(nxt + 1, 1, 3)
            if n > 0:
                f_group(n - 1, 1, 0)
            r_matmul(nxt + 1, 0, 0)
            if nxt + 2 < CHUNKS:
                r_matmul(nxt + 2, 0, 2)
            if n > 0:
                f_group(n - 1, 1, 1)
            r_matmul(nxt + 1, 0, 1)
            f_group(n, 0, 0)
            if nxt + 2 < CHUNKS:
                r_matmul(nxt + 2, 0, 3)
            f_group(n, 0, 1)
            r_matmul(nxt + 1, 1, 0)
            r_matmul(nxt + 1, 1, 1)
            e_quantize(nxt)

        last = CHUNKS - 1
        g_matmul(2, 1, 2)
        g_matmul(2, 1, 3)
        f_add(2, 1, 0)
        f_quantize(0, 0, 0, EARLY)
        f_quantize(1, 0, 0, EARLY)
        e_quantize(last)
        nc.scalar.copy(out=a_f32[:], in_=a_sb[:])
        e_scale(2, 1, 3)
        for g, n in ((1, 1), (0, 2)):
            f_turn(n, g, 0)
            f_turn(n, g, 1)
        o_passes(0, 0, 0, 2)
        for g, n in ((1, 1), (0, 2)):
            f_group(n, g, 0)
            f_group(n, g, 1)
        for t in range(1, EARLY):
            o_passes(0, t, 0, 2)
        g_matmul(last, 0, 0)
        f_add(2, 1, 1)
        g_copy(2, 1, 3)
        g_matmul(last, 0, 1)
        f_add(2, 1, 2)
        f_quantize(2, 0, 0, EARLY)
        f_add_gpsimd(2, 1, 3)
        e_scale(last, 0, 1)
        g_matmul(last, 0, 2)
        f_add(last, 0, 0)
        g_copy(last, 0, 1)
        f_add_gpsimd(last, 0, 1)
        g_matmul(last, 0, 3)
        e_scale(last, 1, 0)
        g_matmul(last, 1, 0)
        f_add(last, 0, 2)
        g_matmul(last, 1, 1)
        f_add(last, 0, 3)
        g_copy(last, 1, 0)
        f_add_gpsimd(last, 1, 0)
        g_matmul(last, 1, 2)
        g_matmul(last, 1, 3)
        f_add(last, 1, 1)
        f_turn(last, 0, 0)
        f_turn(last, 0, 1)
        for t in range(EARLY):
            o_pass(0, t, 2)
        f_add(last, 1, 2)
        f_add(last, 1, 3)
        f_group(last, 0, 0)
        f_group(last, 0, 1)
        for n in (last - 1, last):
            f_turn(n, 1, 0)
            f_turn(n, 1, 1)
        for n in (last - 1, last):
            f_group(n, 1, 0)
            f_group(n, 1, 1)
        f_quantize(0, 0, EARLY, SLOTS)
        f_quantize(1, 0, EARLY, SLOTS)
        f_quantize(last, 0, 0, EARLY)
        f_quantize(2, 0, EARLY, SLOTS)
        f_quantize(last, 0, EARLY, SLOTS)
        for t in range(EARLY):
            o_pass(0, t, last)
        for t in range(EARLY, SLOTS):
            o_passes(0, t, 0, CHUNKS)
        f_quantize(0, 1)
        f_quantize(1, 1)
        o_store(0, 0)
        o_store(0, 1)
        f_quantize(2, 1)
        f_quantize(last, 1, 0, 2)
        o_passes(1, 0, 0, CHUNKS)
        o_store(0, 2)
        o_store(0, 3)
        f_quantize(last, 1, 2, SLOTS)
        o_passes(1, 1, 0, CHUNKS)
        o_store(1, 0)
        for t in (2, 3):
            for k in range(2):
                o_half(1, t, k)
        o_store(1, 1)
        for t in (2, 3):
            for k in range(2):
                o_store_half(1, t, k)
